import numpy as np, ml_dtypes
CORES = [6,15,38,47]
N = 4
BF = ml_dtypes.bfloat16
def gentries(a):
    return np.ascontiguousarray(a.reshape(8, 16, -1).transpose(0, 2, 1)).reshape(8, -1)
def gtable(e):
    e = np.asarray(e); return np.ascontiguousarray(e.reshape(8, -1, 16).transpose(0, 2, 1)).reshape(128, -1).astype(np.int32)
R, A, J, W, Q, SH, RO = 64, 8, 4, 4096, 28, 4, 4
def parts(rng):
    amp = rng.choice(np.array([16, 32, 64, 128]), (N, 8, 1, 1))
    p = (amp * rng.random((N, 8, 16, W))).astype(np.int64)
    s = rng.integers(0, 1009, (N, 8, 1, W)) + rng.integers(0, 16, (N, 8, 16, W))
    c = rng.integers(0, W, (N, 8, R, Q)); nbr = rng.integers(0, N * R, (N, 8, J, R)); ge = rng.integers(0, W, (N, 8, J, R))
    return p, s, c, nbr, ge
def pack(p, s, c, nbr, ge):
    return {"pe": np.ascontiguousarray(p.reshape(N, 128, W)).astype(np.float32).astype(BF), "se": np.ascontiguousarray(s.reshape(N, 128, W)).astype(np.int32),
            "cand": np.ascontiguousarray(c.reshape(N, 8, R * Q)).astype(np.int32),
            "nb": np.stack([gtable(a.reshape(8, -1)) for a in nbr]), "geo": np.stack([gtable(a.reshape(8, -1)) for a in ge])}
def setup_inputs(rng):
    return pack(*parts(rng))
def ladder():
    o = [512 + 8 * (A - 1 - a) for a in range(A)]
    w = [0] * A
    for i in range(A // 2):
        w[(A - 1 + 2 * i) % A] = 512 - 8 * i; w[2 * i] = 200 + 8 * (A // 2 - 1 - i)
    o += w[:A - 1]
    h = 512 - 8 * (A // 2 - 1); ch = [(A - 3 + 3 * i) % A for i in range(A)]; m = ch.index(A - 2)
    for i in range(A): w[ch[i]] = h - (h - 200) * i // m if i < m else 200 - 8 * (i - m)
    return np.array(o + w[:A - 3] + [w[A - 1]])
def setup_inputs_most(rng):
    p, s, c, nbr, ge = parts(rng); o = ladder(); k = W // 1024
    for q in range(N):
        for g in range(8):
            pm = rng.permutation(W); lv = np.zeros(W, np.int64); lv[pm] = np.arange(W) // k
            s[q, g] = lv[None, :]; p[q, g] = rng.integers(0, 2, (16, W))
            v = rng.integers(0, 1024, (R, Q)); v[:, :len(o)] = o[None, :] + rng.integers(-100, 301, (R, 1))
            c[q, g] = pm[v * k + rng.integers(0, k, (R, Q))]
    far = 1 + rng.permutation(N) % (N - 1)
    nbr = ((np.arange(N) + far) % N * R)[:, None, None, None] + rng.integers(0, R, (N, 8, J, R))
    return pack(p, s, c, nbr, ge)
def setup_inputs_ties(rng):
    p, s, c, nbr, ge = parts(rng)
    p[:, ::2] = rng.integers(0, 128, (N, 4, 16, 1)); p[:, 1::2] = rng.integers(0, 2, (N, 4, 16, W))
    lv = rng.integers(0, 4, (N, 8, 1, W)); lv[:, 1::2] = rng.integers(0, 12, (N, 4, 1, W))
    lone = rng.integers(0, 64, (N, 8, 1, W)) == np.arange(16)[:, None]
    s = 1 + lv + rng.integers(0, 900, (N, 8, 16, 1)) - lone
    return pack(p, s, c, nbr, ge)
def setup_inputs_ends(rng):
    p, s, c, nbr, ge = parts(rng)
    c[:, ::2] = rng.choice(np.array([0, 1, W // 2 - 1, W - 5, W - 3, W - 1]), (N, 4, R, Q)); ge[:, ::2] = rng.choice(np.array([0, 1, W - 1]), (N, 4, J, R))
    s[:, ::2, :, 0] = 0; s[:, ::2, :, W - 1] = 1023; s[:, ::2, :, W // 2 - 1] = 500
    p[:, ::4] = 127 * rng.integers(0, 2, (N, 2, 16, W))
    own = np.arange(N)[:, None, None] * R
    nbr[:, 0] = own + np.arange(R)
    nbr[:, 1] = rng.choice(np.array([0, R - 1, (N - 1) * R, N * R - 1]), (N, J, R))
    nbr[:, 3] = rng.integers(0, N * R, (N, 1, R))
    nbr[:, 5] = (own + R) % (N * R) + rng.integers(0, R, (N, J, R))
    nbr[:, 7] = own + rng.integers(0, R, (N, J, R))
    return pack(p, s, c, nbr, ge)
def setup_inputs_still(rng):
    p, s, c, nbr, ge = parts(rng); o = rng.permutation(8); b, h = o[4], o[5]
    c[:, o[4:6], ::4] = 1 << SH; nbr[:, o[4:6]] = 4 * rng.integers(0, N * R // 4, (N, 2, J, R)); ge[:, o[4:6]] = 64 * rng.integers(0, W // 64, (N, 2, J, R))
    p[:, b] = np.tile(rng.integers(0, 128, (N, 16, 64)), (1, 1, W // 64))
    s[:, b] = rng.integers(127 * J, 1016, (N, 1, W)) - J * p[:, b] + rng.integers(0, 8, (N, 16, W))
    t = np.tile(np.argsort(rng.random((N, 1, 64)), axis=-1) & 1, (1, 1, W // 64)); one = np.arange(16)[:, None] == rng.integers(0, 16, (N, 1, 1))
    p[:, h] = np.where(one, 127 * (1 - t), np.tile(rng.integers(0, 128, (N, 16, 64)), (1, 1, W // 64)))
    s[:, h] = 127 * J - J * p[:, h] + np.where(one, rng.integers(0, 101, (N, 1, 1)) + rng.integers(0, 3, (N, 1, W)), rng.integers(0, 56, (N, 1, W)) + 64 * t + rng.integers(0, 8, (N, 16, W)))
    q = int(rng.integers(0, N)); p[q] = rng.integers(0, 128, (8, 16, W)); s[q] = s[q] >> 5
    p[:, o[0]] = rng.integers(0, 128, (N, 16, 1)); s[:, o[0]] = rng.integers(0, 1024, (N, 16, 1))
    lv = rng.integers(0, 1024, (N, 1, W)); p[:, o[1]] = rng.integers(0, 2, (N, 16, W)); s[:, o[1]] = lv; s[:, o[1], int(rng.integers(0, 16))] = 1023 - lv[:, 0]
    for a in range(N):
        for g, sign in ((o[2], 1), (o[3], -1)):
            i = np.argsort(sign * s[a, g, 0][c[a, g]], axis=-1); c[a, g] = np.take_along_axis(c[a, g], i, -1)
    return pack(p, s, c, nbr, ge)
def setup_inputs_spread(rng):
    p, s, c, nbr, ge = parts(rng)
    p = np.minimum((np.exp2(7 * rng.random((N, 8, 1, W))) * rng.random((N, 8, 16, W))).astype(np.int64), 127)
    s = np.minimum((np.exp2(10 * rng.random((N, 8, 1, W))) * (0.875 + 0.125 * rng.random((N, 8, 16, W)))).astype(np.int64), 1023)
    e = rng.choice(np.array([1.0, 2.0, 4.0]), (N, 8, 1, 1))
    c = np.minimum((W * rng.random((N, 8, R, Q)) ** e).astype(np.int64), W - 1)
    nbr = np.minimum((N * R * rng.random((N, 8, J, R)) ** 2).astype(np.int64), N * R - 1)
    ge = np.minimum((W * rng.random((N, 8, J, R)) ** e).astype(np.int64), W - 1)
    return pack(p, s, c, nbr, ge)
def check_inputs(d):
    bad = []
    v = np.asarray(d["pe"]).astype(np.float32)
    if not (np.all(v >= 0) and np.all(v <= 127) and np.all(v == np.floor(v))): bad.append("range of pe")
    for k, hi in (("se", 1023), ("cand", W - 1), ("nb", N * R - 1), ("geo", W - 1)):
        if np.min(d[k]) < 0 or np.max(d[k]) > hi: bad.append("range of " + k)
    return bad
def reference(pe, se, cand, nb, geo):
    p = pe.astype(np.float32).astype(np.int32).reshape(N, 8, 16, W); s = se.astype(np.int32).reshape(N, 8, 16, W)
    qu = cand.astype(np.int64).reshape(N, 8, R, Q)
    nbl = np.stack([gentries(a) for a in nb]).astype(np.int64).reshape(N, 8, J, R); ge = np.stack([gentries(a) for a in geo]).astype(np.int64).reshape(N, 8, J, R)
    pos = np.zeros((N, 8, R, A), np.int64) + np.arange(A); head = np.full((N, 8, R, 1), A, np.int64)
    for t in range(RO):
        c = np.take_along_axis(qu, pos, 3)
        every = c.transpose(1, 0, 2, 3).reshape(8, N * R, A)
        gap = []
        for a in range(N):
            cu = every[np.arange(8)[:, None, None], nbl[a]]
            ix = (((c[a][:, None, :, :, None] * cu[:, :, :, None, :]) >> SH) + ge[a][:, :, :, None, None]) & (W - 1)
            e = np.take_along_axis(p[a], ix.reshape(8, 1, -1), 2).reshape(8, 16, J, R, A, A)
            low = np.min(e - np.roll(e, -(t + 1), axis=4), axis=5)
            own = np.take_along_axis(s[a], c[a].reshape(8, 1, -1), 2).reshape(8, 16, R, A)
            gap.append(own - np.roll(own, -(t + 1), axis=3) + np.add.reduce(low, axis=2))
        gap = np.stack(gap)
        dead = np.all(gap > 0, axis=2)
        if t < RO - 1:
            n = dead.astype(np.int64); upto = np.add.accumulate(n, axis=3)
            pos = np.where(dead, head + upto - n, pos); head = head + upto[..., -1:]
    return {"yc": np.where(dead, -1, c).reshape(N, 8, R * A).astype(np.float32), "yg": gap.reshape(N, 128, R * A).astype(np.float32)}

@@ -1,0 +1,659 @@
+from concourse.bass import DstId, RemoteDMATransfer
+from concourse.mybir import AluOpType, ActivationFunctionType
+
+BF, F32, I32, U16 = "bfloat16", "float32", "int32", "uint16"
+NCH = 4
+BIG = 1024.0
+MODE = ["PAAP", "AAAP", "AAAP", "AAAA"]
+VG = [[[(1, 0), (1, 1)], [(1, 0), (1, 1)], [(1, 0), (2, 0)], [(2, 1)]],
+      [[(1, 0), (0, 0), (0, 1)], [(1, 0), (2, 0)], [(2, 1), (0, 0), (0, 1)], [(1, 0)]],
+      [[(0, 0), (0, 1)], [(1, 0), (3, 0), (2, 0)], [(2, 1), (0, 1)], [(1, 0)]],
+      [[(1, 0), (1, 1), (0, 0)], [(1, 0), (2, 0)], [(1, 0), (2, 1)], [(1, 0), (0, 1)]]]
+NAR = [[[(1, 0), (0, 0)], [], [(3, 1)], [(2, 1), (3, 1)]],
+       [[(3, 1)], [(1, 0)], [(1, 1)], [(2, 1), (0, 0), (0, 1), (3, 1)]],
+       [[(3, 1)], [(3, 0)], [], [(2, 1), (3, 1), (0, 1), (3, 0)]],
+       [[], [], [], []]]
+FIRSTH = [1, 1, 0, 0]
+LASTHALF = [[3, 0], [3, 2], [3], []]
+SPLIT = 1024
+CYC, WAKE, EPS, GCYC, BIAS, ADDUS, DW = 1.04e-3, 0.06, 0.1, 1.6, 3.0, 2.2, 0.5
+NND, NNF, NDMA = 4, 4, 12
+SCRATCH = {
+    "pw": ("sbuf", [128, 4096], BF), "sw": ("sbuf", [128, 4096], I32), "sq": ("sbuf", [128, 1792], F32),
+    "cq": ("sbuf", [128, 1792], BF),
+    "candl": ("sbuf", [128, 112], I32), "clo": ("sbuf", [128, 112], I32), "clob": ("sbuf", [128, 112], BF),
+    "chib": ("sbuf", [128, 112], BF), "cand16": ("sbuf", [128, 112], U16),
+    "nbi": ("sbuf", [128, 16], I32), "nbu": ("sbuf", [128, 16], U16), "geoi": ("sbuf", [128, 16], I32),
+    "geof": ("sbuf", [128, 16], F32), "gm": ("sbuf", [128, 256], F32), "geor": ("sbuf", [128, 16, 4, 16], F32),
+    "w0": ("sbuf", [128, 256], F32), "w1": ("sbuf", [128, 256], F32), "w2": ("sbuf", [128, 256], F32), "w3": ("sbuf", [128, 256], F32),
+    "ones": ("sbuf", [128, 128], BF), "ip": ("sbuf", [128, 128], BF), "im": ("sbuf", [128, 128], BF),
+    "bt": ("sbuf", [128, 128], BF), "bm": ("sbuf", [128, 128], BF), "bf32": ("sbuf", [128, 128], F32), "bn": ("sbuf", [128, 128], BF),
+    "kc": ("sbuf", [128, 128], BF), "selk": ("sbuf", [128, 64, 2], BF), "csel": ("sbuf", [128, 8, 8, 8, 2], BF), "casel": ("sbuf", [128, 2, 64, 2], BF),
+    "thr": ("sbuf", [128, 128], F32), "qrow": ("sbuf", [128, 128], F32), "m16": ("sbuf", [128, 16], F32),
+    "rt0": ("sbuf", [128, 24], BF), "rt1": ("sbuf", [128, 24], BF), "rt2": ("sbuf", [128, 24], BF),
+    "rmin": ("sbuf", [128, 512], BF), "rmax": ("sbuf", [128, 512], BF),
+    "ci": ("sbuf", [128, 16], I32), "cf": ("sbuf", [128, 16], F32),
+    "posc": ("sbuf", [128, 4, 8], F32), "headc": ("sbuf", [128, 4, 8], F32), "sbase": ("sbuf", [128, 4, 8], F32), "sbf": ("sbuf", [128, 4, 8], F32),
+    "t1": ("sbuf", [128, 4, 8], F32), "t3": ("sbuf", [128, 4, 8], F32), "offc": ("sbuf", [128, 32], U16), "offs": ("sbuf", [128, 32], U16),
+    "crow": ("sbuf", [128, 4, 128], BF), "own": ("sbuf", [128, 512], F32), "ns": ("sbuf", [128, 4, 8, 16], F32), "cr": ("sbuf", [128, 8, 16], F32),
+    "nsx": ("sbuf", [128, 4, 16, 8], F32), "crx": ("sbuf", [128, 4, 16, 8], F32),
+    "cn": ("sbuf", [128, 256], F32), "idx": ("sbuf", [128, 16, 4, 16], I32), "off": ("sbuf", [128, 1024], U16),
+    "ygb": ("sbuf", [128, 64, 8], F32), "ycb": ("sbuf", [128, 64, 8], F32),
+    "d0": ("psum", [128, 512], F32), "d1": ("psum", [128, 512], F32), "d2": ("psum", [128, 512], F32), "d3": ("psum", [128, 512], F32),
+    "ca0": ("psum", [128, 2, 4, 64], F32), "ca1": ("psum", [128, 2, 4, 64], F32),
+    "jb": ("psum", [128, 4, 8, 16], F32), "mb": ("psum", [128, 4, 128], F32),
+}
+for _c in range(NCH):
+    SCRATCH["e%d" % _c] = ("sbuf", [128, 4096], BF)
+    SCRATCH["sc%d" % _c] = ("sbuf", [128, 8, 512], BF)
+    SCRATCH["flg%d" % _c] = ("sbuf", [128, 128], BF)
+    SCRATCH["dm%d" % _c] = ("sbuf", [128, 128], BF)
+    SCRATCH["n%d" % _c] = ("sbuf", [128, 512], BF)
+    SCRATCH["f%d" % _c] = ("sbuf", [128, 512], BF)
+SEMAPHORES = ["sV", "sS", "sP", "sG", "loc"] + ["arr%d" % i for i in range(4)] + ["dma%d" % i for i in range(NDMA)] + ["add%d" % i for i in range(8)]
+
+
+def slot(t, al, b):
+    s = t + 1
+    if s in (2, 4):
+        return 2 * al + b
+    return (s * al + 4 * b) % 8
+
+
+def order(prog):
+    n = len(prog)
+    wr, rd, users = {}, {}, {}
+    succs, left = [[] for _ in range(n)], []
+    for i, p in enumerate(prog):
+        s = set(wr[k] for k in p["r"] + p["w"] if k in wr)
+        for k in p["w"]:
+            s.update(rd.get(k, ()))
+        s.discard(i)
+        for k in p["r"]:
+            rd.setdefault(k, []).append(i)
+        for k in p["w"]:
+            wr[k] = i
+            rd[k] = []
+        left.append(len(s))
+        for q in s:
+            succs[q].append(i)
+        for v in p["use"]:
+            users[v] = users.get(v, 0) + 1
+    path = [0.0] * n
+    for i in range(n - 1, -1, -1):
+        p = prog[i]
+        path[i] = p["us"] + p["lat"] + (p["dma"] * DW + 1.8 if p["dma"] else 0.0) + max([path[q] + WAKE for q in succs[i]] or [0.0])
+    rank = [path[i] - BIAS * prog[i]["c"] for i in range(n)]
+    at = [0.0] * n
+    ready = [i for i in range(n) if not left[i]]
+    qfree, bank, engines = {}, {}, 0.0
+    free = {k: 0.0 for k in range(4)}
+    where, seq = {}, []
+    while ready:
+        cand = []
+        for i in ready:
+            p = prog[i]
+            t = max(at[i], qfree.get(p["e"], 0.0))
+            if p["alloc"] is not None:
+                if not free:
+                    continue
+                t = max(t, min(free.values()) + WAKE)
+            for b in p["x"]:
+                if b in bank and bank[b][0] != p["e"]:
+                    t = max(t, bank[b][1] + WAKE)
+            cand.append((t, i))
+        best, i = min(cand)
+        e = prog[i]["e"]
+        t, i = max([c for c in cand if prog[c[1]]["e"] == e and c[0] <= best + EPS], key=lambda c: (rank[c[1]], -c[1]))
+        p = prog[i]
+        if p["alloc"] is not None:
+            k = min(free, key=lambda b: free[b])
+            where[p["alloc"]] = k
+            del free[k]
+        qfree[e] = t + p["us"]
+        if p["dma"]:
+            engines = max(t + 1.2, engines) + p["dma"]
+            end = engines + .6
+        else:
+            end = t + p["us"] + p["lat"]
+        for b in p["x"]:
+            bank[b] = (e, end)
+        for v in p["use"]:
+            users[v] -= 1
+            if not users[v]:
+                free[where[v]] = end
+        ready.remove(i)
+        seq.append(i)
+        for q in succs[i]:
+            left[q] -= 1
+            at[q] = max(at[q], end + WAKE)
+            if not left[q]:
+                ready.append(q)
+    assert len(seq) == n
+    return seq, where
+
+
+def rank_program(g, core, T, topo):
+    rank = T.rank_of(core)
+    if rank is None:
+        return
+    A = AluOpType
+    COPY = ActivationFunctionType.Copy
+    V, S, P = g.vector, g.scalar, g.tensor
+    queue = {"V": V, "S": S, "P": P, "G": g, "Y": g.sync}
+
+    prog = []
+    now = [0]
+    where = {}
+
+    def rec(e, emit, r, w, x, us, lat=0.0, load=0.0, use=(), alloc=None):
+        prog.append({"e": e, "emit": emit, "r": list(r), "w": list(w), "x": list(x), "us": us, "lat": lat, "dma": load, "use": list(use), "alloc": alloc, "c": now[0]})
+
+    def op(e, calls, r=(), w=(), x=(), n=64, us=None, use=(), alloc=None, pre=None):
+        calls = calls if isinstance(calls, list) else [calls]
+
+        def emit():
+            if pre:
+                pre()
+            xs = list(x) + ["d%d" % where[v] for v in list(use) + ([alloc] if alloc is not None else [])]
+            need(e, deps(e, r, w, xs))
+            sem = "s" + e
+            for call in calls:
+                call().then_inc(T.sem[sem], 1)
+                count[sem] += 1
+            done(e, sem, count[sem], r, w, xs)
+        rec(e, emit, r, w, x, max(64, n) * CYC if us is None else us, 0.0, 0.0, use, alloc)
+
+    def dma(e, out, in_, r=(), w=(), load=0.5):
+        def emit():
+            need(e, deps("dma", r, w, ()))
+            sem = "dma%d" % ndma[0]
+            ndma[0] += 1
+            queue[e].dma_start(out, in_).then_inc(T.sem[sem], 16)
+            done(e, sem, 16, r, w)
+        rec(e, emit, r, w, (), .1, 0.0, load)
+
+    nadd = [0] * 8
+
+    def dma_add(i, out, in_, r, w):
+        def emit():
+            need("G", deps("dma", r, w, ()))
+            nadd[i] += 16
+            g.dma_start(out, in_, accum_op=A.add).then_inc(T.sem["add%d" % i], 16)
+            done("G", "add%d" % i, nadd[i], r, w)
+        rec("G", emit, r, w, (), 1.0, 0.0, ADDUS)
+
+    count = {"sV": 0, "sS": 0, "sP": 0, "sG": 0}
+    know = {e: {} for e in queue}
+    snaps = {}
+    wr, rd, bank = {}, {}, {}
+    ndma = [0]
+
+    def need(e, tokens):
+        todo = {}
+        for sem, val in tokens:
+            if know[e].get(sem, 0) < val:
+                todo[sem] = max(todo.get(sem, 0), val)
+        items = sorted(todo.items(), key=lambda it: -sum(snaps[it].values()))
+        for sem, val in items:
+            if know[e].get(sem, 0) >= val:
+                continue
+            queue[e].wait_ge(T.sem[sem], val)
+            for k, v in snaps[(sem, val)].items():
+                know[e][k] = max(know[e].get(k, 0), v)
+            know[e][sem] = max(know[e].get(sem, 0), val)
+
+    def deps(e, r, w, x):
+        own = "s" + e
+        tok = [wr[k] for k in list(r) + list(w) if k in wr]
+        for k in w:
+            tok += [q for q in rd.get(k, ()) if q[0] != own]
+        for k in x:
+            tok += [q for q in bank.get(k, {}).values() if q[0] != own]
+        return tok
+
+    def done(e, sem, val, r, w, x=()):
+        sn = dict(know[e])
+        sn[sem] = val
+        snaps[(sem, val)] = sn
+        tok = (sem, val)
+        for k in r:
+            rd[k] = [q for q in rd.get(k, []) if q[0] != sem] + [tok]
+        for k in w:
+            wr[k] = tok
+            rd[k] = []
+        for k in x:
+            bank.setdefault(k, {})[sem] = tok
+
+    W = [T.w0, T.w1, T.w2, T.w3]
+    D = [T.d0, T.d1, T.d2, T.d3]
+    E = [T["e%d" % c] for c in range(NCH)]
+    SC = [T["sc%d" % c] for c in range(NCH)]
+    RT = [T.rt0, T.rt1, T.rt2]
+    CA = [T.ca0, T.ca1]
+    others = [c for c in T.cores if c != core]
+
+    def ts(out, in0, s1, op0, s2=None, op1=None):
+        if op1 is None:
+            return lambda: V.tensor_scalar(out, in0, s1, None, op0)
+        return lambda: V.tensor_scalar(out, in0, s1, s2, op0, op1)
+
+    def tt(out, a, b, o):
+        return lambda: V.tensor_tensor(out, a, b, o)
+
+    def cp(out, a):
+        return lambda: V.tensor_copy(out, a)
+
+    def ms(out, v):
+        return lambda: V.memset(out, v)
+
+    def mm(out, l, rhs, st, sp):
+        return lambda: P.matmul(out, l, rhs, st, sp)
+
+    def gat(n):
+        return .05 + GCYC * CYC * n
+
+    dma("Y", T.candl[:], T.cand[:], w=["candl"])
+    dma("Y", T.pw[:, 0:SPLIT], T.pe[:, 0:SPLIT], w=["pwa", "yq"], load=1.0)
+    dma("S", T.geoi[:], T.geo[:], w=["geoi"])
+    dma("S", T.nbi[:], T.nb[:], w=["nbi"])
+
+    ci, cf = T.ci, T.cf
+
+    def icol(k):
+        return ci[:, k:k + 1]
+
+    def fcol(k):
+        return cf[:, k:k + 1]
+
+    FREE = {"allow_small_or_imprecise_dtypes": True}
+    op("G", lambda: g.iota(icol(0), [[0, 1]], 0, 1), w=["ci0"], us=.13)
+    op("G", lambda: g.iota(T.posc[:], [[448, 4], [1, 8]], 0, 0, **FREE), w=["posc0", "posc3"], us=.2)
+    op("V", ms(T.ones[:], 1.0), w=["ones"])
+    op("V", ms(T.cq[:], 0.0), w=["cq"], n=896)
+    op("G", lambda: g.affine_select(T.bt[:], T.ones[:], [[-16, 8], [0, 16]], A.is_ge, 0.0, 0, 1), r=["ones"], w=["bt"], us=.43)
+    op("G", lambda: g.affine_select(T.bm[:], T.bt[:], [[16, 8], [0, 16]], A.is_ge, 0.0, 15, -1), r=["bt"], w=["bm"], us=.43)
+    op("G", lambda: g.iota(T.qrow[:], [[0, 8], [1, 16]], 0, 0, **FREE), w=["qrow"], us=.4)
+    op("G", lambda: g.affine_select(T.ip[:], T.ones[:], [[-1, 128]], A.is_equal, 0.0, 0, 1), r=["ones"], w=["ip"], us=.43)
+    op("G", lambda: g.iota(T.headc[:], [[448, 4], [0, 8]], 8, 0, **FREE), w=["headc0", "headc3"], us=.2)
+    op("G", lambda: g.iota(T.sbase[:], [[-7164, 4], [0, 8]], 0, 0, **FREE), w=["sbase"], us=.2)
+    op("V", ts(icol(1), icol(0), 15, A.bitwise_and), r=["ci0"], w=["ci1"])
+    op("V", cp(fcol(1), icol(1)), r=["ci1"], w=["cf1"])
+    op("V", ts(fcol(2), fcol(1), 28.0, A.mult), r=["cf1"], w=["cf2"])
+    op("V", ts(fcol(3), fcol(1), 1.5, A.is_lt), r=["cf1"], w=["cf3"])
+    op("V", ts(T.posc[:], T.posc[:], fcol(2), A.add), r=["posc0", "posc3", "cf2"], w=["posc0", "posc3"])
+    op("V", ts(T.clo[:], T.candl[:], 63, A.bitwise_and), r=["candl"], w=["clo"], n=112)
+    op("V", tt(T.chib[:], T.candl[:], T.clo[:], A.subtract), r=["clo", "candl"], w=["chib"], n=224)
+    op("V", cp(T.clob[:], T.clo[:]), r=["clo"], w=["clob"], n=112)
+    dma("Y", T.cq[0:128:16, :], T.chib[:], r=["chib", "cq", "yq"], w=["cqh", "cqw"])
+    dma("Y", T.cq[1:128:16, :], T.clob[:], r=["clob", "cq", "yq"], w=["cql", "cqv"])
+    dma("Y", T.pw[:, SPLIT:4096], T.pe[:, SPLIT:4096], w=["pw", "cqw"], load=2.4)
+    dma("Y", T.sw[:], T.se[:], w=["sw", "cqw"], load=6.5)
+    op("V", ms(T.csel[:], 0.0), w=["csel"], n=512)
+    op("V", ms(T.casel[:], 0.0), w=["casel"], n=128)
+    op("V", ts(T.selk[:], T.bm[:], fcol(3), A.mult), r=["bm", "cf3"], w=["selk"])
+    op("V", ts(T.m16[:], T.qrow[:, 0:16], fcol(1), A.is_equal), r=["qrow", "cf1"], w=["m16"])
+    op("V", cp(T.geof[:], T.geoi[:]), r=["geoi"], w=["geof"])
+    op("V", cp(T.bf32[:], T.bm[:]), r=["bm"], w=["bf32"], n=128)
+    for u in range(8):
+        op("V", cp(T.csel[:, u, :, u, :], T.selk[:, u:64:8, :]), r=["selk", "csel"], w=["cselu%d" % u])
+    for b in range(2):
+        op("V", cp(T.casel[:, b, :, b], T.selk[:, :, b]), r=["selk", "casel"], w=["caselb%d" % b])
+    GM = ["gm%d%d" % (c, j) for c in range(NCH) for j in range(4)]
+    for c in range(NCH):
+        for j in range(4):
+            lo = 64 * c + 16 * j
+            op("V", ts(T.gm[:, lo:lo + 16], T.m16[:], T.geof[:, 4 * j + c:4 * j + c + 1], A.mult), r=["m16", "geof"], w=["gm%d%d" % (c, j)])
+    op("P", mm(T.jb[:, 2:4, :, :], T.bf32[:], T.gm[:], True, True), r=["bf32"] + GM, w=["jbg"], x=["jb"], us=.8)
+    for c in range(NCH):
+        for al in range(4):
+            o, i = T.geor[:, 4 * c + al, :, :], T.jb[:, 2 + c // 2, 4 * (c % 2):4 * (c % 2) + 4, :]
+            op("S", lambda o=o, i=i: S.activation(o, i, COPY, bias=-65536.0, scale=16.0), r=["jbg"], w=["geor%d" % (4 * c + al)], x=["jb"])
+
+    def crow_of(a, t, c0=0, c1=NCH):
+        return T.crow[:, c0:c1, 16 * a:16 * a + 16] if t else T.cq[:, a:1792:28]
+
+    def crow_keys(t, c0=0, c1=NCH):
+        return ["crow%d" % c for c in range(c0, c1)] if t else ["cq", "cqh", "cql"]
+
+    nsig = [0] * 4
+
+    def send_codes(t, c0, c1):
+        op("P", [mm(T.jb[:, 1, c0:c1, :], T.csel[:, u, :, :, :], crow_of(u, t, c0, c1), u == 0, u == 7) for u in range(8)],
+           r=crow_keys(t, c0, c1) + ["cselu%d" % u for u in range(8)], w=["jbc"], x=["jb"], us=.35)
+        mine = W[t][:, 64 * rank + 16 * c0:64 * rank + 16 * c1]
+        key = "wown%d%d" % (t, c0)
+        op("V", cp(mine, T.jb[:, 1, c0:c1, :]), r=["jbc"], w=[key], x=["jb"])
+
+        def emit():
+            need("G", deps("G", [key], [], []))
+            m = topo.mask(core, others[0])
+            ids = []
+            for o in others:
+                m &= topo.mask(core, o)
+                a = topo.addr(o)
+                ids.append(DstId(rid=a[0], pnc=a[1]))
+            tr = RemoteDMATransfer(dst_ids=ids, dma_engine_mask=m, remote_sem=T.sem["arr%d" % t], srcs=[mine], dsts=[mine for _ in ids])
+            g.remote_dma_fused([tr], local_sem=T.sem.loc)
+            nsig[t] += bin(m).count("1")
+        rec("G", emit, [key], ["sent%d%d" % (t, c0)], [], .6, 3.0 if t else 5.0)
+
+    def own_codes(t):
+        for al in range(4):
+            calls = [mm(CA[al // 2][:, al % 2, j, :], T.casel[:, b, :, :], crow_of(slot(t, al, b), t), b == 0, b == 1) for j in range(4) for b in range(2)]
+            op("P", calls, r=crow_keys(t) + ["caselb0", "caselb1"], w=["ca%d" % al] + ["pr%d" % (4 * c + al) for c in range(NCH)], x=["cab%d" % (al // 2)], us=.35)
+
+    def self_gaps(t):
+        op("V", ts(T.sbf[:], T.posc[:], 16.0, A.mult), r=["posc0", "posc3"], w=["sbf"])
+        op("V", tt(T.sbf[:], T.sbf[:], T.sbase[:], A.add), r=["sbf", "sbase"], w=["sbf"])
+        for c in range(NCH):
+            op("V", cp(T.offs[:, c:32:4], T.sbf[:, c, :]), r=["sbf"], w=["offs%d" % c])
+        op("S", lambda: S.activation(T.own[:], T.sq[:].indirect(T.offs[:]), COPY), r=["sq"] + ["offs%d" % c for c in range(NCH)], w=["own"], us=gat(512))
+        for k in range(8):
+            a = slot(t, k // 2, k % 2)
+            b = (a + 1 + t) % 8
+            if t < 3:
+                op("V", tt(T.ns[:, :, k, :], T.own[:, 64 * b:64 * b + 64], T.own[:, 64 * a:64 * a + 64], A.subtract), r=["own"], w=["ns%d" % k], n=128)
+            else:
+                op("V", tt(T.nsx[:, 0:3, :, k], T.own[:, 64 * b:64 * b + 48], T.own[:, 64 * a:64 * a + 48], A.subtract), r=["own"], w=["nsx%d" % k], n=96)
+                op("V", tt(T.ns[:, 3, k, :], T.own[:, 64 * b + 48:64 * b + 64], T.own[:, 64 * a + 48:64 * a + 64], A.subtract), r=["own"], w=["ns%d" % k])
+
+    NS = ["ns%d" % k for k in range(8)]
+    NX = ["nsx%d" % k for k in range(8)]
+    MB = ["mbp%d" % c for c in range(NCH)]
+
+    def code_rows():
+        op("P", [mm(T.mb[:], T.selk[:], T.crow[:], True, True)], r=crow_keys(3) + ["selk"], w=MB, x=["mb"], us=.3)
+        for a in range(8):
+            op("V", cp(T.crx[:, 0:3, :, a], T.mb[:, 0:3, 16 * a:16 * a + 16]), r=MB, w=["crx%d" % a], x=["mb"])
+            op("V", cp(T.cr[:, a, :], T.mb[:, 3, 16 * a:16 * a + 16]), r=MB, w=["cr%d" % a], x=["mb"])
+
+    waited = {}
+
+    def neighbours(t, c0, c1):
+        def pre():
+            if t not in waited:
+                waited[t] = 1
+                V.wait_ge(T.sem["arr%d" % t], 3 * nsig[t])
+        op("V", cp(T.cn[:, 64 * c0:64 * c1], W[t][:].indirect(T.nbu[:, 4 * c0:4 * c1])), r=["nbu", "wown%d0" % t, "wown%d3" % t, "sent%d0" % t, "sent%d3" % t],
+           w=["cn%d" % c for c in range(c0, c1)], us=gat(64 * (c1 - c0)), pre=pre)
+
+    def index(c, groups):
+        for als in groups:
+            ks = [4 * c + al for al in als]
+            for al in als:
+                ca = CA[al // 2][:, al % 2, :, 16 * c:16 * c + 16]
+                op("V", tt(ca, T.cn[:, 64 * c:64 * c + 64], ca, A.mult), r=["cn%d" % c, "ca%d" % al], w=["pr%d" % (4 * c + al)], x=["cab%d" % (al // 2)])
+            for al in als:
+                k = 4 * c + al
+                ca = CA[al // 2][:, al % 2, :, 16 * c:16 * c + 16]
+                op("V", tt(T.idx[:, k, :, :], ca, T.geor[:, k, :, :], A.add), r=["pr%d" % k, "geor%d" % k], w=["ix%d" % k], x=["cab%d" % (al // 2)])
+            IX = ["ix%d" % k for k in ks]
+            v = T.idx[:, ks[0]:ks[-1] + 1, :, :]
+            op("V", ts(v, v, 4, A.arith_shift_right, 4095, A.bitwise_and), r=IX, w=IX, n=64 * len(ks))
+            op("V", cp(T.off[:, 64 * ks[0]:64 * ks[-1] + 64], v), r=IX, w=["of%d" % k for k in ks], n=64 * len(ks))
+
+    def gather(c, al, hs, sign=1.0, e="S"):
+        k = 4 * c + al
+        lo, n = 64 * k + 32 * hs[0], 32 * len(hs)
+        out, src = E[c][:, 16 * lo - 4096 * c:16 * (lo + n) - 4096 * c], T.pw[:].indirect(T.off[:, lo:lo + n])
+        if e == "V":
+            call = cp(out, src) if sign == 1.0 else ts(out, src, sign, A.mult)
+        else:
+            call = lambda: S.activation(out, src, COPY, scale=sign)
+        op(e, call, r=["pw", "pwa", "of%d" % k], w=["e%d%d%d" % (c, al, h) for h in hs], us=gat(16 * n))
+
+    def added(c, i, into, what):
+        p, q = 1024 * into, 1024 * what
+        dma_add(2 * c + i, E[c][:, p:p + 1024], E[c][:, q:q + 1024], ["e%d%d%d" % (c, what, h) for h in range(2)], ["e%d%d%d" % (c, into, h) for h in range(2)])
+
+    def held(c, al, h):
+        return (E[c], "e%d%d%d" % (c, al, h), 0, 1024 * al + 512 * h)
+
+    nv, nn, nf = [0], [0], [0]
+
+    def bank_diff(terms, r):
+        v = nv[0]
+        nv[0] += 1
+
+        def call(j, b, i):
+            buf, col, fl, sg = terms[i]
+            lo = col + 256 * j
+            rhs = buf[:, lo + (1 - b if fl else b):lo + 256:2]
+            o = 256 * j + 128 * b
+            return lambda: P.matmul(D[where[v]][:, o:o + 128], (T.ip if sg > 0 else T.im)[:], rhs, i == 0, i == len(terms) - 1)
+        calls = [call(j, b, i) for j in range(2) for b in range(2) for i in range(len(terms))]
+        op("P", calls, r=list(r) + ["ip", "im"], w=["vd%d" % v], us=.085 * len(calls), alloc=v)
+        return (v, "vd%d" % v, 1, 0)
+
+    def narrowed(src):
+        i = nn[0] % NND
+        nn[0] += 1
+        out, v = T["n%d" % i], src[0]
+        op("S", lambda: S.activation(out[:], D[where[v]][:], COPY), r=[src[1]], w=["n%d" % i], use=[v], n=512)
+        return (out, "n%d" % i, 2, 0)
+
+    def fused(c, h, al, other):
+        i = nf[0] % NNF
+        nf[0] += 1
+        out, key = T["f%d" % i], "f%d" % i
+        k = 4 * c + al
+        lo = 64 * k + 32 * h
+        p = 1024 * other + 512 * h
+        op("V", tt(out[:], T.pw[:].indirect(T.off[:, lo:lo + 32]), E[c][:, p:p + 512], A.subtract), r=["pw", "pwa", "of%d" % k, "e%d%d%d" % (c, other, h)], w=[key], us=gat(512))
+        return (out, key, 0, 0)
+
+    def scan(c, al, h, src, low):
+        rp = T.rmin if low else T.rmax
+        o0, o1 = (A.max, A.min) if low else (A.min, A.max)
+        k = 4 * h + al
+        if src[2] == 1:
+            calls = [lambda: V.tensor_tensor_scan(SC[c][:, k, :], rp[:], D[where[src[0]]][:], 0.0, o0, o1)]
+        elif src[2] == 2:
+            calls = [lambda: V.tensor_tensor_scan(SC[c][:, k, :], rp[:], src[0][:], 0.0, o0, o1)]
+        else:
+            calls = [lambda j=j, b=b: V.tensor_tensor_scan(SC[c][:, k, 256 * j + 128 * b:256 * j + 128 * b + 128], rp[:, 0:128],
+                                                           src[0][:, src[3] + 256 * j + b:src[3] + 256 * j + 256:2], 0.0, o0, o1) for j in range(2) for b in range(2)]
+        op("V", calls, r=[src[1], "rmin" if low else "rmax"], w=["sc%d%d%d" % (c, al, h)], use=[src[0]] if src[2] == 1 else [], us=(512 if src[2] == 1 else 256) * CYC)
+
+    def jsum(c, sets):
+        calls = []
+        for k0, k1, low in sets:
+            for j in range(4):
+                h, lo = 4 * (j // 2), 256 * (j % 2)
+                calls.append(mm(T.jb[:, 0, 2 * k0:2 * k1, :], (T.ip if low else T.im)[:], SC[c][:, h + k0:h + k1, lo + 7:lo + 256:8], j == 0, j == 3))
+        op("P", calls, r=["ip", "im"] + ["sc%d%d%d" % (c, al, h) for al in range(4) for h in range(2)], w=["jbs"], x=["jb"], us=.045 * len(calls))
+
+    def chunk(t, c):
+        flip = (t != 1)
+        onv, nar = VG[t][c], NAR[t][c]
+        vg = [h for h in range(2) if (1, h) in onv]
+        a = MODE[t][c] == "A"
+        first = [FIRSTH[t], 1 - FIRSTH[t]]
+        halves = [[h] for h in first] if c in LASTHALF[t] else [[0, 1]]
+
+        def gathers(al, hs, sign=1.0, skip=()):
+            for e in "VS":
+                h2 = [h for h in hs if ((al, h) in onv) == (e == "V") and h not in skip]
+                if h2:
+                    gather(c, al, h2, sign, e)
+
+        def diff(k, h, p, q, sp, sq, fl=False):
+            d = bank_diff([(E[c], 1024 * p + 512 * h, False, sp), (E[c], 1024 * q + 512 * h, fl, sq)], ["e%d%d%d" % (c, p, h), "e%d%d%d" % (c, q, h)])
+            return narrowed(d) if (k, h) in nar else d
+
+        if t < 3 and a:
+            for al, sign in ((2, -1.0), (1, 1.0), (0, -1.0), (3, 1.0)):
+                for hs in halves:
+                    gathers(al, hs, sign)
+            m12 = [diff(1, h, 1, 2, 1, 1) for h in range(2)]
+            added(c, 0, 1, 0)
+            m30 = [diff(3, h, 3, 0, 1, 1, flip) for h in range(2)]
+            added(c, 1, 2, 3)
+            for al, src, low in ((1, m12, True), (3, m30, True), (0, [held(c, 1, h) for h in range(2)], False), (2, [held(c, 2, h) for h in range(2)], False)):
+                for h in range(2):
+                    scan(c, al, h, src[h], low)
+            return [(0, 1, False), (1, 2, True), (2, 3, False), (3, 4, True)]
+        if t < 3:
+            for hs in halves:
+                for al in range(4):
+                    gathers(al, hs, 1.0, vg if al == 1 else ())
+            for h in first:
+                if h in vg:
+                    f = fused(c, h, 1, 0)
+                    d = bank_diff([(f[0], 0, False, 1), (E[c], 512 * h, False, 1), (E[c], 2048 + 512 * h, False, -1)], [f[1], "e%d0%d" % (c, h), "e%d2%d" % (c, h)])
+                    d = narrowed(d) if (1, h) in nar else d
+                else:
+                    f = diff(0, h, 1, 0, 1, -1)
+                    d = None
+                scan(c, 0, h, f, False)
+                scan(c, 1, h, d or diff(1, h, 1, 2, 1, -1), True)
+                scan(c, 2, h, diff(2, h, 2, 3, 1, -1), True)
+                scan(c, 3, h, diff(3, h, 3, 0, 1, -1, flip), True)
+            return [(0, 1, False), (1, 4, True)]
+        gathers(3, [0, 1], 1.0 if vg else -1.0)
+        gathers(1, [0, 1], 1.0, vg)
+        if not vg:
+            added(c, 1, 1, 3)
+        gathers(2, [0, 1], -1.0)
+        gathers(0, [0, 1])
+        added(c, 0, 0, 2)
+        for h in range(2):
+            s = fused(c, h, 1, 3) if h in vg else (diff(1, h, 1, 3, 1, -1) if vg else held(c, 1, h))
+            scan(c, 1, h, s, True)
+            scan(c, 3, h, s, False)
+        for h in range(2):
+            scan(c, 0, h, held(c, 0, h), True)
+            scan(c, 2, h, held(c, 0, h), False)
+        return [(0, 2, True), (2, 4, False)]
+
+    def outputs(c, sets):
+        calls = []
+        for k0, k1, low in sets:
+            for k in range(2 * k0, 2 * k1):
+                for j in range(4):
+                    lo = 256 * (j % 2) + 128 * (k % 2)
+                    calls.append(mm(T.mb[:, 0, k:128:8], (T.ip if low else T.im)[:], SC[c][:, 4 * (j // 2) + k // 2, lo + 7:lo + 128:8], j == 0, j == 3))
+        op("P", calls, r=["ip", "im"] + ["sc%d%d%d" % (c, al, h) for al in range(4) for h in range(2)], w=["mbp0"], x=["mb"], us=.045 * len(calls))
+        flg = T["flg%d" % c]
+        op("V", tt(flg[:], T.mb[:, 0, :], T.nsx[:, c, :, :], A.is_gt), r=["mbp0"] + NX, w=["flg%d" % c], x=["mb"], n=128)
+        op("P", [mm(T.mb[:, 1, :], T.kc[:], T.ones[:], True, False), mm(T.mb[:, 1, :], T.bn[:], flg[:], False, True)],
+           r=["flg%d" % c, "bn", "kc", "ones"], w=["mbp1"], x=["mb"], us=.15)
+        op("V", tt(T.ygb[:, 16 * c:16 * c + 16, :], T.mb[:, 0, :], T.nsx[:, c, :, :], A.subtract), r=["mbp0"] + NX, w=["yg%d" % c], x=["mb"], n=128)
+        op("V", tt(T.ycb[:, 16 * c:16 * c + 16, :], T.mb[:, 1, :], T.crx[:, c, :, :], A.min), r=["mbp1"] + ["crx%d" % k for k in range(8)], w=["yc%d" % c], x=["mb"], n=128)
+
+    def post(t, c, sets):
+        if t == 3 and c < 3:
+            outputs(c, sets)
+            return
+        jsum(c, sets)
+        flg, dm = T["flg%d" % c], T["dm%d" % c]
+        op("V", tt(flg[:], T.jb[:, 0, :, :], T.ns[:, c, :, :], A.is_gt), r=["jbs"] + NS, w=["flg%d" % c], x=["jb"], n=128)
+        if t == 3:
+            for k in range(8):
+                op("V", tt(T.ygb[:, 16 * c:16 * c + 16, k], T.jb[:, 0, k, :], T.ns[:, c, k, :], A.subtract), r=["jbs"] + NS, w=["yg%d%d" % (c, k)], x=["jb"])
+            op("P", [mm(T.mb[:, 0, :], T.kc[:], T.ones[:], True, False), mm(T.mb[:, 0, :], T.bn[:], flg[:], False, True)],
+               r=["flg%d" % c, "bn", "kc", "ones"], w=["mbp0"], x=["mb"], us=.15)
+            for k in range(8):
+                op("V", tt(T.ycb[:, 16 * c:16 * c + 16, k], T.mb[:, 0, 16 * k:16 * k + 16], T.cr[:, k, :], A.min), r=["mbp0", "cr%d" % k], w=["yc%d%d" % (c, k)], x=["mb"])
+            return
+        op("P", mm(T.jb[:, 2, :, :], flg[:], T.bm[:], True, True), r=["flg%d" % c, "bm"], w=["jbg"], x=["jb"], us=.08)
+        op("V", tt(dm[:], T.jb[:, 2, :, :], T.thr[:], A.is_ge), r=["jbg", "thr"], w=["dm%d" % c], x=["jb"], n=128)
+        op("P", mm(T.mb[:, c, 0:24], dm[:], RT[t][:], True, True), r=["dm%d" % c, "rt%d" % t], w=["mbp%d" % c], x=["mb"], us=.06)
+
+    def places(c0, c1):
+        p, h, k = T.posc[:, c0:c1, :], T.headc[:, c0:c1, :], c0
+        P3 = MB[c0:c1]
+        op("V", tt(T.t1[:, c0:c1, :], T.mb[:, c0:c1, 0:8], p, A.add), r=P3 + ["posc%d" % k], w=["t1%d" % k], x=["mb"])
+        op("V", tt(T.t3[:, c0:c1, :], T.mb[:, c0:c1, 8:16], h, A.add), r=P3 + ["headc%d" % k], w=["t3%d" % k], x=["mb"])
+        op("V", tt(p, T.t1[:, c0:c1, :], T.t3[:, c0:c1, :], A.min), r=["t1%d" % k, "t3%d" % k], w=["posc%d" % k])
+        op("V", cp(T.offc[:, 8 * c0:8 * c1], p), r=["posc%d" % k], w=["offc%d" % k])
+        for c in range(c0, c1):
+            op("V", cp(T.crow[:, c, :], T.cq[:].indirect(T.offc[:, 8 * c:8 * c + 8])), r=["cq", "cqh", "cql", "offc%d" % k], w=["crow%d" % c], us=gat(128))
+        op("V", tt(h, T.mb[:, c0:c1, 16:24], h, A.add), r=P3 + ["headc%d" % k], w=["headc%d" % k], x=["mb"])
+
+    send_codes(0, 0, NCH)
+    own_codes(0)
+
+    for j in range(4):
+        op("V", cp(T.nbu[:, j:16:4], T.nbi[:, 4 * j:4 * j + 4]), r=["nbi"], w=["nbu"])
+    op("V", ts(icol(3), icol(0), 5, A.arith_shift_right), r=["ci0"], w=["ci3"])
+    op("V", ts(icol(4), icol(0), 4, A.arith_shift_right, 1, A.bitwise_and), r=["ci0"], w=["ci4"])
+    op("V", ts(icol(5), icol(1), 3, A.bitwise_and), r=["ci1"], w=["ci5"])
+    op("V", ts(icol(6), icol(1), 2, A.arith_shift_right), r=["ci1"], w=["ci6"])
+    op("V", cp(fcol(0), icol(0)), r=["ci0"], w=["cf0"])
+    for k in (3, 4, 5, 6):
+        op("V", cp(fcol(k + 2), icol(k)), r=["ci%d" % k], w=["cf%d" % (k + 2)])
+    op("V", ms(T.rmin[:], -BIG), w=["rmin"], n=256)
+    op("V", ms(T.rmax[:], BIG), w=["rmax"], n=256)
+    op("V", ts(T.im[:], T.ip[:], -1.0, A.mult), r=["ip"], w=["im"])
+    op("V", ts(fcol(9), fcol(6), 4.0, A.mult), r=["cf6"], w=["cf9"])
+    op("V", ts(fcol(11), fcol(5), 2.0, A.mult), r=["cf5"], w=["cf11"])
+    op("V", ts(fcol(12), fcol(5), 3.0, A.mult), r=["cf5"], w=["cf12"])
+    op("V", ms(T.rmin[:, 0:512:8], BIG), w=["rmin"])
+    op("V", ms(T.rmax[:, 0:512:8], -BIG), w=["rmax"])
+    op("V", ts(T.headc[:], T.headc[:], fcol(2), A.add), r=["headc0", "headc3", "cf2"], w=["headc0", "headc3"])
+    op("V", tt(fcol(10), fcol(9), fcol(5), A.add), r=["cf9", "cf5"], w=["cf10"])
+    op("V", tt(fcol(11), fcol(11), fcol(6), A.add), r=["cf11", "cf6"], w=["cf11"])
+    op("V", tt(icol(7), fcol(12), fcol(9), A.add), r=["cf12", "cf9"], w=["ci7"])
+    op("V", ts(icol(8), icol(7), 7, A.bitwise_and), r=["ci7"], w=["ci8"])
+    op("V", cp(fcol(12), icol(8)), r=["ci8"], w=["cf12"])
+    for t in range(3):
+        a = fcol(10 + t)
+        k = "cf%d" % (10 + t)
+        op("V", ts(RT[t][:, 0:8], T.qrow[:, 0:8], a, A.is_equal, 4096.0, A.mult), r=["qrow", k], w=["rta%d" % t])
+        op("V", ts(RT[t][:, 8:16], T.qrow[:, 0:8], a, A.is_gt), r=["qrow", k], w=["rtb%d" % t])
+        op("V", ms(RT[t][:, 16:24], 1.0), r=["rta%d" % t, "rtb%d" % t], w=["rt%d" % t])
+    op("V", ts(T.thr[:], T.qrow[:], fcol(1), A.not_equal, 1000.0, A.mult), r=["qrow", "cf1"], w=["thr"], n=128)
+    op("V", ts(fcol(13), fcol(7), 448.0, A.mult), r=["cf7"], w=["cf13"])
+    op("V", ts(fcol(14), fcol(1), -448.0, A.mult), r=["cf1"], w=["cf14"])
+    op("V", ts(T.thr[:], T.thr[:], 15.5, A.max), r=["thr"], w=["thr"], n=128)
+    op("V", tt(fcol(13), fcol(13), fcol(8), A.add), r=["cf13", "cf8"], w=["cf13"])
+    op("V", cp(T.cand16[:], T.candl[:]), r=["candl"], w=["cand16"], n=112)
+    op("V", tt(fcol(13), fcol(13), fcol(14), A.add), r=["cf13", "cf14"], w=["cf13"])
+    op("V", ts(T.sbase[:], T.sbase[:], fcol(13), A.add), r=["sbase", "cf13"], w=["sbase"])
+    op("V", cp(T.sq[:], T.sw[:].indirect(T.cand16[:])), r=["sw", "cand16"], w=["sq"], us=gat(1792))
+    self_gaps(0)
+
+    for t in range(4):
+        neighbours(t, 0, 1)
+        index(0, [[2], [1], [0], [3]])
+        neighbours(t, 1, NCH)
+        for c in range(1, NCH):
+            index(c, [[0, 1, 2, 3]])
+        for c in range(NCH):
+            now[0] = c
+            sets = chunk(t, c)
+            if t == 3 and c == 3:
+                dma("Y", T.yg[:, 0:384], T.ygb[:, 0:48, :], r=["yg%d" % i for i in range(3)])
+                dma("Y", T.yc[:, 0:384], T.ycb[0:128:16, 0:48, :], r=["yc%d" % i for i in range(3)])
+            post(t, c, sets)
+            if t < 3 and c == 2:
+                places(0, 3)
+                send_codes(t + 1, 0, 3)
+        now[0] = 0
+        if t < 3:
+            places(3, 4)
+            send_codes(t + 1, 3, 4)
+            own_codes(t + 1)
+            self_gaps(t + 1)
+        if t == 2:
+            code_rows()
+            op("V", ts(T.bn[:], T.bm[:], -4096.0, A.mult), r=["bm"], w=["bn"])
+            op("V", ts(fcol(14), fcol(0), 0.0, A.is_equal, 65536.0, A.mult), r=["cf0"], w=["cf14"])
+            op("V", ts(fcol(15), fcol(0), 1.0, A.is_equal), r=["cf0"], w=["cf15"])
+            op("V", tt(fcol(14), fcol(14), fcol(15), A.subtract), r=["cf14", "cf15"], w=["cf14"])
+            op("V", ts(T.kc[:], T.ones[:], fcol(14), A.mult), r=["ones", "cf14"], w=["kc"])
+    dma("Y", T.yg[:, 384:512], T.ygb[:, 48:64, :], r=["yg3%d" % k for k in range(8)])
+    dma("S", T.yc[:, 384:512], T.ycb[0:128:16, 48:64, :], r=["yc3%d" % k for k in range(8)])
+
+    seq, banks = order(prog)
+    where.update(banks)
+    for i in seq:
+        prog[i]["emit"]()
+    g.wait_ge(T.sem.loc, sum(nsig))
+    for e in ("sV", "sS", "sP", "sG"):
+        if know["Y"].get(e, 0) < count[e]:
+            g.sync.wait_ge(T.sem[e], count[e])
+    for i in range(ndma[0]):
+        g.sync.wait_ge(T.sem["dma%d" % i], 16)

@@ -1,63 +1,60 @@
 from concourse.bass import DstId, RemoteDMATransfer
 from concourse.mybir import AluOpType, ActivationFunctionType
 
-BF, F32, I32, U16 = "bfloat16", "float32", "int32", "uint16"
-NCH = 4
+BF, F16, F32, I32, U16 = "bfloat16", "float16", "float32", "int32", "uint16"
 BIG = 1024.0
-MODE = ["PAAP", "AAAP", "AAAP", "AAAA"]
-VG = [[[(1, 0), (1, 1)], [(1, 0), (1, 1)], [(1, 0), (2, 0)], [(2, 1)]],
-      [[(1, 0), (0, 0), (0, 1)], [(1, 0), (2, 0)], [(2, 1), (0, 0), (0, 1)], [(1, 0)]],
-      [[(0, 0), (0, 1)], [(1, 0), (3, 0), (2, 0)], [(2, 1), (0, 1)], [(1, 0)]],
-      [[(1, 0), (1, 1), (0, 0)], [(1, 0), (2, 0)], [(1, 0), (2, 1)], [(1, 0), (0, 1)]]]
-NAR = [[[(1, 0), (0, 0)], [], [(3, 1)], [(2, 1), (3, 1)]],
-       [[(3, 1)], [(1, 0)], [(1, 1)], [(2, 1), (0, 0), (0, 1), (3, 1)]],
-       [[(3, 1)], [(3, 0)], [], [(2, 1), (3, 1), (0, 1), (3, 0)]],
-       [[], [], [], []]]
-FIRSTH = [1, 1, 0, 0]
-LASTHALF = [[3, 0], [3, 2], [3], []]
-SPLIT = 1024
-CYC, WAKE, EPS, GCYC, BIAS, ADDUS, DW = 1.04e-3, 0.06, 0.1, 1.6, 3.0, 2.2, 0.5
-NND, NNF, NDMA = 4, 4, 12
+MODE = [["PPF", "PAF", "AAF", "PAF"], ["AAP", "PAF", "AAP", "PAF"], ["AAP", "PAF", "AAP", "PAF"], ["AF", "AA", "AF", "AF"]]
+VG = [[[], [], [], []], [[], [], [], []], [[], [], [], []], [[], [], [], []]]
+UNITS = [[(0, 2), (0, 0), (0, 3), (0, 1), (1, 2), (1, 1), (1, 3), (1, 0)], [(0, 2), (0, 0), (0, 3), (0, 1), (1, 2), (1, 0), (1, 3), (1, 1)]]
+LISTS = [[(0, [2]), (0, [0]), (0, [3]), (0, [1]), (1, [0, 1, 2, 3])], [(0, [2]), (0, [0]), (0, [3]), (0, [1]), (1, [0, 1, 2, 3])]]
+HALVES = [[(1, 0)], []]
+EARLY = [0, 1]
+CHAIN = "S"
+PACE = [0, 0, 0, 1, 4, 7, 8, 9]
+ON = {"flag": "V", "dead": "V", "cn": "V", "mine": "V", "yg": "S", "rows": "S"}
+CYC, PEC, WAKE, EPS, GCYC, BIAS, ADDUS, DW, FLIGHT = 0.85e-3, 0.72e-3, 0.06, 0.2, 1.56, 0.0, 1.7, 1.0, 4.4
+TAB, SEND = 3.1, 1.2
+PASSES, KEEP, MIX = 12, 1.0, 0.8
+ORDER = []
+ND, NDMA = 4, 30
 SCRATCH = {
-    "pw": ("sbuf", [128, 4096], BF), "sw": ("sbuf", [128, 4096], I32), "sq": ("sbuf", [128, 1792], F32),
-    "cq": ("sbuf", [128, 1792], BF),
-    "candl": ("sbuf", [128, 112], I32), "clo": ("sbuf", [128, 112], I32), "clob": ("sbuf", [128, 112], BF),
-    "chib": ("sbuf", [128, 112], BF), "cand16": ("sbuf", [128, 112], U16),
-    "nbi": ("sbuf", [128, 16], I32), "nbu": ("sbuf", [128, 16], U16), "geoi": ("sbuf", [128, 16], I32),
-    "geof": ("sbuf", [128, 16], F32), "gm": ("sbuf", [128, 256], F32), "geor": ("sbuf", [128, 16, 4, 16], F32),
-    "w0": ("sbuf", [128, 256], F32), "w1": ("sbuf", [128, 256], F32), "w2": ("sbuf", [128, 256], F32), "w3": ("sbuf", [128, 256], F32),
-    "ones": ("sbuf", [128, 128], BF), "ip": ("sbuf", [128, 128], BF), "im": ("sbuf", [128, 128], BF),
-    "bt": ("sbuf", [128, 128], BF), "bm": ("sbuf", [128, 128], BF), "bf32": ("sbuf", [128, 128], F32), "bn": ("sbuf", [128, 128], BF),
-    "kc": ("sbuf", [128, 128], BF), "selk": ("sbuf", [128, 64, 2], BF), "csel": ("sbuf", [128, 8, 8, 8, 2], BF), "casel": ("sbuf", [128, 2, 64, 2], BF),
-    "thr": ("sbuf", [128, 128], F32), "qrow": ("sbuf", [128, 128], F32), "m16": ("sbuf", [128, 16], F32),
-    "rt0": ("sbuf", [128, 24], BF), "rt1": ("sbuf", [128, 24], BF), "rt2": ("sbuf", [128, 24], BF),
+    "pw0": ("sbuf", [128, 4096], BF), "pw1": ("sbuf", [128, 4096], BF), "sw0": ("sbuf", [128, 4096], I32), "sw1": ("sbuf", [128, 4096], I32),
+    "cq0": ("sbuf", [128, 896], I32), "cq1": ("sbuf", [128, 896], I32), "candl": ("sbuf", [128, 4, 28], I32), "tin": ("sbuf", [128, 4, 32], F32),
+    "ngi": ("sbuf", [128, 2, 16], I32), "ngf": ("sbuf", [128, 2, 16], F32), "nbu": ("sbuf", [128, 16], U16),
+    "gm": ("sbuf", [128, 2, 8, 16], F32), "geor": ("sbuf", [128, 2, 4, 2, 16], F32),
+    "ones": ("sbuf", [128, 128], BF), "zero": ("sbuf", [128, 128], BF), "ip": ("sbuf", [128, 128], BF), "im": ("sbuf", [128, 128], BF),
+    "ip16": ("sbuf", [128, 128], F16), "im16": ("sbuf", [128, 128], F16),
+    "bm": ("sbuf", [128, 128], BF), "bf32": ("sbuf", [128, 128], F32), "bn": ("sbuf", [128, 128], BF), "kc": ("sbuf", [128, 128], BF),
+    "selk": ("sbuf", [128, 128], F16), "casel": ("sbuf", [128, 2, 128], F16), "hrow": ("sbuf", [128, 128], BF), "csel": ("sbuf", [128, 16, 128], F16),
+    "lnb": ("sbuf", [128, 4, 128], F32), "m16": ("sbuf", [128, 16], F32),
+    "prow": ("sbuf", [128, 128], BF), "qrow": ("sbuf", [128, 128], BF), "grow": ("sbuf", [128, 128], BF), "krow": ("sbuf", [128, 128], BF), "lrow": ("sbuf", [128, 128], F32),
+    "tg": ("sbuf", [128, 16], BF), "rt": ("sbuf", [128, 3, 16], BF), "ru": ("sbuf", [128, 3, 16], BF), "kk": ("sbuf", [128, 2, 16], BF),
+    "arow": ("sbuf", [128, 16], BF), "brow": ("sbuf", [128, 64], BF), "thr": ("sbuf", [128, 128], F32),
     "rmin": ("sbuf", [128, 512], BF), "rmax": ("sbuf", [128, 512], BF),
-    "ci": ("sbuf", [128, 16], I32), "cf": ("sbuf", [128, 16], F32),
-    "posc": ("sbuf", [128, 4, 8], F32), "headc": ("sbuf", [128, 4, 8], F32), "sbase": ("sbuf", [128, 4, 8], F32), "sbf": ("sbuf", [128, 4, 8], F32),
-    "t1": ("sbuf", [128, 4, 8], F32), "t3": ("sbuf", [128, 4, 8], F32), "offc": ("sbuf", [128, 32], U16), "offs": ("sbuf", [128, 32], U16),
-    "crow": ("sbuf", [128, 4, 128], BF), "own": ("sbuf", [128, 512], F32), "ns": ("sbuf", [128, 4, 8, 16], F32), "cr": ("sbuf", [128, 8, 16], F32),
-    "nsx": ("sbuf", [128, 4, 16, 8], F32), "crx": ("sbuf", [128, 4, 16, 8], F32),
+    "ci": ("sbuf", [128, 16], I32), "cf": ("sbuf", [128, 24], F32),
+    "pos": ("sbuf", [128, 2, 16, 2], F32), "offc": ("sbuf", [128, 32], U16), "offs": ("sbuf", [128, 32], U16), "tl": ("sbuf", [128, 2, 2, 32], F32),
+    "crow": ("sbuf", [128, 2, 256], F16), "own": ("sbuf", [128, 2, 256], F16), "crx": ("sbuf", [128, 4, 128], F32),
     "cn": ("sbuf", [128, 256], F32), "idx": ("sbuf", [128, 16, 4, 16], I32), "off": ("sbuf", [128, 1024], U16),
-    "ygb": ("sbuf", [128, 64, 8], F32), "ycb": ("sbuf", [128, 64, 8], F32),
-    "d0": ("psum", [128, 512], F32), "d1": ("psum", [128, 512], F32), "d2": ("psum", [128, 512], F32), "d3": ("psum", [128, 512], F32),
-    "ca0": ("psum", [128, 2, 4, 64], F32), "ca1": ("psum", [128, 2, 4, 64], F32),
-    "jb": ("psum", [128, 4, 8, 16], F32), "mb": ("psum", [128, 4, 128], F32),
+    "flg": ("sbuf", [128, 4, 128], BF), "dm": ("sbuf", [128, 12, 128], BF),
+    "gh": ("sbuf", [128, 4, 128], F16), "back": ("sbuf", [128, 2, 64], F16), "ygb": ("sbuf", [128, 2, 256], F32), "ycb": ("sbuf", [128, 4, 128], F32),
+    "ca": ("psum", [128, 4, 2, 4, 16], F32), "gp0": ("psum", [128, 16, 4, 8], F32), "gp1": ("psum", [128, 16, 4, 8], F32), "mb": ("psum", [128, 16, 2, 16], F32),
 }
-for _c in range(NCH):
-    SCRATCH["e%d" % _c] = ("sbuf", [128, 4096], BF)
-    SCRATCH["sc%d" % _c] = ("sbuf", [128, 8, 512], BF)
-    SCRATCH["flg%d" % _c] = ("sbuf", [128, 128], BF)
-    SCRATCH["dm%d" % _c] = ("sbuf", [128, 128], BF)
-    SCRATCH["n%d" % _c] = ("sbuf", [128, 512], BF)
-    SCRATCH["f%d" % _c] = ("sbuf", [128, 512], BF)
-SEMAPHORES = ["sV", "sS", "sP", "sG", "loc"] + ["arr%d" % i for i in range(4)] + ["dma%d" % i for i in range(NDMA)] + ["add%d" % i for i in range(8)]
+for _k in range(ND):
+    SCRATCH["d%d" % _k] = ("psum", [128, 512], F32)
+for _n in range(4):
+    SCRATCH["e%d" % _n] = ("sbuf", [128, 4, 1024], BF)
+    SCRATCH["sc%d" % _n] = ("sbuf", [128, 4, 1024], BF)
+for _n in range(8):
+    SCRATCH["w%d" % _n] = ("sbuf", [128, 256], F32)
+SEMAPHORES = ["loc0", "sV", "sS", "sP", "sG", "loc"] + ["arr%d" % i for i in range(8)] + ["dma%d" % i for i in range(NDMA)] + ["add%d" % i for i in range(12)]
+
+
+def lane(t, b):
+    return (b, 2) if t % 2 else (4 * b, t + 1)
 
 
 def slot(t, al, b):
-    s = t + 1
-    if s in (2, 4):
-        return 2 * al + b
-    return (s * al + 4 * b) % 8
+    return (lane(t, b)[0] + al * lane(t, b)[1]) % 8
 
 
 def order(prog):
@@ -84,10 +81,28 @@ def order(prog):
         p = prog[i]
         path[i] = p["us"] + p["lat"] + (p["dma"] * DW + 1.8 if p["dma"] else 0.0) + max([path[q] + WAKE for q in succs[i]] or [0.0])
     rank = [path[i] - BIAS * prog[i]["c"] for i in range(n)]
+    best = None
+    for _ in range(PASSES):
+        total, seq, where, ends = place(prog, succs, list(left), dict(users), rank)
+        if best is None or total < best[0]:
+            best = (total, seq, where)
+        tail, after = [0.0] * n, {}
+        for i in reversed(seq):
+            p = prog[i]
+            own = p["us"] + p["lat"] + (p["dma"] * DW + 1.8 if p["dma"] else 0.0) + max([tail[q] + WAKE for q in succs[i]] or [0.0])
+            tail[i] = max(own, p["us"] * KEEP + after.get(p["e"], 0.0))
+            after[p["e"]] = tail[i]
+            rank[i] = MIX * rank[i] + (1 - MIX) * own
+    return best[1], best[2]
+
+
+def place(prog, succs, left, users, rank):
+    n = len(prog)
+    ends = [0.0] * n
     at = [0.0] * n
     ready = [i for i in range(n) if not left[i]]
     qfree, bank, engines = {}, {}, 0.0
-    free = {k: 0.0 for k in range(4)}
+    free = {k: 0.0 for k in range(ND)}
     where, seq = {}, []
     while ready:
         cand = []
@@ -112,8 +127,8 @@ def order(prog):
             del free[k]
         qfree[e] = t + p["us"]
         if p["dma"]:
-            engines = max(t + 1.2, engines) + p["dma"]
-            end = engines + .6
+            engines = max(t + 1.2 + (p["us"] if p["lat"] else 0.0), engines) + p["dma"]
+            end = engines + (p["lat"] or .5)
         else:
             end = t + p["us"] + p["lat"]
         for b in p["x"]:
@@ -124,13 +139,14 @@ def order(prog):
                 free[where[v]] = end
         ready.remove(i)
         seq.append(i)
+        ends[i] = end
         for q in succs[i]:
             left[q] -= 1
             at[q] = max(at[q], end + WAKE)
             if not left[q]:
                 ready.append(q)
     assert len(seq) == n
-    return seq, where
+    return max(ends), seq, where, ends
 
 
 def rank_program(g, core, T, topo):
@@ -138,7 +154,7 @@ def rank_program(g, core, T, topo):
     if rank is None:
         return
     A = AluOpType
-    COPY = ActivationFunctionType.Copy
+    ACT = ActivationFunctionType
     V, S, P = g.vector, g.scalar, g.tensor
     queue = {"V": V, "S": S, "P": P, "G": g, "Y": g.sync}
 
@@ -149,7 +165,7 @@ def rank_program(g, core, T, topo):
     def rec(e, emit, r, w, x, us, lat=0.0, load=0.0, use=(), alloc=None):
         prog.append({"e": e, "emit": emit, "r": list(r), "w": list(w), "x": list(x), "us": us, "lat": lat, "dma": load, "use": list(use), "alloc": alloc, "c": now[0]})
 
-    def op(e, calls, r=(), w=(), x=(), n=64, us=None, use=(), alloc=None, pre=None):
+    def op(e, calls, r=(), w=(), x=(), n=64, us=None, use=(), alloc=None, pre=None, ro=(), wo=()):
         calls = calls if isinstance(calls, list) else [calls]
 
         def emit():
@@ -162,18 +178,21 @@ def rank_program(g, core, T, topo):
                 call().then_inc(T.sem[sem], 1)
                 count[sem] += 1
             done(e, sem, count[sem], r, w, xs)
-        rec(e, emit, r, w, x, max(64, n) * CYC if us is None else us, 0.0, 0.0, use, alloc)
+        rec(e, emit, list(r) + list(ro), list(w) + list(wo), x, max(64, n) * CYC if us is None else us, 0.0, 0.0, use, alloc)
 
-    def dma(e, out, in_, r=(), w=(), load=0.5):
+    def dma(e, pairs, r=(), w=(), load=0.3, ro=(), wo=(), pre=None):
         def emit():
+            if pre:
+                pre()
             need(e, deps("dma", r, w, ()))
-            sem = "dma%d" % ndma[0]
-            ndma[0] += 1
-            queue[e].dma_start(out, in_).then_inc(T.sem[sem], 16)
-            done(e, sem, 16, r, w)
-        rec(e, emit, r, w, (), .1, 0.0, load)
+            sem = "dma%d" % len(ndma)
+            ndma.append(16 * len(pairs))
+            for out, in_ in pairs:
+                queue[e].dma_start(out, in_).then_inc(T.sem[sem], 16)
+            done(e, sem, ndma[-1], r, w)
+        rec(e, emit, list(r) + list(ro), list(w) + list(wo), (), .07 * len(pairs), 0.0, load)
 
-    nadd = [0] * 8
+    nadd = [0] * 12
 
     def dma_add(i, out, in_, r, w):
         def emit():
@@ -187,7 +206,7 @@ def rank_program(g, core, T, topo):
     know = {e: {} for e in queue}
     snaps = {}
     wr, rd, bank = {}, {}, {}
-    ndma = [0]
+    ndma = []
 
     def need(e, tokens):
         todo = {}
@@ -225,12 +244,11 @@ def rank_program(g, core, T, topo):
         for k in x:
             bank.setdefault(k, {})[sem] = tok
 
-    W = [T.w0, T.w1, T.w2, T.w3]
-    D = [T.d0, T.d1, T.d2, T.d3]
-    E = [T["e%d" % c] for c in range(NCH)]
-    SC = [T["sc%d" % c] for c in range(NCH)]
-    RT = [T.rt0, T.rt1, T.rt2]
-    CA = [T.ca0, T.ca1]
+    W = [T["w%d" % i] for i in range(8)]
+    D = [T["d%d" % i] for i in range(ND)]
+    E = [T["e%d" % n] for n in range(4)]
+    SC = [T["sc%d" % n] for n in range(4)]
+    PW, SW, CQ, GP = [T.pw0, T.pw1], [T.sw0, T.sw1], [T.cq0, T.cq1], [T.gp0, T.gp1]
     others = [c for c in T.cores if c != core]
 
     def ts(out, in0, s1, op0, s2=None, op1=None):
@@ -241,7 +259,9 @@ def rank_program(g, core, T, topo):
     def tt(out, a, b, o):
         return lambda: V.tensor_tensor(out, a, b, o)
 
-    def cp(out, a):
+    def cp(out, a, e="V"):
+        if e == "S":
+            return lambda: S.activation(out, a, ACT.Copy)
         return lambda: V.tensor_copy(out, a)
 
     def ms(out, v):
@@ -251,12 +271,24 @@ def rank_program(g, core, T, topo):
         return lambda: P.matmul(out, l, rhs, st, sp)
 
     def gat(n):
-        return .05 + GCYC * CYC * n
+        return .06 + GCYC * CYC * n
 
-    dma("Y", T.candl[:], T.cand[:], w=["candl"])
-    dma("Y", T.pw[:, 0:SPLIT], T.pe[:, 0:SPLIT], w=["pwa", "yq"], load=1.0)
-    dma("S", T.geoi[:], T.geo[:], w=["geoi"])
-    dma("S", T.nbi[:], T.nb[:], w=["nbi"])
+    def pe(*ns):
+        return sum(max(64, n) for n in ns) * PEC
+
+    def table(win, src, ph, ks):
+        return [(win[32 * k + 16 * h:32 * k + 16 * h + 16, :], src[64 * ph + 16 * k:64 * ph + 16 * k + 16, :]) for k in ks for h in range(2)]
+
+    def queues(ph):
+        op("V", ms(CQ[ph][:], 4096), w=["cq%d" % ph], n=896)
+        dma("S", [(CQ[ph][0:128:16, 448 * c:448 * c + 448], T.cand[4 * ph:4 * ph + 4, 896 * c:896 * c + 896]) for c in range(2)], w=["cq%d" % ph], wo=["qS"], load=.1)
+
+    for ph in range(2):
+        dma("Y", [(T.candl[:, 2 * ph + c, :], T.cand[4 * ph:4 * ph + 4, 896 * c:896 * c + 896]) for c in range(2)], w=["candl%d" % ph], wo=["qY"])
+    dma("S", [(T.ngi[:, 0, :], T.nb[:]), (T.ngi[:, 1, :], T.geo[:])], w=["ngi"], wo=["qS"])
+    queues(0)
+    dma("Y", table(T.pw0, T.pe, 0, range(4)), w=["pw0"], wo=["qY"], load=TAB)
+    queues(1)
 
     ci, cf = T.ci, T.cf
 
@@ -267,393 +299,363 @@ def rank_program(g, core, T, topo):
         return cf[:, k:k + 1]
 
     FREE = {"allow_small_or_imprecise_dtypes": True}
+
+    def iota(name, out, pattern, base=0, cm=0):
+        n = 1
+        for _, m in pattern:
+            n *= m
+        op("G", lambda: g.iota(out, pattern, base, cm, **FREE), w=[name], us=.13 + 2 * n * CYC)
+
     op("G", lambda: g.iota(icol(0), [[0, 1]], 0, 1), w=["ci0"], us=.13)
-    op("G", lambda: g.iota(T.posc[:], [[448, 4], [1, 8]], 0, 0, **FREE), w=["posc0", "posc3"], us=.2)
+    iota("lrow", T.lrow[:], [[16, 4], [128, 2], [1, 16]])
+    iota("qrow", T.qrow[:], [[0, 8], [1, 16]])
+    iota("grow", T.grow[:], [[1, 8], [0, 16]])
+    iota("pos", T.pos[:], [[0, 4], [1, 8], [448, 2]])
+    iota("arow", T.arow[:], [[0, 2], [1, 8]])
+    iota("hrow", T.hrow[:], [[2, 8], [1, 2], [0, 8]])
+    iota("prow", T.prow[:], [[1, 128]])
+    iota("krow", T.krow[:], [[8, 4], [0, 4], [1, 8]])
+    iota("brow", T.brow[:], [[32, 4], [1, 16]])
     op("V", ms(T.ones[:], 1.0), w=["ones"])
-    op("V", ms(T.cq[:], 0.0), w=["cq"], n=896)
-    op("G", lambda: g.affine_select(T.bt[:], T.ones[:], [[-16, 8], [0, 16]], A.is_ge, 0.0, 0, 1), r=["ones"], w=["bt"], us=.43)
-    op("G", lambda: g.affine_select(T.bm[:], T.bt[:], [[16, 8], [0, 16]], A.is_ge, 0.0, 15, -1), r=["bt"], w=["bm"], us=.43)
-    op("G", lambda: g.iota(T.qrow[:], [[0, 8], [1, 16]], 0, 0, **FREE), w=["qrow"], us=.4)
-    op("G", lambda: g.affine_select(T.ip[:], T.ones[:], [[-1, 128]], A.is_equal, 0.0, 0, 1), r=["ones"], w=["ip"], us=.43)
-    op("G", lambda: g.iota(T.headc[:], [[448, 4], [0, 8]], 8, 0, **FREE), w=["headc0", "headc3"], us=.2)
-    op("G", lambda: g.iota(T.sbase[:], [[-7164, 4], [0, 8]], 0, 0, **FREE), w=["sbase"], us=.2)
-    op("V", ts(icol(1), icol(0), 15, A.bitwise_and), r=["ci0"], w=["ci1"])
-    op("V", cp(fcol(1), icol(1)), r=["ci1"], w=["cf1"])
-    op("V", ts(fcol(2), fcol(1), 28.0, A.mult), r=["cf1"], w=["cf2"])
-    op("V", ts(fcol(3), fcol(1), 1.5, A.is_lt), r=["cf1"], w=["cf3"])
-    op("V", ts(T.posc[:], T.posc[:], fcol(2), A.add), r=["posc0", "posc3", "cf2"], w=["posc0", "posc3"])
-    op("V", ts(T.clo[:], T.candl[:], 63, A.bitwise_and), r=["candl"], w=["clo"], n=112)
-    op("V", tt(T.chib[:], T.candl[:], T.clo[:], A.subtract), r=["clo", "candl"], w=["chib"], n=224)
-    op("V", cp(T.clob[:], T.clo[:]), r=["clo"], w=["clob"], n=112)
-    dma("Y", T.cq[0:128:16, :], T.chib[:], r=["chib", "cq", "yq"], w=["cqh", "cqw"])
-    dma("Y", T.cq[1:128:16, :], T.clob[:], r=["clob", "cq", "yq"], w=["cql", "cqv"])
-    dma("Y", T.pw[:, SPLIT:4096], T.pe[:, SPLIT:4096], w=["pw", "cqw"], load=2.4)
-    dma("Y", T.sw[:], T.se[:], w=["sw", "cqw"], load=6.5)
-    op("V", ms(T.csel[:], 0.0), w=["csel"], n=512)
-    op("V", ms(T.casel[:], 0.0), w=["casel"], n=128)
-    op("V", ts(T.selk[:], T.bm[:], fcol(3), A.mult), r=["bm", "cf3"], w=["selk"])
-    op("V", ts(T.m16[:], T.qrow[:, 0:16], fcol(1), A.is_equal), r=["qrow", "cf1"], w=["m16"])
-    op("V", cp(T.geof[:], T.geoi[:]), r=["geoi"], w=["geof"])
-    op("V", cp(T.bf32[:], T.bm[:]), r=["bm"], w=["bf32"], n=128)
-    for u in range(8):
-        op("V", cp(T.csel[:, u, :, u, :], T.selk[:, u:64:8, :]), r=["selk", "csel"], w=["cselu%d" % u])
+    op("V", ms(T.zero[:], 0.0), w=["zero"])
+
+    def bits(k, shift, mask):
+        op("V", ts(icol(k), icol(0), shift, A.arith_shift_right, mask, A.bitwise_and), r=["ci0"], w=["ci%d" % k])
+        op("V", cp(fcol(k), icol(k)), r=["ci%d" % k], w=["cf%d" % k])
+
+    op("V", cp(fcol(0), icol(0)), r=["ci0"], w=["cf0"])
+    bits(1, 0, 15)
+    bits(2, 4, 7)
+    bits(3, 5, 3)
+    bits(4, 0, 31)
+    bits(5, 1, 15)
+    bits(6, 0, 1)
+    op("V", ts(T.bm[:], T.grow[:], fcol(2), A.is_equal), r=["grow", "cf2"], w=["bm"], n=128)
+    op("V", ts(T.bf32[:], T.grow[:], fcol(2), A.is_equal), r=["grow", "cf2"], w=["bf32"], n=128)
+    op("V", ts(fcol(7), fcol(1), 1.5, A.is_lt), r=["cf1"], w=["cf7"])
+    op("V", ts(T.selk[:], T.bm[:], fcol(7), A.mult), r=["bm", "cf7"], w=["selk"], n=128)
+    op("V", ts(fcol(9), fcol(1), 1.5, A.is_gt, 64.0, A.mult), r=["cf1"], w=["cf9"])
+    op("V", ts(fcol(9), fcol(2), 2.0, A.mult, fcol(9), A.add), r=["cf2"], w=["cf9"])
     for b in range(2):
-        op("V", cp(T.casel[:, b, :, b], T.selk[:, :, b]), r=["selk", "casel"], w=["caselb%d" % b])
-    GM = ["gm%d%d" % (c, j) for c in range(NCH) for j in range(4)]
-    for c in range(NCH):
-        for j in range(4):
-            lo = 64 * c + 16 * j
-            op("V", ts(T.gm[:, lo:lo + 16], T.m16[:], T.geof[:, 4 * j + c:4 * j + c + 1], A.mult), r=["m16", "geof"], w=["gm%d%d" % (c, j)])
-    op("P", mm(T.jb[:, 2:4, :, :], T.bf32[:], T.gm[:], True, True), r=["bf32"] + GM, w=["jbg"], x=["jb"], us=.8)
-    for c in range(NCH):
-        for al in range(4):
-            o, i = T.geor[:, 4 * c + al, :, :], T.jb[:, 2 + c // 2, 4 * (c % 2):4 * (c % 2) + 4, :]
-            op("S", lambda o=o, i=i: S.activation(o, i, COPY, bias=-65536.0, scale=16.0), r=["jbg"], w=["geor%d" % (4 * c + al)], x=["jb"])
+        op("V", ts(T.casel[:, b, :], T.hrow[:], -1.0 * b, A.add, fcol(9), A.is_equal), r=["hrow", "cf9"], w=["caselb%d" % b], n=128)
+    op("V", ts(fcol(8), fcol(1), 28.0, A.mult), r=["cf1"], w=["cf8"])
+    op("V", ts(T.m16[:], T.qrow[:, 0:16], fcol(1), A.is_equal), r=["qrow", "cf1"], w=["m16"])
+    for i in range(4):
+        op("V", ts(T.lnb[:, i, :], T.lrow[:], 64.0 * (i // 2) - 128.0 * (i % 2), A.add, fcol(0), A.is_equal), r=["lrow", "cf0"], w=["lnb%d" % i], n=128)
 
-    def crow_of(a, t, c0=0, c1=NCH):
-        return T.crow[:, c0:c1, 16 * a:16 * a + 16] if t else T.cq[:, a:1792:28]
+    nsig = [0] * 8
 
-    def crow_keys(t, c0=0, c1=NCH):
-        return ["crow%d" % c for c in range(c0, c1)] if t else ["cq", "cqh", "cql"]
-
-    nsig = [0] * 4
-
-    def send_codes(t, c0, c1):
-        op("P", [mm(T.jb[:, 1, c0:c1, :], T.csel[:, u, :, :, :], crow_of(u, t, c0, c1), u == 0, u == 7) for u in range(8)],
-           r=crow_keys(t, c0, c1) + ["cselu%d" % u for u in range(8)], w=["jbc"], x=["jb"], us=.35)
-        mine = W[t][:, 64 * rank + 16 * c0:64 * rank + 16 * c1]
-        key = "wown%d%d" % (t, c0)
-        op("V", cp(mine, T.jb[:, 1, c0:c1, :]), r=["jbc"], w=[key], x=["jb"])
+    def send(t, ph):
+        i = 2 * t + ph
+        mine = W[i][:, 64 * rank:64 * rank + 64]
 
         def emit():
-            need("G", deps("G", [key], [], []))
+            need("G", deps("G", ["wown%d" % i], [], []))
             m = topo.mask(core, others[0])
             ids = []
             for o in others:
                 m &= topo.mask(core, o)
                 a = topo.addr(o)
                 ids.append(DstId(rid=a[0], pnc=a[1]))
-            tr = RemoteDMATransfer(dst_ids=ids, dma_engine_mask=m, remote_sem=T.sem["arr%d" % t], srcs=[mine], dsts=[mine for _ in ids])
-            g.remote_dma_fused([tr], local_sem=T.sem.loc)
-            nsig[t] += bin(m).count("1")
-        rec("G", emit, [key], ["sent%d%d" % (t, c0)], [], .6, 3.0 if t else 5.0)
+            tr = RemoteDMATransfer(dst_ids=ids, dma_engine_mask=m, remote_sem=T.sem["arr%d" % i], srcs=[mine], dsts=[mine for _ in ids])
+            g.remote_dma_fused([tr], local_sem=T.sem["loc" if t else "loc0"])
+            nsig[i] += bin(m).count("1")
+        rec("G", emit, ["wown%d" % i], ["sent%d" % i], [], .6 if i else 3.0, FLIGHT - SEND - 1.2, SEND)
 
-    def own_codes(t):
-        for al in range(4):
-            calls = [mm(CA[al // 2][:, al % 2, j, :], T.casel[:, b, :, :], crow_of(slot(t, al, b), t), b == 0, b == 1) for j in range(4) for b in range(2)]
-            op("P", calls, r=crow_keys(t) + ["caselb0", "caselb1"], w=["ca%d" % al] + ["pr%d" % (4 * c + al) for c in range(NCH)], x=["cab%d" % (al // 2)], us=.35)
+    for ph in range(2):
+        cand, tin = T.candl[:, 2 * ph:2 * ph + 2, :], T.tin[:, 2 * ph:2 * ph + 2, :]
+        op("V", [cp(T.tin[:, 2 * ph:2 * ph + 2, 8 * i:8 * i + 8], T.candl[:, 2 * ph:2 * ph + 2, 0:8]) for i in range(4)], r=["candl%d" % ph], w=["tin%d" % ph], n=256)
+        op("V", lambda ph=ph, tin=tin: V.transpose(W[ph][:, 64 * rank:64 * rank + 64], tin), r=["tin%d" % ph], w=["wown%d" % ph])
+        send(0, ph)
+        op("V", [cp(T.offs[:, 16 * ph + 8 * b:16 * ph + 8 * b + 8], T.candl[:, 2 * ph:2 * ph + 2, 4 * b:4 * b + 4]) for b in range(2)], r=["candl%d" % ph], w=["offs%d" % ph], n=128)
 
-    def self_gaps(t):
-        op("V", ts(T.sbf[:], T.posc[:], 16.0, A.mult), r=["posc0", "posc3"], w=["sbf"])
-        op("V", tt(T.sbf[:], T.sbf[:], T.sbase[:], A.add), r=["sbf", "sbase"], w=["sbf"])
-        for c in range(NCH):
-            op("V", cp(T.offs[:, c:32:4], T.sbf[:, c, :]), r=["sbf"], w=["offs%d" % c])
-        op("S", lambda: S.activation(T.own[:], T.sq[:].indirect(T.offs[:]), COPY), r=["sq"] + ["offs%d" % c for c in range(NCH)], w=["own"], us=gat(512))
-        for k in range(8):
-            a = slot(t, k // 2, k % 2)
-            b = (a + 1 + t) % 8
-            if t < 3:
-                op("V", tt(T.ns[:, :, k, :], T.own[:, 64 * b:64 * b + 64], T.own[:, 64 * a:64 * a + 64], A.subtract), r=["own"], w=["ns%d" % k], n=128)
-            else:
-                op("V", tt(T.nsx[:, 0:3, :, k], T.own[:, 64 * b:64 * b + 48], T.own[:, 64 * a:64 * a + 48], A.subtract), r=["own"], w=["nsx%d" % k], n=96)
-                op("V", tt(T.ns[:, 3, k, :], T.own[:, 64 * b + 48:64 * b + 64], T.own[:, 64 * a + 48:64 * a + 64], A.subtract), r=["own"], w=["ns%d" % k])
+    op("V", cp(T.ngf[:], T.ngi[:]), r=["ngi"], w=["ngf"])
+    for ph in range(2):
+        op("P", [mm(T.mb[:, 8:10, ph, 0:8], T.lnb[:, 2 * ph + h, :], T.ngf[:, :, h:16:2], h == 0, h == 1) for h in range(2)],
+           r=["ngf", "lnb%d" % (2 * ph), "lnb%d" % (2 * ph + 1)], w=["mbn%d" % ph], x=["mb"], us=pe(256, 256))
+        op("V", [cp(T.nbu[:, 8 * ph + 4 * c:8 * ph + 4 * c + 4], T.mb[:, 8, ph, c:8:2]) for c in range(2)], r=["mbn%d" % ph], w=["nbu%d" % ph], x=["mb"], n=128)
+        for i in range(8):
+            op("V", ts(T.gm[:, ph, i, :], T.m16[:], T.mb[:, 9, ph, i:i + 1], A.mult), r=["m16", "mbn%d" % ph], w=["gm%d%d" % (ph, i)], x=["mb"])
+        op("P", mm(GP[ph][:, 12:16, :, :], T.bf32[:], T.gm[:, ph, :, :], True, True), r=["bf32"] + ["gm%d%d" % (ph, i) for i in range(8)], w=["gpg%d" % ph],
+           wo=["grp%d" % ph], x=["gp%d" % ph], us=pe(512))
+        op("S", lambda ph=ph: S.activation(T.geor[:, ph, :, :, :], GP[ph][:, 12:16, :, :], ACT.Copy, bias=-65536.0, scale=16.0), r=["gpg%d" % ph], w=["geor%d" % ph], x=["gp%d" % ph], n=128)
 
-    NS = ["ns%d" % k for k in range(8)]
-    NX = ["nsx%d" % k for k in range(8)]
-    MB = ["mbp%d" % c for c in range(NCH)]
+    def sends(t, ph):
+        key = "pos%d" % ph
+        lo = 16 * ph
+        lanes = [slice(a, a + 3 * s + 1, s) for a, s in (lane(t, 0), lane(t, 1))]
+        op("V", [ts(T.offc[:, lo + 8 * b:lo + 8 * b + 8], T.pos[:, ph, lanes[b], :], fcol(8), A.add) for b in range(2)], r=["pos", key, "cf8"], w=["offc%d" % ph], n=128)
+        op("V", ts(T.crow[:, ph, :], CQ[ph][:].indirect(T.offc[:, lo:lo + 16]), -2048.0, A.add), r=["cq%d" % ph, "offc%d" % ph], w=["crow%d" % ph], us=gat(256))
+        if t:
+            i = 2 * t + ph
+            op("P", [mm(T.mb[:, 2:4, h, :], T.csel[:, 8 * h + slot(t, k % 4, k // 4), :], T.crow[:, ph, 32 * k:32 * k + 32], k == 0, k == 7) for h in range(2) for k in range(8)],
+               r=["crow%d" % ph] + ["csel%d" % k for k in range(16)], w=["mbc"], x=["mb"], us=pe(*[32] * 16))
+            mine = W[i][:, 64 * rank:64 * rank + 64]
+            op(ON["mine"], cp(mine, T.mb[:, 2:4, :, :], ON["mine"]), r=["mbc"], w=["wown%d" % i], x=["mb"])
+            send(t, ph)
+            op("V", lambda: V.transpose(T.tl[:, ph, :, :], mine), r=["wown%d" % i], w=["tl%d" % ph])
+            op("V", [cp(T.offs[:, lo + 8 * b:lo + 8 * b + 8], T.tl[:, ph, :, lanes[b]]) for b in range(2)], r=["tl%d" % ph], w=["offs%d" % ph], n=128)
 
-    def code_rows():
-        op("P", [mm(T.mb[:], T.selk[:], T.crow[:], True, True)], r=crow_keys(3) + ["selk"], w=MB, x=["mb"], us=.3)
-        for a in range(8):
-            op("V", cp(T.crx[:, 0:3, :, a], T.mb[:, 0:3, 16 * a:16 * a + 16]), r=MB, w=["crx%d" % a], x=["mb"])
-            op("V", cp(T.cr[:, a, :], T.mb[:, 3, 16 * a:16 * a + 16]), r=MB, w=["cr%d" % a], x=["mb"])
+    def codes(t, ph):
+        lo = 16 * ph
+        calls = [mm(T.ca[:, :, :, j, :], T.casel[:, b, :], T.crow[:, ph, 128 * b:128 * b + 128], b == 0, b == 1) for j in range(4) for b in range(2)]
+        op("P", calls, r=["crow%d" % ph, "caselb0", "caselb1"], w=["ca%d%d" % (c, al) for c in range(2) for al in range(4)], x=["ca"], us=pe(*[128] * 8))
 
-    waited = {}
+    def selves(t, ph):
+        op("V", cp(T.own[:, ph, :], SW[ph][:].indirect(T.offs[:, 16 * ph:16 * ph + 16])), r=["sw%d" % q for q in range(4 * ph, 4 * ph + 4)] + ["offs%d" % ph], w=["own%d" % ph], us=gat(256))
 
-    def neighbours(t, c0, c1):
-        def pre():
-            if t not in waited:
-                waited[t] = 1
-                V.wait_ge(T.sem["arr%d" % t], 3 * nsig[t])
-        op("V", cp(T.cn[:, 64 * c0:64 * c1], W[t][:].indirect(T.nbu[:, 4 * c0:4 * c1])), r=["nbu", "wown%d0" % t, "wown%d3" % t, "sent%d0" % t, "sent%d3" % t],
-           w=["cn%d" % c for c in range(c0, c1)], us=gat(64 * (c1 - c0)), pre=pre)
+    def neighbours(t, ph):
+        i, e = 2 * t + ph, ON["cn"]
+        op(e, cp(T.cn[:, 128 * ph:128 * ph + 128], W[i][:].indirect(T.nbu[:, 8 * ph:8 * ph + 8]), e), r=["nbu%d" % ph, "wown%d" % i, "sent%d" % i],
+           w=["cn%d" % ph], us=gat(128), pre=lambda: queue[e].wait_ge(T.sem["arr%d" % i], 3 * nsig[i]))
 
-    def index(c, groups):
+    def index(n, groups):
+        ph, c = n // 2, n % 2
         for als in groups:
-            ks = [4 * c + al for al in als]
+            ks = [4 * n + al for al in als]
             for al in als:
-                ca = CA[al // 2][:, al % 2, :, 16 * c:16 * c + 16]
-                op("V", tt(ca, T.cn[:, 64 * c:64 * c + 64], ca, A.mult), r=["cn%d" % c, "ca%d" % al], w=["pr%d" % (4 * c + al)], x=["cab%d" % (al // 2)])
+                ca = T.ca[:, al, c, :, :]
+                op("V", tt(ca, T.cn[:, 64 * n:64 * n + 64], ca, A.mult), r=["cn%d" % ph], w=["ca%d%d" % (c, al)], x=["ca"])
             for al in als:
-                k = 4 * c + al
-                ca = CA[al // 2][:, al % 2, :, 16 * c:16 * c + 16]
-                op("V", tt(T.idx[:, k, :, :], ca, T.geor[:, k, :, :], A.add), r=["pr%d" % k, "geor%d" % k], w=["ix%d" % k], x=["cab%d" % (al // 2)])
+                op("V", tt(T.idx[:, 4 * n + al, :, :], T.ca[:, al, c, :, :], T.geor[:, ph, :, c, :], A.add), r=["ca%d%d" % (c, al), "geor%d" % ph], w=["ix%d" % (4 * n + al)], x=["ca"])
             IX = ["ix%d" % k for k in ks]
             v = T.idx[:, ks[0]:ks[-1] + 1, :, :]
             op("V", ts(v, v, 4, A.arith_shift_right, 4095, A.bitwise_and), r=IX, w=IX, n=64 * len(ks))
             op("V", cp(T.off[:, 64 * ks[0]:64 * ks[-1] + 64], v), r=IX, w=["of%d" % k for k in ks], n=64 * len(ks))
 
-    def gather(c, al, hs, sign=1.0, e="S"):
-        k = 4 * c + al
-        lo, n = 64 * k + 32 * hs[0], 32 * len(hs)
-        out, src = E[c][:, 16 * lo - 4096 * c:16 * (lo + n) - 4096 * c], T.pw[:].indirect(T.off[:, lo:lo + n])
-        if e == "V":
+    def ekeys(n, al, hs=(0, 1)):
+        return ["e%d%d%d" % (n, al, h) for h in hs]
+
+    def part(n, al, hs):
+        return E[n][:, al, 512 * hs[0]:512 * hs[-1] + 512]
+
+    def gather(n, al, hs, sign=1.0, e="S", minus=None):
+        k, ph = 4 * n + al, n // 2
+        out, src = part(n, al, hs), PW[ph][:].indirect(T.off[:, 64 * k + 32 * hs[0]:64 * k + 32 * hs[-1] + 32])
+        r = ["pw%d" % ph, "of%d" % k]
+        if minus is not None:
+            e, call, r = "V", tt(out, src, part(n, minus, hs), A.subtract), r + ekeys(n, minus, hs)
+        elif e == "V":
             call = cp(out, src) if sign == 1.0 else ts(out, src, sign, A.mult)
         else:
-            call = lambda: S.activation(out, src, COPY, scale=sign)
-        op(e, call, r=["pw", "pwa", "of%d" % k], w=["e%d%d%d" % (c, al, h) for h in hs], us=gat(16 * n))
+            call = lambda: S.activation(out, src, ACT.Copy, scale=sign)
+        op(e, call, r=r, w=ekeys(n, al, hs), wo=["turn" + e] if e in CHAIN else [], us=gat(512 * len(hs)))
 
-    def added(c, i, into, what):
-        p, q = 1024 * into, 1024 * what
-        dma_add(2 * c + i, E[c][:, p:p + 1024], E[c][:, q:q + 1024], ["e%d%d%d" % (c, what, h) for h in range(2)], ["e%d%d%d" % (c, into, h) for h in range(2)])
+    def added(n, i, into, what):
+        dma_add(3 * n + i, part(n, into, (0, 1)), part(n, what, (0, 1)), ekeys(n, what), ekeys(n, into))
+        return [(part(n, into, [h]), "e%d%d%d" % (n, into, h), None) for h in range(2)]
 
-    def held(c, al, h):
-        return (E[c], "e%d%d%d" % (c, al, h), 0, 1024 * al + 512 * h)
+    nv = [0]
 
-    nv, nn, nf = [0], [0], [0]
-
-    def bank_diff(terms, r):
+    def bank_diff(n, h, terms, early=0):
         v = nv[0]
         nv[0] += 1
+        for lo, hi in ((0, early), (early, len(terms))):
+            calls = []
+            for i in range(lo, hi):
+                al, fl, sg = terms[i]
+                for q in (range(16) if fl else [None]):
+                    rhs = part(n, al, [h]) if q is None else E[n][:, al, 512 * h + (q + 8) % 16:512 * h + 512:16]
+                    calls.append(lambda i=i, q=q, sg=sg, rhs=rhs: P.matmul(D[where[v]][:] if q is None else D[where[v]][:, q:512:16], (T.ip if sg > 0 else T.im)[:], rhs,
+                                                                          i == 0, i == len(terms) - 1 and q in (None, 15)))
+            if calls:
+                op("P", calls, r=["e%d%d%d" % (n, al, h) for al, _, _ in terms[lo:hi]] + ["ip", "im"], w=["vd%d" % v] if hi == len(terms) else [], wo=["vo%d" % v],
+                   us=pe(*[1024 if fl else 512 for _, fl, _ in terms[lo:hi]]), alloc=None if lo else v, use=[v] if lo else [])
+        return (None, "vd%d" % v, v)
 
-        def call(j, b, i):
-            buf, col, fl, sg = terms[i]
-            lo = col + 256 * j
-            rhs = buf[:, lo + (1 - b if fl else b):lo + 256:2]
-            o = 256 * j + 128 * b
-            return lambda: P.matmul(D[where[v]][:, o:o + 128], (T.ip if sg > 0 else T.im)[:], rhs, i == 0, i == len(terms) - 1)
-        calls = [call(j, b, i) for j in range(2) for b in range(2) for i in range(len(terms))]
-        op("P", calls, r=list(r) + ["ip", "im"], w=["vd%d" % v], us=.085 * len(calls), alloc=v)
-        return (v, "vd%d" % v, 1, 0)
-
-    def narrowed(src):
-        i = nn[0] % NND
-        nn[0] += 1
-        out, v = T["n%d" % i], src[0]
-        op("S", lambda: S.activation(out[:], D[where[v]][:], COPY), r=[src[1]], w=["n%d" % i], use=[v], n=512)
-        return (out, "n%d" % i, 2, 0)
-
-    def fused(c, h, al, other):
-        i = nf[0] % NNF
-        nf[0] += 1
-        out, key = T["f%d" % i], "f%d" % i
-        k = 4 * c + al
-        lo = 64 * k + 32 * h
-        p = 1024 * other + 512 * h
-        op("V", tt(out[:], T.pw[:].indirect(T.off[:, lo:lo + 32]), E[c][:, p:p + 512], A.subtract), r=["pw", "pwa", "of%d" % k, "e%d%d%d" % (c, other, h)], w=[key], us=gat(512))
-        return (out, key, 0, 0)
-
-    def scan(c, al, h, src, low):
+    def scan(n, al, h, src, low):
         rp = T.rmin if low else T.rmax
         o0, o1 = (A.max, A.min) if low else (A.min, A.max)
-        k = 4 * h + al
-        if src[2] == 1:
-            calls = [lambda: V.tensor_tensor_scan(SC[c][:, k, :], rp[:], D[where[src[0]]][:], 0.0, o0, o1)]
-        elif src[2] == 2:
-            calls = [lambda: V.tensor_tensor_scan(SC[c][:, k, :], rp[:], src[0][:], 0.0, o0, o1)]
-        else:
-            calls = [lambda j=j, b=b: V.tensor_tensor_scan(SC[c][:, k, 256 * j + 128 * b:256 * j + 128 * b + 128], rp[:, 0:128],
-                                                           src[0][:, src[3] + 256 * j + b:src[3] + 256 * j + 256:2], 0.0, o0, o1) for j in range(2) for b in range(2)]
-        op("V", calls, r=[src[1], "rmin" if low else "rmax"], w=["sc%d%d%d" % (c, al, h)], use=[src[0]] if src[2] == 1 else [], us=(512 if src[2] == 1 else 256) * CYC)
+        buf, key, v = src
+        op("V", lambda: V.tensor_tensor_scan(SC[n][:, al, 512 * h:512 * h + 512], rp[:], buf if v is None else D[where[v]][:], 0.0, o0, o1),
+           r=[key, "rmin" if low else "rmax"], w=["sc%d%d%d" % (n, al, h)], use=[] if v is None else [v], n=256 if v is None else 512)
 
-    def jsum(c, sets):
-        calls = []
-        for k0, k1, low in sets:
-            for j in range(4):
-                h, lo = 4 * (j // 2), 256 * (j % 2)
-                calls.append(mm(T.jb[:, 0, 2 * k0:2 * k1, :], (T.ip if low else T.im)[:], SC[c][:, h + k0:h + k1, lo + 7:lo + 256:8], j == 0, j == 3))
-        op("P", calls, r=["ip", "im"] + ["sc%d%d%d" % (c, al, h) for al in range(4) for h in range(2)], w=["jbs"], x=["jb"], us=.045 * len(calls))
-
-    def chunk(t, c):
-        flip = (t != 1)
-        onv, nar = VG[t][c], NAR[t][c]
-        vg = [h for h in range(2) if (1, h) in onv]
-        a = MODE[t][c] == "A"
-        first = [FIRSTH[t], 1 - FIRSTH[t]]
-        halves = [[h] for h in first] if c in LASTHALF[t] else [[0, 1]]
-
-        def gathers(al, hs, sign=1.0, skip=()):
-            for e in "VS":
-                h2 = [h for h in hs if ((al, h) in onv) == (e == "V") and h not in skip]
-                if h2:
-                    gather(c, al, h2, sign, e)
-
-        def diff(k, h, p, q, sp, sq, fl=False):
-            d = bank_diff([(E[c], 1024 * p + 512 * h, False, sp), (E[c], 1024 * q + 512 * h, fl, sq)], ["e%d%d%d" % (c, p, h), "e%d%d%d" % (c, q, h)])
-            return narrowed(d) if (k, h) in nar else d
-
-        if t < 3 and a:
-            for al, sign in ((2, -1.0), (1, 1.0), (0, -1.0), (3, 1.0)):
-                for hs in halves:
-                    gathers(al, hs, sign)
-            m12 = [diff(1, h, 1, 2, 1, 1) for h in range(2)]
-            added(c, 0, 1, 0)
-            m30 = [diff(3, h, 3, 0, 1, 1, flip) for h in range(2)]
-            added(c, 1, 2, 3)
-            for al, src, low in ((1, m12, True), (3, m30, True), (0, [held(c, 1, h) for h in range(2)], False), (2, [held(c, 2, h) for h in range(2)], False)):
-                for h in range(2):
-                    scan(c, al, h, src[h], low)
-            return [(0, 1, False), (1, 2, True), (2, 3, False), (3, 4, True)]
-        if t < 3:
-            for hs in halves:
-                for al in range(4):
-                    gathers(al, hs, 1.0, vg if al == 1 else ())
-            for h in first:
-                if h in vg:
-                    f = fused(c, h, 1, 0)
-                    d = bank_diff([(f[0], 0, False, 1), (E[c], 512 * h, False, 1), (E[c], 2048 + 512 * h, False, -1)], [f[1], "e%d0%d" % (c, h), "e%d2%d" % (c, h)])
-                    d = narrowed(d) if (1, h) in nar else d
-                else:
-                    f = diff(0, h, 1, 0, 1, -1)
-                    d = None
-                scan(c, 0, h, f, False)
-                scan(c, 1, h, d or diff(1, h, 1, 2, 1, -1), True)
-                scan(c, 2, h, diff(2, h, 2, 3, 1, -1), True)
-                scan(c, 3, h, diff(3, h, 3, 0, 1, -1, flip), True)
-            return [(0, 1, False), (1, 4, True)]
-        gathers(3, [0, 1], 1.0 if vg else -1.0)
-        gathers(1, [0, 1], 1.0, vg)
-        if not vg:
-            added(c, 1, 1, 3)
-        gathers(2, [0, 1], -1.0)
-        gathers(0, [0, 1])
-        added(c, 0, 0, 2)
-        for h in range(2):
-            s = fused(c, h, 1, 3) if h in vg else (diff(1, h, 1, 3, 1, -1) if vg else held(c, 1, h))
-            scan(c, 1, h, s, True)
-            scan(c, 3, h, s, False)
-        for h in range(2):
-            scan(c, 0, h, held(c, 0, h), True)
-            scan(c, 2, h, held(c, 0, h), False)
-        return [(0, 2, True), (2, 4, False)]
-
-    def outputs(c, sets):
-        calls = []
-        for k0, k1, low in sets:
-            for k in range(2 * k0, 2 * k1):
-                for j in range(4):
-                    lo = 256 * (j % 2) + 128 * (k % 2)
-                    calls.append(mm(T.mb[:, 0, k:128:8], (T.ip if low else T.im)[:], SC[c][:, 4 * (j // 2) + k // 2, lo + 7:lo + 128:8], j == 0, j == 3))
-        op("P", calls, r=["ip", "im"] + ["sc%d%d%d" % (c, al, h) for al in range(4) for h in range(2)], w=["mbp0"], x=["mb"], us=.045 * len(calls))
-        flg = T["flg%d" % c]
-        op("V", tt(flg[:], T.mb[:, 0, :], T.nsx[:, c, :, :], A.is_gt), r=["mbp0"] + NX, w=["flg%d" % c], x=["mb"], n=128)
-        op("P", [mm(T.mb[:, 1, :], T.kc[:], T.ones[:], True, False), mm(T.mb[:, 1, :], T.bn[:], flg[:], False, True)],
-           r=["flg%d" % c, "bn", "kc", "ones"], w=["mbp1"], x=["mb"], us=.15)
-        op("V", tt(T.ygb[:, 16 * c:16 * c + 16, :], T.mb[:, 0, :], T.nsx[:, c, :, :], A.subtract), r=["mbp0"] + NX, w=["yg%d" % c], x=["mb"], n=128)
-        op("V", tt(T.ycb[:, 16 * c:16 * c + 16, :], T.mb[:, 1, :], T.crx[:, c, :, :], A.min), r=["mbp1"] + ["crx%d" % k for k in range(8)], w=["yc%d" % c], x=["mb"], n=128)
-
-    def post(t, c, sets):
-        if t == 3 and c < 3:
-            outputs(c, sets)
+    def unit(t, n, al):
+        fused = MODE[t][n][al % 2] == "F" if t == 3 else MODE[t][n][2] == "F"
+        if fused and al in ((0, 1) if t == 3 else (3,)):
+            for h in range(2):
+                gather(n, al, [h], minus=al + 2 if t == 3 else 2)
             return
-        jsum(c, sets)
-        flg, dm = T["flg%d" % c], T["dm%d" % c]
-        op("V", tt(flg[:], T.jb[:, 0, :, :], T.ns[:, c, :, :], A.is_gt), r=["jbs"] + NS, w=["flg%d" % c], x=["jb"], n=128)
+        sign = (-1.0 if al > 1 and not fused else 1.0) if t == 3 else (-1.0 if al % 2 else 1.0)
+        for e in "VS":
+            hs = [h for h in range(2) if ((al, h) in VG[t][n]) == (e == "V")]
+            for some in ([[h] for h in hs] if (n % 2, al) in HALVES[t == 3] else [hs] if hs else []):
+                gather(n, al, some, sign, e)
+
+    def chunk(t, n):
+        mode = MODE[t][n]
+
+        def held(al):
+            return [(part(n, al, [h]), "e%d%d%d" % (n, al, h), None) for h in range(2)]
+
         if t == 3:
-            for k in range(8):
-                op("V", tt(T.ygb[:, 16 * c:16 * c + 16, k], T.jb[:, 0, k, :], T.ns[:, c, k, :], A.subtract), r=["jbs"] + NS, w=["yg%d%d" % (c, k)], x=["jb"])
-            op("P", [mm(T.mb[:, 0, :], T.kc[:], T.ones[:], True, False), mm(T.mb[:, 0, :], T.bn[:], flg[:], False, True)],
-               r=["flg%d" % c, "bn", "kc", "ones"], w=["mbp0"], x=["mb"], us=.15)
-            for k in range(8):
-                op("V", tt(T.ycb[:, 16 * c:16 * c + 16, k], T.mb[:, 0, 16 * k:16 * k + 16], T.cr[:, k, :], A.min), r=["mbp0", "cr%d" % k], w=["yc%d%d" % (c, k)], x=["mb"])
+            low = [True, True, False, False]
+            for p, m in enumerate(mode):
+                if m == "F":
+                    src = held(p)
+                else:
+                    src = added(n, p, p, p + 2) if m == "A" else [bank_diff(n, h, [(p, False, 1), (p + 2, False, 1)]) for h in range(2)]
+                for h in range(2):
+                    scan(n, p, h, src[h], True)
+                    scan(n, p + 2, h, src[h], False)
+            return low
+        flip = t != 1
+        low = [True, mode[1] == "P" and mode[2] != "F", mode[2] != "F", mode != "AAA"]
+        src, s1, s3 = {}, -1 if low[1] else 1, 1 if low[3] else -1
+        src[3] = [bank_diff(n, h, [(3, False, s3), (2, False, s3), (0, flip, -s3)] if mode[2] == "F" else [(3, False, -s3), (0, flip, -s3)],
+                            EARLY[n % 2] * (2 if mode[2] == "F" else 1)) for h in range(2)]
+        if mode[0] == "P":
+            src[0] = [bank_diff(n, h, [(0, False, 1), (1, False, 1)]) for h in range(2)]
+        if mode[1] == "P":
+            src[1] = [bank_diff(n, h, [(1, False, s1), (2, False, s1)]) for h in range(2)]
+        if mode[2] == "P":
+            src[2] = [bank_diff(n, h, [(2, False, 1), (3, False, 1)]) for h in range(2)]
+        if mode[2] == "F":
+            src[2] = held(3)
+        if mode[2] == "A":
+            src[2] = added(n, 2, 3, 2)
+        if mode[0] == "A":
+            src[0] = added(n, 0, 0, 1)
+        if mode[1] == "A":
+            src[1] = added(n, 1, 2, 1)
+        for al in (2, 3, 0, 1):
+            for h in range(2):
+                scan(n, al, h, src[al][h], low[al])
+        return low
+
+    def post(t, n, low):
+        ph, c = n // 2, n % 2
+        gp, bk, grp = GP[c], "gp%d" % c, "grp%d" % c
+        gap, cnt, flg = gp[:, 0:4, :, :], gp[:, 4:8, :, :], T.flg[:, n, :]
+        if t == 3:
+            op("P", [mm(gp[:, 8:12, :, slot(t, k % 4, k // 4)], T.selk[:], T.crow[:, ph, 32 * k + 16 * c:32 * k + 16 * c + 16], True, True) for k in range(8)],
+               r=["crow%d" % ph, "selk"], w=["rows%d" % c], wo=[grp], x=[bk], us=pe(*[64] * 8))
+            op(ON["rows"], cp(T.crx[:, n, :], gp[:, 8:12, :, :], ON["rows"]), r=["rows%d" % c], w=["crx%d" % n], x=[bk], n=128)
+        calls = [mm(gap, T.zero[:], T.ones[:], True, False)]
+
+        def own(b, a0, a1):
+            return T.own[:, ph, 128 * b + 64 * c + 16 * a0:128 * b + 64 * c + 16 * a1]
+        for b in range(2):
+            if t == 3:
+                for al in range(4):
+                    calls += [mm(gp[:, 0:4, :, 2 * al + b], sign[:], own(b, a, a + 1), False, False) for sign, a in ((T.ip16, al), (T.im16, (al + 2) % 4))]
+            else:
+                calls += [mm(gp[:, 0:4, :, b:8:2], T.ip16[:], own(b, 0, 4), False, False), mm(gp[:, 0:3, :, b:8:2], T.im16[:], own(b, 1, 4), False, False),
+                          mm(gp[:, 3, :, b:8:2], T.im16[:], own(b if t == 1 else 1 - b, 0, 1), False, False)]
+        op("P", calls, r=["own%d" % ph, "zero", "ones", "ip16", "im16"], w=["gap%d%d" % (c, al) for al in range(4)], wo=[grp], x=[bk], us=pe(128, *[64] * (len(calls) - 1)))
+        if t == 3:
+            sets = [[al] for al in range(4)]
+        elif low == [True, False, True, False]:
+            sets = [[0, 2], [1, 3]]
+        else:
+            sets = [[0, 3]] + ([[1, 2]] if low[1] == low[2] else [[1], [2]])
+        left = [4 * len(sets)]
+
+        def last():
+            left[0] -= 1
+            return left[0] == 0
+        for als in sets:
+            pick = slice(als[0], als[-1] + 1, max(1, als[-1] - als[0]))
+            out = gp[:, 0:4, :, 2 * als[0]:2 * als[0] + 2] if t == 3 else gp[:, pick, :, :]
+            calls = [lambda out=out, pick=pick, j=j: P.matmul(out, (T.ip if low[pick.start] else T.im)[:], SC[n][:, pick, 256 * j + 7:256 * j + 256:8], False, last()) for j in range(4)]
+            op("P", calls, r=["ip", "im"] + ["sc%d%d%d" % (n, al, h) for al in als for h in range(2)], ro=[grp] + ["gap%d%d" % (c, al) for al in als],
+               w=["sum%d%d" % (c, al) for al in als], x=[bk], us=pe(64, 64, 64, 64))
+        GK = ["gap%d%d" % (c, al) for al in range(4)] + ["sum%d%d" % (c, al) for al in range(4)]
+        if t == 3:
+            op("V", cp(T.gh[:, n, :], gap), r=GK, w=["gh%d" % n], x=[bk], n=128)
+            op("P", [mm(T.mb[64 * c:64 * c + 64, 8 + 4 * h:12 + 4 * h, :, :], T.back[:, h, :], T.gh[:, n, :], True, True) for h in range(2)],
+               r=["gh%d" % n, "back"], w=["mby%d" % c], x=["mb"], us=pe(128, 128))
+            op("V", ts(flg, T.gh[:, n, :], 0.0, A.is_gt), r=["gh%d" % n], w=["flg%d" % n])
+            op("P", [mm(cnt, T.kc[:], T.ones[:], True, False), mm(cnt, T.bn[:], flg, False, True)], r=["flg%d" % n, "bn", "kc", "ones"], w=["cnt%d" % c], wo=[grp], x=[bk], us=pe(128, 128))
+            op("V", tt(T.ycb[:, n, :], cnt, T.crx[:, n, :], A.min), r=["cnt%d" % c, "crx%d" % n], w=["yc%d" % n], x=[bk], n=128)
+            dma("Y", [(T.yc[4 * ph:4 * ph + 4, 256 * c:256 * c + 256], T.ycb[0:128:16, n, :])], r=["yc%d" % n])
+            if c:
+                op(ON["yg"], cp(T.ygb[:, ph, :], T.mb[:, 8:16, :, :], ON["yg"]), r=["mby0", "mby1"], w=["yg%d" % ph], x=["mb"], n=256)
+                for e, k in (("Y", 0), ("S" if ph else "Y", 1)):
+                    dma(e, [(T.yg[64 * ph:64 * ph + 64, 256 * k:256 * k + 256], T.ygb[64 * k:64 * k + 64, ph, :])], r=["yg%d" % ph])
             return
-        op("P", mm(T.jb[:, 2, :, :], flg[:], T.bm[:], True, True), r=["flg%d" % c, "bm"], w=["jbg"], x=["jb"], us=.08)
-        op("V", tt(dm[:], T.jb[:, 2, :, :], T.thr[:], A.is_ge), r=["jbg", "thr"], w=["dm%d" % c], x=["jb"], n=128)
-        op("P", mm(T.mb[:, c, 0:24], dm[:], RT[t][:], True, True), r=["dm%d" % c, "rt%d" % t], w=["mbp%d" % c], x=["mb"], us=.06)
+        if ON["flag"] == "S":
+            call = lambda: S.activation(flg, gap, ACT.Sign, bias=-0.5)
+        else:
+            call = ts(flg, gap, 0.0, A.is_gt)
+        op(ON["flag"], call, r=GK, w=["flg%d" % n], x=[bk], n=128)
+        op("P", mm(cnt, flg, T.bm[:], True, True), r=["flg%d" % n, "bm"], w=["cnt%d" % c], wo=[grp], x=[bk], us=pe(128))
+        dm = T.dm[:, 4 * t + n, :]
+        op("V", tt(dm, cnt, T.thr[:], A.is_ge), r=["cnt%d" % c, "thr"], w=["dm%d%d" % (t, n)], x=[bk], n=128)
+        out = T.mb[:, 0, :, c:16:2]
+        calls = [mm(out, T.ip[:], T.kk[:, c, :], True, False)] + [mm(out, T.dm[:, 4 * s + n, :], T.ones[:, 0:16], False, False) for s in range(t)]
+        calls.append(mm(out, dm, T.rt[:, t, :], False, True))
+        op("P", calls, r=["dm%d%d" % (s, n) for s in range(t + 1)] + ["rt%d" % t, "kk", "ip", "ones"], w=["mbp%d" % c], x=["mb"], us=pe(*[64] * len(calls)))
+        if c == 1:
+            op("V", tt(T.pos[:, ph, :, :], T.mb[:, 0, :, :], T.pos[:, ph, :, :], A.max), r=["mbp0", "mbp1", "pos"], w=["pos%d" % ph], x=["mb"])
 
-    def places(c0, c1):
-        p, h, k = T.posc[:, c0:c1, :], T.headc[:, c0:c1, :], c0
-        P3 = MB[c0:c1]
-        op("V", tt(T.t1[:, c0:c1, :], T.mb[:, c0:c1, 0:8], p, A.add), r=P3 + ["posc%d" % k], w=["t1%d" % k], x=["mb"])
-        op("V", tt(T.t3[:, c0:c1, :], T.mb[:, c0:c1, 8:16], h, A.add), r=P3 + ["headc%d" % k], w=["t3%d" % k], x=["mb"])
-        op("V", tt(p, T.t1[:, c0:c1, :], T.t3[:, c0:c1, :], A.min), r=["t1%d" % k, "t3%d" % k], w=["posc%d" % k])
-        op("V", cp(T.offc[:, 8 * c0:8 * c1], p), r=["posc%d" % k], w=["offc%d" % k])
-        for c in range(c0, c1):
-            op("V", cp(T.crow[:, c, :], T.cq[:].indirect(T.offc[:, 8 * c:8 * c + 8])), r=["cq", "cqh", "cql", "offc%d" % k], w=["crow%d" % c], us=gat(128))
-        op("V", tt(h, T.mb[:, c0:c1, 16:24], h, A.add), r=P3 + ["headc%d" % k], w=["headc%d" % k], x=["mb"])
-
-    send_codes(0, 0, NCH)
-    own_codes(0)
-
-    for j in range(4):
-        op("V", cp(T.nbu[:, j:16:4], T.nbi[:, 4 * j:4 * j + 4]), r=["nbi"], w=["nbu"])
-    op("V", ts(icol(3), icol(0), 5, A.arith_shift_right), r=["ci0"], w=["ci3"])
-    op("V", ts(icol(4), icol(0), 4, A.arith_shift_right, 1, A.bitwise_and), r=["ci0"], w=["ci4"])
-    op("V", ts(icol(5), icol(1), 3, A.bitwise_and), r=["ci1"], w=["ci5"])
-    op("V", ts(icol(6), icol(1), 2, A.arith_shift_right), r=["ci1"], w=["ci6"])
-    op("V", cp(fcol(0), icol(0)), r=["ci0"], w=["cf0"])
-    for k in (3, 4, 5, 6):
-        op("V", cp(fcol(k + 2), icol(k)), r=["ci%d" % k], w=["cf%d" % (k + 2)])
+    for name, v in (("ip", 1.0), ("im", -1.0), ("ip16", 1.0), ("im16", -1.0)):
+        op("V", ts(T[name][:], T.prow[:], fcol(0), A.is_equal, v, A.mult), r=["prow", "cf0"], w=[name], n=128)
     op("V", ms(T.rmin[:], -BIG), w=["rmin"], n=256)
     op("V", ms(T.rmax[:], BIG), w=["rmax"], n=256)
-    op("V", ts(T.im[:], T.ip[:], -1.0, A.mult), r=["ip"], w=["im"])
-    op("V", ts(fcol(9), fcol(6), 4.0, A.mult), r=["cf6"], w=["cf9"])
-    op("V", ts(fcol(11), fcol(5), 2.0, A.mult), r=["cf5"], w=["cf11"])
-    op("V", ts(fcol(12), fcol(5), 3.0, A.mult), r=["cf5"], w=["cf12"])
     op("V", ms(T.rmin[:, 0:512:8], BIG), w=["rmin"])
     op("V", ms(T.rmax[:, 0:512:8], -BIG), w=["rmax"])
-    op("V", ts(T.headc[:], T.headc[:], fcol(2), A.add), r=["headc0", "headc3", "cf2"], w=["headc0", "headc3"])
-    op("V", tt(fcol(10), fcol(9), fcol(5), A.add), r=["cf9", "cf5"], w=["cf10"])
-    op("V", tt(fcol(11), fcol(11), fcol(6), A.add), r=["cf11", "cf6"], w=["cf11"])
-    op("V", tt(icol(7), fcol(12), fcol(9), A.add), r=["cf12", "cf9"], w=["ci7"])
-    op("V", ts(icol(8), icol(7), 7, A.bitwise_and), r=["ci7"], w=["ci8"])
-    op("V", cp(fcol(12), icol(8)), r=["ci8"], w=["cf12"])
-    for t in range(3):
-        a = fcol(10 + t)
-        k = "cf%d" % (10 + t)
-        op("V", ts(RT[t][:, 0:8], T.qrow[:, 0:8], a, A.is_equal, 4096.0, A.mult), r=["qrow", k], w=["rta%d" % t])
-        op("V", ts(RT[t][:, 8:16], T.qrow[:, 0:8], a, A.is_gt), r=["qrow", k], w=["rtb%d" % t])
-        op("V", ms(RT[t][:, 16:24], 1.0), r=["rta%d" % t, "rtb%d" % t], w=["rt%d" % t])
-    op("V", ts(T.thr[:], T.qrow[:], fcol(1), A.not_equal, 1000.0, A.mult), r=["qrow", "cf1"], w=["thr"], n=128)
-    op("V", ts(fcol(13), fcol(7), 448.0, A.mult), r=["cf7"], w=["cf13"])
-    op("V", ts(fcol(14), fcol(1), -448.0, A.mult), r=["cf1"], w=["cf14"])
-    op("V", ts(T.thr[:], T.thr[:], 15.5, A.max), r=["thr"], w=["thr"], n=128)
-    op("V", tt(fcol(13), fcol(13), fcol(8), A.add), r=["cf13", "cf8"], w=["cf13"])
-    op("V", cp(T.cand16[:], T.candl[:]), r=["candl"], w=["cand16"], n=112)
-    op("V", tt(fcol(13), fcol(13), fcol(14), A.add), r=["cf13", "cf14"], w=["cf13"])
-    op("V", ts(T.sbase[:], T.sbase[:], fcol(13), A.add), r=["sbase", "cf13"], w=["sbase"])
-    op("V", cp(T.sq[:], T.sw[:].indirect(T.cand16[:])), r=["sw", "cand16"], w=["sq"], us=gat(1792))
-    self_gaps(0)
+    op("V", ts(T.thr[:], T.qrow[:], fcol(5), A.not_equal, 64.0, A.mult), r=["qrow", "cf5"], w=["thr"], n=128)
+    op("V", ts(T.thr[:], T.thr[:], 15.5, A.max), w=["thr"], n=128)
+    op("V", ms(T.kk[:, 0, :], -56.0), w=["kk"])
+    op("V", ms(T.kk[:, 1, :], 392.0), w=["kk"])
+    for t, (m, k) in enumerate(((1.0, 4.0), (2.0, 1.0), (3.0, 4.0))):
+        a, key = fcol(10 + t), "cf%d" % (10 + t)
+        op("V", ts(fcol(13 + t), fcol(6), k, A.mult), r=["cf6"], w=["cf%d" % (13 + t)])
+        op("V", ts(icol(10 + t) if t == 2 else a, fcol(3), m, A.mult, fcol(13 + t), A.add), r=["cf3", "cf%d" % (13 + t)], w=[key])
+        if t == 2:
+            op("V", ts(icol(12), icol(12), 7, A.bitwise_and), r=[key], w=[key])
+            op("V", cp(a, icol(12)), r=[key], w=[key])
+        op("V", ts(T.rt[:, t, :], T.arow[:], a, A.is_equal, 64.0, A.mult), r=["arow", key], w=["rt%d" % t])
+        op("V", ts(T.ru[:, t, :], T.arow[:], a, A.is_gt), r=["arow", key], w=["ru%d" % t])
+        op("V", tt(T.rt[:, t, :], T.rt[:, t, :], T.ru[:, t, :], A.add), r=["ru%d" % t], w=["rt%d" % t])
+    for h in range(2):
+        op("V", ts(fcol(16 + h), fcol(4), 16.0 * h - .5, A.is_gt, -64.0, A.mult), r=["cf4"], w=["cf%d" % (16 + h)])
+        op("V", ts(fcol(18 + h), fcol(4), 16.0 * h + 1.5, A.is_gt, 64.0, A.mult), r=["cf4"], w=["cf%d" % (18 + h)])
+        op("V", ts(fcol(20 + h), fcol(3), 8.0, A.mult, fcol(16 + h), A.add), r=["cf3", "cf%d" % (16 + h)], w=["cf%d" % (20 + h)])
+        op("V", ts(fcol(20 + h), fcol(20 + h), 64.0, A.add, fcol(18 + h), A.add), r=["cf%d" % (18 + h)], w=["cf%d" % (20 + h)])
+        op("V", ts(T.tg[:, 8 * h:8 * h + 8], T.qrow[:, 0:8], fcol(20 + h), A.add), r=["qrow", "cf%d" % (20 + h)], w=["tg%d" % h])
+        for u in range(8):
+            k = 8 * h + u
+            op("V", ts(T.csel[:, k, :], T.krow[:], T.tg[:, k:k + 1], A.is_equal), r=["krow", "tg%d" % h], w=["csel%d" % k])
+    op("V", [ts(T.back[:, h, :], T.brow[:], 16.0 * h, A.add, fcol(0), A.is_equal) for h in range(2)], r=["brow", "cf0"], w=["back"], n=128)
+    op("V", ts(T.bn[:], T.bm[:], -4096.0, A.mult), r=["bm"], w=["bn"])
+    op("V", ts(fcol(22), fcol(0), 0.0, A.is_equal, 65536.0, A.mult), r=["cf0"], w=["cf22"])
+    op("V", ts(fcol(23), fcol(0), 1.0, A.is_equal), r=["cf0"], w=["cf23"])
+    op("V", ts(T.kc[:], T.ones[:], fcol(22), A.mult, fcol(23), A.subtract), r=["ones", "cf22", "cf23"], w=["kc"], n=128)
 
     for t in range(4):
-        neighbours(t, 0, 1)
-        index(0, [[2], [1], [0], [3]])
-        neighbours(t, 1, NCH)
-        for c in range(1, NCH):
-            index(c, [[0, 1, 2, 3]])
-        for c in range(NCH):
-            now[0] = c
-            sets = chunk(t, c)
-            if t == 3 and c == 3:
-                dma("Y", T.yg[:, 0:384], T.ygb[:, 0:48, :], r=["yg%d" % i for i in range(3)])
-                dma("Y", T.yc[:, 0:384], T.ycb[0:128:16, 0:48, :], r=["yc%d" % i for i in range(3)])
-            post(t, c, sets)
-            if t < 3 and c == 2:
-                places(0, 3)
-                send_codes(t + 1, 0, 3)
-        now[0] = 0
-        if t < 3:
-            places(3, 4)
-            send_codes(t + 1, 3, 4)
-            own_codes(t + 1)
-            self_gaps(t + 1)
-        if t == 2:
-            code_rows()
-            op("V", ts(T.bn[:], T.bm[:], -4096.0, A.mult), r=["bm"], w=["bn"])
-            op("V", ts(fcol(14), fcol(0), 0.0, A.is_equal, 65536.0, A.mult), r=["cf0"], w=["cf14"])
-            op("V", ts(fcol(15), fcol(0), 1.0, A.is_equal), r=["cf0"], w=["cf15"])
-            op("V", tt(fcol(14), fcol(14), fcol(15), A.subtract), r=["cf14", "cf15"], w=["cf14"])
-            op("V", ts(T.kc[:], T.ones[:], fcol(14), A.mult), r=["ones", "cf14"], w=["kc"])
-    dma("Y", T.yg[:, 384:512], T.ygb[:, 48:64, :], r=["yg3%d" % k for k in range(8)])
-    dma("S", T.yc[:, 384:512], T.ycb[0:128:16, 48:64, :], r=["yc3%d" % k for k in range(8)])
+        if t == 0:
+            sends(0, 0)
+            sends(0, 1)
+            dma("Y", table(T.pw1, T.pe, 1, range(4)), w=["pw1"], ro=["sent0", "sent1"], wo=["qY"], load=TAB, pre=lambda: g.sync.wait_ge(T.sem.loc0, nsig[0] + nsig[1]))
+        for ph in range(2):
+            now[0] = 2 * ph
+            if t:
+                sends(t, ph)
+            codes(t, ph)
+            neighbours(t, ph)
+            for c, als in LISTS[t == 3]:
+                index(2 * ph + c, [als])
+            for i, (c, al) in enumerate(UNITS[t == 3]):
+                unit(t, 2 * ph + c, al)
+                for q in range(8):
+                    if t == 0 and PACE[q] == 8 * ph + i:
+                        dma("Y", table(SW[q // 4], T.se, q // 4, [q % 4]), r=ekeys(2 * ph + c, al, [0]) if 8 * ph + i else [], w=["sw%d" % q], wo=["qY"], load=TAB / 2)
+            selves(t, ph)
+            for n in (2 * ph, 2 * ph + 1):
+                now[0] = n
+                post(t, n, chunk(t, n))
 
-    seq, banks = order(prog)
+    if not ORDER:
+        ORDER.append(order(prog))
+    seq, banks = ORDER[0]
     where.update(banks)
     for i in seq:
         prog[i]["emit"]()
-    g.wait_ge(T.sem.loc, sum(nsig))
+    g.wait_ge(T.sem.loc, sum(nsig[2:]))
     for e in ("sV", "sS", "sP", "sG"):
         if know["Y"].get(e, 0) < count[e]:
             g.sync.wait_ge(T.sem[e], count[e])
-    for i in range(ndma[0]):
-        g.sync.wait_ge(T.sem["dma%d" % i], 16)
+    for i, v in enumerate(ndma):
+        g.sync.wait_ge(T.sem["dma%d" % i], v)

@@ -3,7 +3,7 @@ from concourse.mybir import AluOpType, ActivationFunctionType
 
 BF, F16, F32, I32, U16 = "bfloat16", "float16", "float32", "int32", "uint16"
 BIG = 1024.0
-MODE = [["PPF", "PAF", "AAF", "PAF"], ["AAP", "PAF", "AAP", "PAF"], ["AAP", "PAF", "AAP", "PAF"], ["AF", "AA", "AF", "AF"]]
+MODE = [["PPF", "PPF", "PAF", "AAF"], ["AAP", "PAF", "AAP", "PAF"], ["AAP", "PAF", "AAP", "PAF"], ["AF", "AA", "AF", "PF"]]
 VG = [[[], [], [], []], [[], [], [], []], [[], [], [], []], [[], [], [], []]]
 UNITS = [[(0, 2), (0, 0), (0, 3), (0, 1), (1, 2), (1, 1), (1, 3), (1, 0)], [(0, 2), (0, 0), (0, 3), (0, 1), (1, 2), (1, 0), (1, 3), (1, 1)]]
 LISTS = [[(0, [2]), (0, [0]), (0, [3]), (0, [1]), (1, [0, 1, 2, 3])], [(0, [2]), (0, [0]), (0, [3]), (0, [1]), (1, [0, 1, 2, 3])]]
@@ -12,10 +12,11 @@ EARLY = [0, 1]
 CHAIN = "S"
 PACE = [0, 0, 0, 1, 4, 7, 8, 9]
 ON = {"flag": "V", "dead": "V", "cn": "V", "mine": "V", "yg": "S", "rows": "S"}
-CYC, PEC, WAKE, EPS, GCYC, BIAS, ADDUS, DW, FLIGHT = 0.85e-3, 0.72e-3, 0.06, 0.2, 1.56, 0.0, 1.7, 1.0, 4.4
-TAB, SEND = 3.1, 1.2
+CYC, PEC, WAKE, EPS, GCYC, ADDUS, DW, FLIGHT = 1.0e-3, 0.75e-3, 0.07, 0.3, 1.6, 2.0, 1.0, 4.6
+TAB, SEND, ISSUE = 3.75, 1.5, 0.1
 PASSES, KEEP, MIX = 12, 1.0, 0.8
-ORDER = []
+ORDER, LOG = [], []
+START, LAND, IDLE = 1.4, 0.5, 8.0
 ND, NDMA = 4, 30
 SCRATCH = {
     "pw0": ("sbuf", [128, 4096], BF), "pw1": ("sbuf", [128, 4096], BF), "sw0": ("sbuf", [128, 4096], I32), "sw1": ("sbuf", [128, 4096], I32),
@@ -29,7 +30,7 @@ SCRATCH = {
     "lnb": ("sbuf", [128, 4, 128], F32), "m16": ("sbuf", [128, 16], F32),
     "prow": ("sbuf", [128, 128], BF), "qrow": ("sbuf", [128, 128], BF), "grow": ("sbuf", [128, 128], BF), "krow": ("sbuf", [128, 128], BF), "lrow": ("sbuf", [128, 128], F32),
     "tg": ("sbuf", [128, 16], BF), "rt": ("sbuf", [128, 3, 16], BF), "ru": ("sbuf", [128, 3, 16], BF), "kk": ("sbuf", [128, 2, 16], BF),
-    "arow": ("sbuf", [128, 16], BF), "brow": ("sbuf", [128, 64], BF), "thr": ("sbuf", [128, 128], F32),
+    "arow": ("sbuf", [128, 16], BF), "brow": ("sbuf", [128, 64], BF), "thr": ("sbuf", [128, 128], BF),
     "rmin": ("sbuf", [128, 512], BF), "rmax": ("sbuf", [128, 512], BF),
     "ci": ("sbuf", [128, 16], I32), "cf": ("sbuf", [128, 24], F32),
     "pos": ("sbuf", [128, 2, 16, 2], F32), "offc": ("sbuf", [128, 32], U16), "offs": ("sbuf", [128, 32], U16), "tl": ("sbuf", [128, 2, 2, 32], F32),
@@ -62,25 +63,32 @@ def order(prog):
     wr, rd, users = {}, {}, {}
     succs, left = [[] for _ in range(n)], []
     for i, p in enumerate(prog):
-        s = set(wr[k] for k in p["r"] + p["w"] if k in wr)
+        s = {}
+        for k in p["r"] + p["w"]:
+            if k in wr:
+                s[wr[k]] = s.get(wr[k], False) or k not in p["soft"]
         for k in p["w"]:
-            s.update(rd.get(k, ()))
-        s.discard(i)
+            for q in rd.get(k, ()):
+                s[q] = s.get(q, False) or (k not in p["soft"] and (prog[q]["e"] != p["e"] or prog[q]["dma"] > 0))
+        s.pop(i, None)
         for k in p["r"]:
             rd.setdefault(k, []).append(i)
         for k in p["w"]:
             wr[k] = i
             rd[k] = []
         left.append(len(s))
-        for q in s:
-            succs[q].append(i)
+        for q, hard in s.items():
+            succs[q].append((i, hard))
         for v in p["use"]:
             users[v] = users.get(v, 0) + 1
-    path = [0.0] * n
-    for i in range(n - 1, -1, -1):
+
+    def way(i, tail):
         p = prog[i]
-        path[i] = p["us"] + p["lat"] + (p["dma"] * DW + 1.8 if p["dma"] else 0.0) + max([path[q] + WAKE for q in succs[i]] or [0.0])
-    rank = [path[i] - BIAS * prog[i]["c"] for i in range(n)]
+        wait = p["lat"] + (p["dma"] * DW + START + LAND if p["dma"] else 0.0) + WAKE
+        return p["us"] + max([tail[q] + (wait if hard else 0.0) for q, hard in succs[i]] + [wait])
+    rank = [0.0] * n
+    for i in range(n - 1, -1, -1):
+        rank[i] = way(i, rank)
     best = None
     for _ in range(PASSES):
         total, seq, where, ends = place(prog, succs, list(left), dict(users), rank)
@@ -89,10 +97,13 @@ def order(prog):
         tail, after = [0.0] * n, {}
         for i in reversed(seq):
             p = prog[i]
-            own = p["us"] + p["lat"] + (p["dma"] * DW + 1.8 if p["dma"] else 0.0) + max([tail[q] + WAKE for q in succs[i]] or [0.0])
-            tail[i] = max(own, p["us"] * KEEP + after.get(p["e"], 0.0))
+            own = way(i, tail)
+            tail[i] = max(own, p["us"] * KEEP + after.get(p["e"], 0.0), p["dma"] + after.get("dma", 0.0) if p["dma"] else 0.0)
             after[p["e"]] = tail[i]
+            if p["dma"]:
+                after["dma"] = tail[i]
             rank[i] = MIX * rank[i] + (1 - MIX) * own
+    LOG.append(best[0])
     return best[1], best[2]
 
 
@@ -117,9 +128,9 @@ def place(prog, succs, left, users, rank):
                 if b in bank and bank[b][0] != p["e"]:
                     t = max(t, bank[b][1] + WAKE)
             cand.append((t, i))
-        best, i = min(cand)
+        best, i = min((t + prog[i]["us"], i) for t, i in cand)
         e = prog[i]["e"]
-        t, i = max([c for c in cand if prog[c[1]]["e"] == e and c[0] <= best + EPS], key=lambda c: (rank[c[1]], -c[1]))
+        t, i = max([c for c in cand if prog[c[1]]["e"] == e and c[0] <= best + EPS], key=lambda c: (rank[c[1]] - IDLE * c[0], -c[1]))
         p = prog[i]
         if p["alloc"] is not None:
             k = min(free, key=lambda b: free[b])
@@ -127,8 +138,8 @@ def place(prog, succs, left, users, rank):
             del free[k]
         qfree[e] = t + p["us"]
         if p["dma"]:
-            engines = max(t + 1.2 + (p["us"] if p["lat"] else 0.0), engines) + p["dma"]
-            end = engines + (p["lat"] or .5)
+            engines = max(t + START + (p["us"] if p["lat"] else 0.0), engines) + p["dma"]
+            end = engines + (p["lat"] or LAND)
         else:
             end = t + p["us"] + p["lat"]
         for b in p["x"]:
@@ -140,9 +151,9 @@ def place(prog, succs, left, users, rank):
         ready.remove(i)
         seq.append(i)
         ends[i] = end
-        for q in succs[i]:
+        for q, hard in succs[i]:
             left[q] -= 1
-            at[q] = max(at[q], end + WAKE)
+            at[q] = max(at[q], end + WAKE if hard else qfree[e])
             if not left[q]:
                 ready.append(q)
     assert len(seq) == n
@@ -162,8 +173,8 @@ def rank_program(g, core, T, topo):
     now = [0]
     where = {}
 
-    def rec(e, emit, r, w, x, us, lat=0.0, load=0.0, use=(), alloc=None):
-        prog.append({"e": e, "emit": emit, "r": list(r), "w": list(w), "x": list(x), "us": us, "lat": lat, "dma": load, "use": list(use), "alloc": alloc, "c": now[0]})
+    def rec(e, emit, r, w, x, us, lat=0.0, load=0.0, use=(), alloc=None, soft=()):
+        prog.append({"e": e, "emit": emit, "r": list(r), "w": list(w), "x": list(x), "us": us, "lat": lat, "dma": load, "use": list(use), "alloc": alloc, "soft": list(soft)})
 
     def op(e, calls, r=(), w=(), x=(), n=64, us=None, use=(), alloc=None, pre=None, ro=(), wo=()):
         calls = calls if isinstance(calls, list) else [calls]
@@ -178,7 +189,7 @@ def rank_program(g, core, T, topo):
                 call().then_inc(T.sem[sem], 1)
                 count[sem] += 1
             done(e, sem, count[sem], r, w, xs)
-        rec(e, emit, list(r) + list(ro), list(w) + list(wo), x, max(64, n) * CYC if us is None else us, 0.0, 0.0, use, alloc)
+        rec(e, emit, list(r) + list(ro), list(w) + list(wo), x, max(64, n) * CYC if us is None else us, 0.0, 0.0, use, alloc, list(ro) + list(wo))
 
     def dma(e, pairs, r=(), w=(), load=0.3, ro=(), wo=(), pre=None):
         def emit():
@@ -190,7 +201,7 @@ def rank_program(g, core, T, topo):
             for out, in_ in pairs:
                 queue[e].dma_start(out, in_).then_inc(T.sem[sem], 16)
             done(e, sem, ndma[-1], r, w)
-        rec(e, emit, list(r) + list(ro), list(w) + list(wo), (), .07 * len(pairs), 0.0, load)
+        rec(e, emit, list(r) + list(ro), list(w) + list(wo), (), ISSUE * len(pairs), 0.0, load, soft=list(ro) + list(wo))
 
     nadd = [0] * 12
 
@@ -579,9 +590,13 @@ def rank_program(g, core, T, topo):
         else:
             call = ts(flg, gap, 0.0, A.is_gt)
         op(ON["flag"], call, r=GK, w=["flg%d" % n], x=[bk], n=128)
-        op("P", mm(cnt, flg, T.bm[:], True, True), r=["flg%d" % n, "bm"], w=["cnt%d" % c], wo=[grp], x=[bk], us=pe(128))
         dm = T.dm[:, 4 * t + n, :]
-        op("V", tt(dm, cnt, T.thr[:], A.is_ge), r=["cnt%d" % c, "thr"], w=["dm%d%d" % (t, n)], x=[bk], n=128)
+        if ON["dead"] == "S":
+            op("P", [mm(cnt, T.ip[:], T.thr[:], True, False), mm(cnt, flg, T.bm[:], False, True)], r=["flg%d" % n, "bm", "thr", "ip"], w=["cnt%d" % c], wo=[grp], x=[bk], us=pe(128, 128))
+            op("S", lambda: S.activation(dm, cnt, ACT.Relu), r=["cnt%d" % c], w=["dm%d%d" % (t, n)], x=[bk], n=128)
+        else:
+            op("P", mm(cnt, flg, T.bm[:], True, True), r=["flg%d" % n, "bm"], w=["cnt%d" % c], wo=[grp], x=[bk], us=pe(128))
+            op("V", tt(dm, cnt, T.thr[:], A.is_ge), r=["cnt%d" % c, "thr"], w=["dm%d%d" % (t, n)], x=[bk], n=128)
         out = T.mb[:, 0, :, c:16:2]
         calls = [mm(out, T.ip[:], T.kk[:, c, :], True, False)] + [mm(out, T.dm[:, 4 * s + n, :], T.ones[:, 0:16], False, False) for s in range(t)]
         calls.append(mm(out, dm, T.rt[:, t, :], False, True))
@@ -595,8 +610,9 @@ def rank_program(g, core, T, topo):
     op("V", ms(T.rmax[:], BIG), w=["rmax"], n=256)
     op("V", ms(T.rmin[:, 0:512:8], BIG), w=["rmin"])
     op("V", ms(T.rmax[:, 0:512:8], -BIG), w=["rmax"])
-    op("V", ts(T.thr[:], T.qrow[:], fcol(5), A.not_equal, 64.0, A.mult), r=["qrow", "cf5"], w=["thr"], n=128)
-    op("V", ts(T.thr[:], T.thr[:], 15.5, A.max), w=["thr"], n=128)
+    sg = -1.0 if ON["dead"] == "S" else 1.0
+    op("V", ts(T.thr[:], T.qrow[:], fcol(5), A.not_equal, 64.0 * sg, A.mult), r=["qrow", "cf5"], w=["thr"])
+    op("V", ts(T.thr[:], T.thr[:], -15.0 if sg < 0 else 15.5, A.add), w=["thr"])
     op("V", ms(T.kk[:, 0, :], -56.0), w=["kk"])
     op("V", ms(T.kk[:, 1, :], 392.0), w=["kk"])
     for t, (m, k) in enumerate(((1.0, 4.0), (2.0, 1.0), (3.0, 4.0))):
@@ -628,7 +644,7 @@ def rank_program(g, core, T, topo):
         if t == 0:
             sends(0, 0)
             sends(0, 1)
-            dma("Y", table(T.pw1, T.pe, 1, range(4)), w=["pw1"], ro=["sent0", "sent1"], wo=["qY"], load=TAB, pre=lambda: g.sync.wait_ge(T.sem.loc0, nsig[0] + nsig[1]))
+            dma("Y", table(T.pw1, T.pe, 1, range(4)), w=["pw1"], r=["sent0", "sent1"], wo=["qY"], load=TAB, pre=lambda: g.sync.wait_ge(T.sem.loc0, nsig[0] + nsig[1]))
         for ph in range(2):
             now[0] = 2 * ph
             if t:

@@ -3,41 +3,45 @@ from concourse.mybir import AluOpType, ActivationFunctionType
 
 BF, F16, F32, I32, U16 = "bfloat16", "float16", "float32", "int32", "uint16"
 BIG = 1024.0
-MODE = [["PPF", "PPF", "PAF", "AAF"], ["AAP", "PAF", "AAP", "PAF"], ["AAP", "PAF", "AAP", "PAF"], ["AF", "AA", "AF", "PF"]]
+MODE = [["PPF", "PPF", "PAF", "AAF"], ["AAP", "PAF", "AAP", "PAF"], ["AAP", "PAF", "AAP", "PAF"], ["AA", "AA", "AF", "AF"]]
 VG = [[[], [], [], []], [[], [], [], []], [[], [], [], []], [[], [], [], []]]
-UNITS = [[(0, 2), (0, 0), (0, 3), (0, 1), (1, 2), (1, 1), (1, 3), (1, 0)], [(0, 2), (0, 0), (0, 3), (0, 1), (1, 2), (1, 0), (1, 3), (1, 1)]]
-LISTS = [[(0, [2]), (0, [0]), (0, [3]), (0, [1]), (1, [0, 1, 2, 3])], [(0, [2]), (0, [0]), (0, [3]), (0, [1]), (1, [0, 1, 2, 3])]]
-HALVES = [[(1, 0)], []]
-EARLY = [0, 1]
-CHAIN = "S"
+UNITS = [[(0, 2), (1, 2), (0, 3), (1, 3), (0, 0), (0, 1), (1, 1), (1, 0)], [(0, 2), (0, 0), (0, 3), (0, 1), (1, 2), (1, 0), (1, 3), (1, 1)],
+         [(0, 2), (0, 0), (0, 3), (0, 1), (1, 2), (1, 0), (1, 3), (1, 1)]]
+HALVES = [[(1, 0), (0, 3), (1, 3), (0, 0)], [], [(1, 1), (0, 1)]]
+SPLIT = [[], [], [(1, 0), (1, 1), (1, 2), (1, 3)]]
+LISTS = [[[2], [3], [1], [0]], [[2], [0], [3], [1]], [[2], [0], [3], [1]]]
+EARLY = [1, 1]
 PACE = [0, 0, 0, 1, 4, 7, 8, 9]
-ON = {"flag": "V", "dead": "V", "cn": "V", "mine": "V", "yg": "S", "rows": "S"}
-CYC, PEC, WAKE, EPS, GCYC, ADDUS, DW, FLIGHT = 1.0e-3, 0.75e-3, 0.07, 0.3, 1.6, 2.0, 1.0, 4.6
-TAB, SEND, ISSUE = 3.75, 1.5, 0.1
-PASSES, KEEP, MIX = 12, 1.0, 0.8
+ON = {"flag": "V", "cn": "V", "mine": "V"}
+WAKE, EPS, IDLE, ADDUS, FLIGHT = 0.07, 0.3, 8.0, 2.0, 1.9
+START, LAND, TAB, SEND, ISSUE, CALL = 1.4, 0.5, 3.75, 1.5, 0.1, 0.025
+PASSES, MIX = 4, 0.8
+TRIES, STRETCH, NOISE, SEED = 600, 40, 2.0, 1
+PLANS = [(.9e-3, 1.6, .75e-3, .9), (.95e-3, 1.5, .72e-3, .9), (1.0e-3, 1.5, .75e-3, .9), (1.0e-3, 1.75, .8e-3, .85)]
+SPEEDS = [(.83e-3, 1.56, .714e-3, .85), (.91e-3, 1.2, .714e-3, .9), (.95e-3, 2.0, .714e-3, .9), (1.04e-3, 1.56, .714e-3, .8), (1.04e-3, 1.3, .89e-3, .9),
+          (1.16e-3, 1.15, .714e-3, .9), (1.16e-3, 1.8, 1.0e-3, .9), (1.2e-3, 2.0, .714e-3, .9)]
 ORDER, LOG = [], []
-START, LAND, IDLE = 1.4, 0.5, 8.0
 ND, NDMA = 4, 30
 SCRATCH = {
     "pw0": ("sbuf", [128, 4096], BF), "pw1": ("sbuf", [128, 4096], BF), "sw0": ("sbuf", [128, 4096], I32), "sw1": ("sbuf", [128, 4096], I32),
     "cq0": ("sbuf", [128, 896], I32), "cq1": ("sbuf", [128, 896], I32), "candl": ("sbuf", [128, 4, 28], I32), "tin": ("sbuf", [128, 4, 32], F32),
-    "ngi": ("sbuf", [128, 2, 16], I32), "ngf": ("sbuf", [128, 2, 16], F32), "nbu": ("sbuf", [128, 16], U16),
-    "gm": ("sbuf", [128, 2, 8, 16], F32), "geor": ("sbuf", [128, 2, 4, 2, 16], F32),
+    "ngi": ("sbuf", [128, 2, 16], I32), "ngf": ("sbuf", [128, 2, 16], F32), "nbu": ("sbuf", [128, 16], U16), "gl": ("sbuf", [128, 2, 8], F32),
+    "gm": ("sbuf", [128, 2, 8, 16], F32), "geor": ("sbuf", [128, 2, 4, 128], F32),
     "ones": ("sbuf", [128, 128], BF), "zero": ("sbuf", [128, 128], BF), "ip": ("sbuf", [128, 128], BF), "im": ("sbuf", [128, 128], BF),
-    "ip16": ("sbuf", [128, 128], F16), "im16": ("sbuf", [128, 128], F16),
+    "ip16": ("sbuf", [128, 128], F16), "im16": ("sbuf", [128, 128], F16), "one32": ("sbuf", [128, 128], F32),
     "bm": ("sbuf", [128, 128], BF), "bf32": ("sbuf", [128, 128], F32), "bn": ("sbuf", [128, 128], BF), "kc": ("sbuf", [128, 128], BF),
-    "selk": ("sbuf", [128, 128], F16), "casel": ("sbuf", [128, 2, 128], F16), "hrow": ("sbuf", [128, 128], BF), "csel": ("sbuf", [128, 16, 128], F16),
-    "lnb": ("sbuf", [128, 4, 128], F32), "m16": ("sbuf", [128, 16], F32),
-    "prow": ("sbuf", [128, 128], BF), "qrow": ("sbuf", [128, 128], BF), "grow": ("sbuf", [128, 128], BF), "krow": ("sbuf", [128, 128], BF), "lrow": ("sbuf", [128, 128], F32),
-    "tg": ("sbuf", [128, 16], BF), "rt": ("sbuf", [128, 3, 16], BF), "ru": ("sbuf", [128, 3, 16], BF), "kk": ("sbuf", [128, 2, 16], BF),
-    "arow": ("sbuf", [128, 16], BF), "brow": ("sbuf", [128, 64], BF), "thr": ("sbuf", [128, 128], BF),
-    "rmin": ("sbuf", [128, 512], BF), "rmax": ("sbuf", [128, 512], BF),
-    "ci": ("sbuf", [128, 16], I32), "cf": ("sbuf", [128, 24], F32),
+    "casel": ("sbuf", [128, 2, 128], F16), "xsel": ("sbuf", [128, 2, 128], F16), "csel": ("sbuf", [128, 16, 128], F16),
+    "lnb": ("sbuf", [128, 4, 128], F32), "m16": ("sbuf", [128, 16], F32), "thr": ("sbuf", [128, 128], BF), "back": ("sbuf", [128, 2, 64], F16),
+    "prow": ("sbuf", [128, 128], BF), "qrow": ("sbuf", [128, 128], BF), "grow": ("sbuf", [128, 128], BF), "hrow": ("sbuf", [128, 128], BF),
+    "krow": ("sbuf", [128, 128], BF), "arow": ("sbuf", [128, 16], BF), "brow": ("sbuf", [128, 64], BF),
+    "rt": ("sbuf", [128, 3, 16], BF), "ru": ("sbuf", [128, 3, 16], BF), "kk": ("sbuf", [128, 2, 16], BF),
+    "rmin": ("sbuf", [128, 1024], BF), "rmax": ("sbuf", [128, 1024], BF),
+    "ci": ("sbuf", [128, 8], I32), "cf": ("sbuf", [128, 24], F32),
     "pos": ("sbuf", [128, 2, 16, 2], F32), "offc": ("sbuf", [128, 32], U16), "offs": ("sbuf", [128, 32], U16), "tl": ("sbuf", [128, 2, 2, 32], F32),
     "crow": ("sbuf", [128, 2, 256], F16), "own": ("sbuf", [128, 2, 256], F16), "crx": ("sbuf", [128, 4, 128], F32),
-    "cn": ("sbuf", [128, 256], F32), "idx": ("sbuf", [128, 16, 4, 16], I32), "off": ("sbuf", [128, 1024], U16),
+    "cn": ("sbuf", [128, 256], F32), "idx": ("sbuf", [128, 1024], I32), "off": ("sbuf", [128, 1024], U16),
     "flg": ("sbuf", [128, 4, 128], BF), "dm": ("sbuf", [128, 12, 128], BF),
-    "gh": ("sbuf", [128, 4, 128], F16), "back": ("sbuf", [128, 2, 64], F16), "ygb": ("sbuf", [128, 2, 256], F32), "ycb": ("sbuf", [128, 4, 128], F32),
+    "gh": ("sbuf", [128, 4, 128], F16), "ygb": ("sbuf", [128, 2, 256], F32), "ycb": ("sbuf", [128, 4, 128], F32),
     "ca": ("psum", [128, 4, 2, 4, 16], F32), "gp0": ("psum", [128, 16, 4, 8], F32), "gp1": ("psum", [128, 16, 4, 8], F32), "mb": ("psum", [128, 16, 2, 16], F32),
 }
 for _k in range(ND):
@@ -47,7 +51,11 @@ for _n in range(4):
     SCRATCH["sc%d" % _n] = ("sbuf", [128, 4, 1024], BF)
 for _n in range(8):
     SCRATCH["w%d" % _n] = ("sbuf", [128, 256], F32)
-SEMAPHORES = ["loc0", "sV", "sS", "sP", "sG", "loc"] + ["arr%d" % i for i in range(8)] + ["dma%d" % i for i in range(NDMA)] + ["add%d" % i for i in range(12)]
+SEMAPHORES = ["loc0", "loc", "sV", "sS", "sP", "sG"] + ["arr%d" % i for i in range(8)] + ["dma%d" % i for i in range(NDMA)] + ["add%d" % i for i in range(12)]
+
+
+def kind(t, n):
+    return 1 + n // 2 if t == 3 else 0
 
 
 def lane(t, b):
@@ -69,7 +77,7 @@ def order(prog):
                 s[wr[k]] = s.get(wr[k], False) or k not in p["soft"]
         for k in p["w"]:
             for q in rd.get(k, ()):
-                s[q] = s.get(q, False) or (k not in p["soft"] and (prog[q]["e"] != p["e"] or prog[q]["dma"] > 0))
+                s[q] = s.get(q, False) or (k not in p["soft"] and (prog[q]["e"] != p["e"] or prog[q]["load"] > 0))
         s.pop(i, None)
         for k in p["r"]:
             rd.setdefault(k, []).append(i)
@@ -84,32 +92,85 @@ def order(prog):
 
     def way(i, tail):
         p = prog[i]
-        wait = p["lat"] + (p["dma"] * DW + START + LAND if p["dma"] else 0.0) + WAKE
+        wait = p["lat"] + (p["dma"] + START + LAND if p["dma"] else 0.0) + WAKE
         return p["us"] + max([tail[q] + (wait if hard else 0.0) for q, hard in succs[i]] + [wait])
-    rank = [0.0] * n
-    for i in range(n - 1, -1, -1):
-        rank[i] = way(i, rank)
-    best = None
-    for _ in range(PASSES):
-        total, seq, where, ends = place(prog, succs, list(left), dict(users), rank)
-        if best is None or total < best[0]:
-            best = (total, seq, where)
-        tail, after = [0.0] * n, {}
-        for i in reversed(seq):
-            p = prog[i]
-            own = way(i, tail)
-            tail[i] = max(own, p["us"] * KEEP + after.get(p["e"], 0.0), p["dma"] + after.get("dma", 0.0) if p["dma"] else 0.0)
-            after[p["e"]] = tail[i]
-            if p["dma"]:
-                after["dma"] = tail[i]
-            rank[i] = MIX * rank[i] + (1 - MIX) * own
-    LOG.append(best[0])
-    return best[1], best[2]
+
+    def speeds(cyc, gat, pec, dma):
+        for p in prog:
+            c = p["cost"]
+            p["us"] = c[0] + (c[1] + c[2] * gat) * cyc + c[3] * pec
+            p["dma"], p["lat"] = p["load"] * dma, p["far"] * dma
+
+    found = []
+    for plan in PLANS:
+        speeds(*plan)
+        rank = [0.0] * n
+        for i in range(n - 1, -1, -1):
+            rank[i] = way(i, rank)
+        for _ in range(PASSES):
+            seq, where = place(prog, succs, list(left), dict(users), rank)
+            found.append((seq, where, plan, list(rank)))
+            tail, after = [0.0] * n, {}
+            for i in reversed(seq):
+                p = prog[i]
+                own = way(i, tail)
+                tail[i] = max(own, p["us"] + after.get(p["e"], 0.0), p["dma"] + after.get("dma", 0.0) if p["dma"] else 0.0)
+                after[p["e"]] = tail[i]
+                if p["dma"]:
+                    after["dma"] = tail[i]
+                rank[i] = MIX * rank[i] + (1 - MIX) * own
+    costs, least = [], []
+    for s in SPEEDS:
+        speeds(*s)
+        costs.append([dict(p) for p in prog])
+        least.append(min(replay(prog, succs, f[0], f[1]) for f in found))
+
+    def worth(seq, where):
+        row = [replay(c, succs, seq, where) / b for c, b in zip(costs, least)]
+        return sum(row) / len(row) + max(row)
+    seq, where, plan, rank = min(found, key=lambda f: worth(f[0], f[1]))
+    speeds(*plan)
+    now, x = worth(seq, where), SEED
+    for _ in range(TRIES):
+        x = (x * 1103515245 + 12345) % 2 ** 31
+        lo = x % n
+        trial = list(rank)
+        for i in seq[lo:lo + STRETCH]:
+            x = (x * 1103515245 + 12345) % 2 ** 31
+            trial[i] += NOISE * (x / 2.0 ** 30 - 1.0)
+        s, w = place(prog, succs, list(left), dict(users), trial)
+        v = worth(s, w)
+        if v < now:
+            now, seq, where, rank = v, s, w, trial
+    LOG.append(now)
+    return seq, where
+
+
+def replay(prog, succs, seq, where):
+    at = [0.0] * len(prog)
+    qfree, bank, engines, total = {}, {}, 0.0, 0.0
+    for i in seq:
+        p = prog[i]
+        e = p["e"]
+        t = max(at[i], qfree.get(e, 0.0))
+        xs = p["x"] + [where[v] for v in p["use"]] + ([] if p["alloc"] is None else [where[p["alloc"]]])
+        for b in xs:
+            if b in bank and bank[b][0] != e:
+                t = max(t, bank[b][1] + WAKE)
+        end = qfree[e] = t + p["us"]
+        if p["dma"]:
+            engines = max(t + START + (p["us"] if p["lat"] else 0.0), engines) + p["dma"]
+            end = engines + (p["lat"] or LAND)
+        for b in xs:
+            bank[b] = (e, end)
+        for q, hard in succs[i]:
+            at[q] = max(at[q], end + WAKE if hard else qfree[e])
+        total = max(total, end)
+    return total
 
 
 def place(prog, succs, left, users, rank):
     n = len(prog)
-    ends = [0.0] * n
     at = [0.0] * n
     ready = [i for i in range(n) if not left[i]]
     qfree, bank, engines = {}, {}, 0.0
@@ -141,7 +202,7 @@ def place(prog, succs, left, users, rank):
             engines = max(t + START + (p["us"] if p["lat"] else 0.0), engines) + p["dma"]
             end = engines + (p["lat"] or LAND)
         else:
-            end = t + p["us"] + p["lat"]
+            end = t + p["us"]
         for b in p["x"]:
             bank[b] = (e, end)
         for v in p["use"]:
@@ -150,14 +211,13 @@ def place(prog, succs, left, users, rank):
                 free[where[v]] = end
         ready.remove(i)
         seq.append(i)
-        ends[i] = end
         for q, hard in succs[i]:
             left[q] -= 1
             at[q] = max(at[q], end + WAKE if hard else qfree[e])
             if not left[q]:
                 ready.append(q)
     assert len(seq) == n
-    return max(ends), seq, where, ends
+    return seq, where
 
 
 def rank_program(g, core, T, topo):
@@ -170,11 +230,10 @@ def rank_program(g, core, T, topo):
     queue = {"V": V, "S": S, "P": P, "G": g, "Y": g.sync}
 
     prog = []
-    now = [0]
     where = {}
 
-    def rec(e, emit, r, w, x, us, lat=0.0, load=0.0, use=(), alloc=None, soft=()):
-        prog.append({"e": e, "emit": emit, "r": list(r), "w": list(w), "x": list(x), "us": us, "lat": lat, "dma": load, "use": list(use), "alloc": alloc, "soft": list(soft)})
+    def rec(e, emit, r, w, x, cost, far=0.0, load=0.0, use=(), alloc=None, soft=()):
+        prog.append({"e": e, "emit": emit, "r": list(r), "w": list(w), "x": list(x), "cost": cost, "far": far, "load": load, "use": list(use), "alloc": alloc, "soft": list(soft)})
 
     def op(e, calls, r=(), w=(), x=(), n=64, us=None, use=(), alloc=None, pre=None, ro=(), wo=()):
         calls = calls if isinstance(calls, list) else [calls]
@@ -189,9 +248,9 @@ def rank_program(g, core, T, topo):
                 call().then_inc(T.sem[sem], 1)
                 count[sem] += 1
             done(e, sem, count[sem], r, w, xs)
-        rec(e, emit, list(r) + list(ro), list(w) + list(wo), x, max(64, n) * CYC if us is None else us, 0.0, 0.0, use, alloc, list(ro) + list(wo))
+        rec(e, emit, list(r) + list(ro), list(w) + list(wo), x, (CALL * len(calls), max(64, n), 0, 0) if us is None else us, 0.0, 0.0, use, alloc, list(ro) + list(wo))
 
-    def dma(e, pairs, r=(), w=(), load=0.3, ro=(), wo=(), pre=None):
+    def dma(e, pairs, r=(), w=(), load=0.3, wo=(), pre=None):
         def emit():
             if pre:
                 pre()
@@ -201,7 +260,7 @@ def rank_program(g, core, T, topo):
             for out, in_ in pairs:
                 queue[e].dma_start(out, in_).then_inc(T.sem[sem], 16)
             done(e, sem, ndma[-1], r, w)
-        rec(e, emit, list(r) + list(ro), list(w) + list(wo), (), ISSUE * len(pairs), 0.0, load, soft=list(ro) + list(wo))
+        rec(e, emit, r, list(w) + list(wo), (), (ISSUE * len(pairs), 0, 0, 0), 0.0, load, soft=wo)
 
     nadd = [0] * 12
 
@@ -211,7 +270,7 @@ def rank_program(g, core, T, topo):
             nadd[i] += 16
             g.dma_start(out, in_, accum_op=A.add).then_inc(T.sem["add%d" % i], 16)
             done("G", "add%d" % i, nadd[i], r, w)
-        rec("G", emit, r, w, (), 1.0, 0.0, ADDUS)
+        rec("G", emit, r, w, (), (1.0, 0, 0, 0), 0.0, ADDUS)
 
     count = {"sV": 0, "sS": 0, "sP": 0, "sG": 0}
     know = {e: {} for e in queue}
@@ -275,6 +334,9 @@ def rank_program(g, core, T, topo):
             return lambda: S.activation(out, a, ACT.Copy)
         return lambda: V.tensor_copy(out, a)
 
+    def lin(out, a, scale, bias=0.0):
+        return lambda: S.activation(out, a, ACT.Identity, bias=bias, scale=scale)
+
     def ms(out, v):
         return lambda: V.memset(out, v)
 
@@ -282,77 +344,77 @@ def rank_program(g, core, T, topo):
         return lambda: P.matmul(out, l, rhs, st, sp)
 
     def gat(n):
-        return .06 + GCYC * CYC * n
+        return (.06, 0, n, 0)
 
     def pe(*ns):
-        return sum(max(64, n) for n in ns) * PEC
+        return (0.0, 0, 0, sum(max(64, n) for n in ns))
+
+    def countdown(k):
+        left = [k]
+
+        def last():
+            left[0] -= 1
+            return left[0] == 0
+        return last
 
     def table(win, src, ph, ks):
         return [(win[32 * k + 16 * h:32 * k + 16 * h + 16, :], src[64 * ph + 16 * k:64 * ph + 16 * k + 16, :]) for k in ks for h in range(2)]
 
     def queues(ph):
         op("V", ms(CQ[ph][:], 4096), w=["cq%d" % ph], n=896)
-        dma("S", [(CQ[ph][0:128:16, 448 * c:448 * c + 448], T.cand[4 * ph:4 * ph + 4, 896 * c:896 * c + 896]) for c in range(2)], w=["cq%d" % ph], wo=["qS"], load=.1)
+        dma("YS"[ph], [(CQ[ph][0:128:16, 448 * c:448 * c + 448], T.cand[4 * ph:4 * ph + 4, 896 * c:896 * c + 896]) for c in range(2)], w=["cq%d" % ph], wo=["q" + "YS"[ph]], load=.1)
 
-    for ph in range(2):
-        dma("Y", [(T.candl[:, 2 * ph + c, :], T.cand[4 * ph:4 * ph + 4, 896 * c:896 * c + 896]) for c in range(2)], w=["candl%d" % ph], wo=["qY"])
-    dma("S", [(T.ngi[:, 0, :], T.nb[:]), (T.ngi[:, 1, :], T.geo[:])], w=["ngi"], wo=["qS"])
+    def first(e, n):
+        dma(e, [(T.candl[:, n, :], T.cand[4 * (n // 2):4 * (n // 2) + 4, 896 * (n % 2):896 * (n % 2) + 896])], w=["candl%d" % n], wo=["q" + e])
+
+    first("Y", 0)
+    first("S", 1)
+    dma("S", [(T.ngi[:, 0, :], T.nb[:]), (T.ngi[:, 1, :], T.geo[:])], w=["ngi"], wo=["qS"], load=.6)
+    first("Y", 2)
+    first("Y", 3)
     queues(0)
     dma("Y", table(T.pw0, T.pe, 0, range(4)), w=["pw0"], wo=["qY"], load=TAB)
     queues(1)
 
-    ci, cf = T.ci, T.cf
-
     def icol(k):
-        return ci[:, k:k + 1]
+        return T.ci[:, k:k + 1]
 
     def fcol(k):
-        return cf[:, k:k + 1]
+        return T.cf[:, k:k + 1]
 
-    FREE = {"allow_small_or_imprecise_dtypes": True}
-
-    def iota(name, out, pattern, base=0, cm=0):
+    def iota(name, pattern, base=0):
         n = 1
         for _, m in pattern:
             n *= m
-        op("G", lambda: g.iota(out, pattern, base, cm, **FREE), w=[name], us=.13 + 2 * n * CYC)
+        op("G", lambda: g.iota(T[name][:], pattern, base, 0, allow_small_or_imprecise_dtypes=True), w=[name], us=(.13, 2 * n, 0, 0))
 
-    op("G", lambda: g.iota(icol(0), [[0, 1]], 0, 1), w=["ci0"], us=.13)
-    iota("lrow", T.lrow[:], [[16, 4], [128, 2], [1, 16]])
-    iota("qrow", T.qrow[:], [[0, 8], [1, 16]])
-    iota("grow", T.grow[:], [[1, 8], [0, 16]])
-    iota("pos", T.pos[:], [[0, 4], [1, 8], [448, 2]])
-    iota("arow", T.arow[:], [[0, 2], [1, 8]])
-    iota("hrow", T.hrow[:], [[2, 8], [1, 2], [0, 8]])
-    iota("prow", T.prow[:], [[1, 128]])
-    iota("krow", T.krow[:], [[8, 4], [0, 4], [1, 8]])
-    iota("brow", T.brow[:], [[32, 4], [1, 16]])
-    op("V", ms(T.ones[:], 1.0), w=["ones"])
-    op("V", ms(T.zero[:], 0.0), w=["zero"])
+    def select(out, in_, pattern, base, cm, r, w):
+        op("G", lambda: g.affine_select(out, in_, pattern, A.is_equal, 0.0, base, cm), r=r, w=w, us=(.17, 256, 0, 0))
 
-    def bits(k, shift, mask):
-        op("V", ts(icol(k), icol(0), shift, A.arith_shift_right, mask, A.bitwise_and), r=["ci0"], w=["ci%d" % k])
-        op("V", cp(fcol(k), icol(k)), r=["ci%d" % k], w=["cf%d" % k])
-
-    op("V", cp(fcol(0), icol(0)), r=["ci0"], w=["cf0"])
-    bits(1, 0, 15)
-    bits(2, 4, 7)
-    bits(3, 5, 3)
-    bits(4, 0, 31)
-    bits(5, 1, 15)
-    bits(6, 0, 1)
-    op("V", ts(T.bm[:], T.grow[:], fcol(2), A.is_equal), r=["grow", "cf2"], w=["bm"], n=128)
-    op("V", ts(T.bf32[:], T.grow[:], fcol(2), A.is_equal), r=["grow", "cf2"], w=["bf32"], n=128)
-    op("V", ts(fcol(7), fcol(1), 1.5, A.is_lt), r=["cf1"], w=["cf7"])
-    op("V", ts(T.selk[:], T.bm[:], fcol(7), A.mult), r=["bm", "cf7"], w=["selk"], n=128)
-    op("V", ts(fcol(9), fcol(1), 1.5, A.is_gt, 64.0, A.mult), r=["cf1"], w=["cf9"])
-    op("V", ts(fcol(9), fcol(2), 2.0, A.mult, fcol(9), A.add), r=["cf2"], w=["cf9"])
-    for b in range(2):
-        op("V", ts(T.casel[:, b, :], T.hrow[:], -1.0 * b, A.add, fcol(9), A.is_equal), r=["hrow", "cf9"], w=["caselb%d" % b], n=128)
-    op("V", ts(fcol(8), fcol(1), 28.0, A.mult), r=["cf1"], w=["cf8"])
-    op("V", ts(T.m16[:], T.qrow[:, 0:16], fcol(1), A.is_equal), r=["qrow", "cf1"], w=["m16"])
+    op("G", lambda: g.iota(icol(0), [[0, 1]], 0, 1), w=["ci0"], us=(.13, 0, 0, 0))
+    iota("qrow", [[0, 8], [1, 16]])
+    iota("grow", [[1, 8], [0, 16]])
+    iota("pos", [[0, 4], [1, 8], [448, 2]])
+    iota("arow", [[0, 2], [1, 8]])
+    iota("hrow", [[2, 8], [1, 2], [0, 8]])
+    iota("prow", [[1, 128]])
+    iota("krow", [[4, 4], [0, 32]])
+    iota("brow", [[32, 4], [1, 16]])
+    iota("kk", [[448, 2], [0, 16]], -56)
+    op("V", ms(T.one32[:], 1.0), w=["one32"], n=128)
+    op("S", cp(T.ones[:], T.one32[:], "S"), r=["one32"], w=["ones"], n=128)
+    op("S", lin(T.zero[:], T.one32[:], 0.0), r=["one32"], w=["zero"], n=128)
+    op("V", [ts(icol(k), icol(0), shift, A.arith_shift_right, mask, A.bitwise_and) for k, shift, mask in ((1, 0, 15), (2, 4, 7), (3, 5, 3), (4, 1, 15), (5, 0, 1))], r=["ci0"], w=["ci"], n=320)
+    op("V", cp(T.cf[:, 0:6], T.ci[:, 0:6]), r=["ci0", "ci"], w=["cf"])
+    op("V", ts(T.bf32[:], T.grow[:], fcol(2), A.is_equal), r=["grow", "cf"], w=["bf32"], n=128)
+    op("S", cp(T.bm[:], T.bf32[:], "S"), r=["bf32"], w=["bm"], n=128)
+    op("V", ts(fcol(6), fcol(1), 1.5, A.is_gt, 64.0, A.mult), r=["cf"], w=["cf6"])
+    op("S", lin(fcol(7), fcol(2), 2.0, fcol(6)), r=["cf", "cf6"], w=["cf7"])
+    op("V", [ts(T.casel[:, b, :], T.hrow[:], -1.0 * b, A.add, fcol(7), A.is_equal) for b in range(2)], r=["hrow", "cf7"], w=["casel"], n=128)
+    op("S", lin(fcol(8), fcol(1), 28.0), r=["cf"], w=["cf8"])
+    op("V", ts(T.m16[:], T.qrow[:, 0:16], fcol(1), A.is_equal), r=["qrow", "cf"], w=["m16"])
     for i in range(4):
-        op("V", ts(T.lnb[:, i, :], T.lrow[:], 64.0 * (i // 2) - 128.0 * (i % 2), A.add, fcol(0), A.is_equal), r=["lrow", "cf0"], w=["lnb%d" % i], n=128)
+        select(T.lnb[:, i, :], T.one32[:], [[-16, 4], [-128, 2], [-1, 16]], 128 * (i % 2) - 64 * (i // 2), 1, ["one32"], ["lnb%d" % i])
 
     nsig = [0] * 8
 
@@ -371,31 +433,33 @@ def rank_program(g, core, T, topo):
             tr = RemoteDMATransfer(dst_ids=ids, dma_engine_mask=m, remote_sem=T.sem["arr%d" % i], srcs=[mine], dsts=[mine for _ in ids])
             g.remote_dma_fused([tr], local_sem=T.sem["loc" if t else "loc0"])
             nsig[i] += bin(m).count("1")
-        rec("G", emit, ["wown%d" % i], ["sent%d" % i], [], .6 if i else 3.0, FLIGHT - SEND - 1.2, SEND)
+        rec("G", emit, ["wown%d" % i], ["sent%d" % i], [], (.6 if i else 3.6, 0, 0, 0), FLIGHT, SEND)
 
     for ph in range(2):
-        cand, tin = T.candl[:, 2 * ph:2 * ph + 2, :], T.tin[:, 2 * ph:2 * ph + 2, :]
-        op("V", [cp(T.tin[:, 2 * ph:2 * ph + 2, 8 * i:8 * i + 8], T.candl[:, 2 * ph:2 * ph + 2, 0:8]) for i in range(4)], r=["candl%d" % ph], w=["tin%d" % ph], n=256)
-        op("V", lambda ph=ph, tin=tin: V.transpose(W[ph][:, 64 * rank:64 * rank + 64], tin), r=["tin%d" % ph], w=["wown%d" % ph])
+        keys, two = ["candl%d" % (2 * ph), "candl%d" % (2 * ph + 1)], slice(2 * ph, 2 * ph + 2)
+        op("V", [cp(T.tin[:, two, 8 * i:8 * i + 8], T.candl[:, two, 0:8]) for i in range(1 if ph else 4)], r=keys, w=["tin%d" % ph], n=64 if ph else 256)
+        if ph:
+            op("S", [cp(T.tin[:, two, 8 * i:8 * i + 8], T.tin[:, two, 0:8], "S") for i in range(1, 4)], r=["tin1"], w=["tin2"], n=192)
+        op("V", lambda ph=ph, two=two: V.transpose(W[ph][:, 64 * rank:64 * rank + 64], T.tin[:, two, :]), r=["tin%d" % ph, "tin%d" % (2 * ph)], w=["wown%d" % ph])
         send(0, ph)
-        op("V", [cp(T.offs[:, 16 * ph + 8 * b:16 * ph + 8 * b + 8], T.candl[:, 2 * ph:2 * ph + 2, 4 * b:4 * b + 4]) for b in range(2)], r=["candl%d" % ph], w=["offs%d" % ph], n=128)
+        op("V", [cp(T.offs[:, 16 * ph + 8 * b:16 * ph + 8 * b + 8], T.candl[:, two, 4 * b:4 * b + 4]) for b in range(2)], r=keys, w=["offs%d" % ph], n=128)
 
     op("V", cp(T.ngf[:], T.ngi[:]), r=["ngi"], w=["ngf"])
     for ph in range(2):
         op("P", [mm(T.mb[:, 8:10, ph, 0:8], T.lnb[:, 2 * ph + h, :], T.ngf[:, :, h:16:2], h == 0, h == 1) for h in range(2)],
            r=["ngf", "lnb%d" % (2 * ph), "lnb%d" % (2 * ph + 1)], w=["mbn%d" % ph], x=["mb"], us=pe(256, 256))
         op("V", [cp(T.nbu[:, 8 * ph + 4 * c:8 * ph + 4 * c + 4], T.mb[:, 8, ph, c:8:2]) for c in range(2)], r=["mbn%d" % ph], w=["nbu%d" % ph], x=["mb"], n=128)
-        for i in range(8):
-            op("V", ts(T.gm[:, ph, i, :], T.m16[:], T.mb[:, 9, ph, i:i + 1], A.mult), r=["m16", "mbn%d" % ph], w=["gm%d%d" % (ph, i)], x=["mb"])
-        op("P", mm(GP[ph][:, 12:16, :, :], T.bf32[:], T.gm[:, ph, :, :], True, True), r=["bf32"] + ["gm%d%d" % (ph, i) for i in range(8)], w=["gpg%d" % ph],
-           wo=["grp%d" % ph], x=["gp%d" % ph], us=pe(512))
-        op("S", lambda ph=ph: S.activation(T.geor[:, ph, :, :, :], GP[ph][:, 12:16, :, :], ACT.Copy, bias=-65536.0, scale=16.0), r=["gpg%d" % ph], w=["geor%d" % ph], x=["gp%d" % ph], n=128)
+        op("S", cp(T.gl[:, ph, :], T.mb[:, 9, ph, 0:8], "S"), r=["mbn%d" % ph], w=["gl%d" % ph], x=["mb"])
+        op("S", [lin(T.gm[:, ph, 4 * (i % 2) + i // 2, :], T.m16[:], T.gl[:, ph, i:i + 1]) for i in range(8)], r=["m16", "gl%d" % ph], w=["gm%d" % ph], n=512)
+        op("P", mm(GP[ph][:, 12:16, :, :], T.bf32[:], T.gm[:, ph, :, :], True, True), r=["bf32", "gm%d" % ph], w=["gpg%d" % ph], wo=["grp%d" % ph], x=["gp%d" % ph], us=pe(512))
+        for al in (2, 0, 1, 3):
+            op("S", lin(T.geor[:, ph, al, :], GP[ph][:, 12:16, :, :], 16.0, -65536.0), r=["gpg%d" % ph], w=["geor%d%d" % (ph, al)], x=["gp%d" % ph], n=128)
 
     def sends(t, ph):
-        key = "pos%d" % ph
         lo = 16 * ph
         lanes = [slice(a, a + 3 * s + 1, s) for a, s in (lane(t, 0), lane(t, 1))]
-        op("V", [ts(T.offc[:, lo + 8 * b:lo + 8 * b + 8], T.pos[:, ph, lanes[b], :], fcol(8), A.add) for b in range(2)], r=["pos", key, "cf8"], w=["offc%d" % ph], n=128)
+        both = [(T.offc[:, lo + 8 * b:lo + 8 * b + 8], lanes[b]) for b in range(2)] if t else [(T.offc[:, lo:lo + 16], slice(0, 8))]
+        op("V", [ts(out, T.pos[:, ph, a, :], fcol(8), A.add) for out, a in both], r=["pos", "pos%d" % ph, "cf8"], w=["offc%d" % ph], n=64 * len(both))
         op("V", ts(T.crow[:, ph, :], CQ[ph][:].indirect(T.offc[:, lo:lo + 16]), -2048.0, A.add), r=["cq%d" % ph, "offc%d" % ph], w=["crow%d" % ph], us=gat(256))
         if t:
             i = 2 * t + ph
@@ -408,11 +472,10 @@ def rank_program(g, core, T, topo):
             op("V", [cp(T.offs[:, lo + 8 * b:lo + 8 * b + 8], T.tl[:, ph, :, lanes[b]]) for b in range(2)], r=["tl%d" % ph], w=["offs%d" % ph], n=128)
 
     def codes(t, ph):
-        lo = 16 * ph
         calls = [mm(T.ca[:, :, :, j, :], T.casel[:, b, :], T.crow[:, ph, 128 * b:128 * b + 128], b == 0, b == 1) for j in range(4) for b in range(2)]
-        op("P", calls, r=["crow%d" % ph, "caselb0", "caselb1"], w=["ca%d%d" % (c, al) for c in range(2) for al in range(4)], x=["ca"], us=pe(*[128] * 8))
+        op("P", calls, r=["crow%d" % ph, "casel"], w=["ca%d" % al for al in range(4)], x=["ca"], us=pe(*[128] * 8))
 
-    def selves(t, ph):
+    def selves(ph):
         op("V", cp(T.own[:, ph, :], SW[ph][:].indirect(T.offs[:, 16 * ph:16 * ph + 16])), r=["sw%d" % q for q in range(4 * ph, 4 * ph + 4)] + ["offs%d" % ph], w=["own%d" % ph], us=gat(256))
 
     def neighbours(t, ph):
@@ -420,19 +483,14 @@ def rank_program(g, core, T, topo):
         op(e, cp(T.cn[:, 128 * ph:128 * ph + 128], W[i][:].indirect(T.nbu[:, 8 * ph:8 * ph + 8]), e), r=["nbu%d" % ph, "wown%d" % i, "sent%d" % i],
            w=["cn%d" % ph], us=gat(128), pre=lambda: queue[e].wait_ge(T.sem["arr%d" % i], 3 * nsig[i]))
 
-    def index(n, groups):
-        ph, c = n // 2, n % 2
-        for als in groups:
-            ks = [4 * n + al for al in als]
-            for al in als:
-                ca = T.ca[:, al, c, :, :]
-                op("V", tt(ca, T.cn[:, 64 * n:64 * n + 64], ca, A.mult), r=["cn%d" % ph], w=["ca%d%d" % (c, al)], x=["ca"])
-            for al in als:
-                op("V", tt(T.idx[:, 4 * n + al, :, :], T.ca[:, al, c, :, :], T.geor[:, ph, :, c, :], A.add), r=["ca%d%d" % (c, al), "geor%d" % ph], w=["ix%d" % (4 * n + al)], x=["ca"])
-            IX = ["ix%d" % k for k in ks]
-            v = T.idx[:, ks[0]:ks[-1] + 1, :, :]
-            op("V", ts(v, v, 4, A.arith_shift_right, 4095, A.bitwise_and), r=IX, w=IX, n=64 * len(ks))
-            op("V", cp(T.off[:, 64 * ks[0]:64 * ks[-1] + 64], v), r=IX, w=["of%d" % k for k in ks], n=64 * len(ks))
+    def index(ph, als):
+        a0, a1 = als[0], als[-1] + 1
+        lo, hi, keys = 512 * ph + 128 * a0, 512 * ph + 128 * a1, ["ix%d%d" % (ph, al) for al in als]
+        for al in als:
+            op("V", tt(T.ca[:, al, :, :, :], T.cn[:, 128 * ph:128 * ph + 128], T.ca[:, al, :, :, :], A.mult), r=["cn%d" % ph], w=["ca%d" % al], x=["ca"], n=128)
+        op("V", tt(T.idx[:, lo:hi], T.ca[:, a0:a1, :, :, :], T.geor[:, ph, a0:a1, :], A.add), r=["ca%d" % al for al in als] + ["geor%d%d" % (ph, al) for al in als], w=keys, x=["ca"], n=hi - lo)
+        op("V", ts(T.idx[:, lo:hi], T.idx[:, lo:hi], 4, A.arith_shift_right, 4095, A.bitwise_and), w=keys, n=hi - lo)
+        op("V", cp(T.off[:, lo:hi], T.idx[:, lo:hi]), r=keys, w=["of%d%d" % (ph, al) for al in als], n=hi - lo)
 
     def ekeys(n, al, hs=(0, 1)):
         return ["e%d%d%d" % (n, al, h) for h in hs]
@@ -441,20 +499,29 @@ def rank_program(g, core, T, topo):
         return E[n][:, al, 512 * hs[0]:512 * hs[-1] + 512]
 
     def gather(n, al, hs, sign=1.0, e="S", minus=None):
-        k, ph = 4 * n + al, n // 2
-        out, src = part(n, al, hs), PW[ph][:].indirect(T.off[:, 64 * k + 32 * hs[0]:64 * k + 32 * hs[-1] + 32])
-        r = ["pw%d" % ph, "of%d" % k]
+        ph, lo = n // 2, 512 * (n // 2) + 128 * al + 64 * (n % 2)
+        out, src = part(n, al, hs), PW[ph][:].indirect(T.off[:, lo + 32 * hs[0]:lo + 32 * hs[-1] + 32])
+        r = ["pw%d" % ph, "of%d%d" % (ph, al)]
         if minus is not None:
             e, call, r = "V", tt(out, src, part(n, minus, hs), A.subtract), r + ekeys(n, minus, hs)
         elif e == "V":
             call = cp(out, src) if sign == 1.0 else ts(out, src, sign, A.mult)
         else:
             call = lambda: S.activation(out, src, ACT.Copy, scale=sign)
-        op(e, call, r=r, w=ekeys(n, al, hs), wo=["turn" + e] if e in CHAIN else [], us=gat(512 * len(hs)))
+        op(e, call, r=r, w=ekeys(n, al, hs), wo=["turn"] if e == "S" else [], us=gat(512 * len(hs)))
+
+    def unit(t, n, al):
+        fused = MODE[t][n][al % 2] == "F" if t == 3 else MODE[t][n][2] == "F"
+        minus = (al + 2 if t == 3 else 2) if fused and al in ((0, 1) if t == 3 else (3,)) else None
+        sign = (-1.0 if al > 1 and not fused else 1.0) if t == 3 else (-1.0 if al % 2 else 1.0)
+        for e in "VS":
+            hs = [h for h in range(2) if ((al, h) in VG[t][n]) == (e == "V")]
+            for some in ([[h] for h in hs] if (n % 2, al) in HALVES[kind(t, n)] else [hs] if hs else []):
+                gather(n, al, some, sign, e, minus)
 
     def added(n, i, into, what):
         dma_add(3 * n + i, part(n, into, (0, 1)), part(n, what, (0, 1)), ekeys(n, what), ekeys(n, into))
-        return [(part(n, into, [h]), "e%d%d%d" % (n, into, h), None) for h in range(2)]
+        return into
 
     nv = [0]
 
@@ -472,66 +539,41 @@ def rank_program(g, core, T, topo):
             if calls:
                 op("P", calls, r=["e%d%d%d" % (n, al, h) for al, _, _ in terms[lo:hi]] + ["ip", "im"], w=["vd%d" % v] if hi == len(terms) else [], wo=["vo%d" % v],
                    us=pe(*[1024 if fl else 512 for _, fl, _ in terms[lo:hi]]), alloc=None if lo else v, use=[v] if lo else [])
-        return (None, "vd%d" % v, v)
+        return v
 
-    def scan(n, al, h, src, low):
-        rp = T.rmin if low else T.rmax
+    def scans(t, n, al, src, low):
+        rp, key = (T.rmin, "rmin") if low else (T.rmax, "rmax")
         o0, o1 = (A.max, A.min) if low else (A.min, A.max)
-        buf, key, v = src
-        op("V", lambda: V.tensor_tensor_scan(SC[n][:, al, 512 * h:512 * h + 512], rp[:], buf if v is None else D[where[v]][:], 0.0, o0, o1),
-           r=[key, "rmin" if low else "rmax"], w=["sc%d%d%d" % (n, al, h)], use=[] if v is None else [v], n=256 if v is None else 512)
-
-    def unit(t, n, al):
-        fused = MODE[t][n][al % 2] == "F" if t == 3 else MODE[t][n][2] == "F"
-        if fused and al in ((0, 1) if t == 3 else (3,)):
-            for h in range(2):
-                gather(n, al, [h], minus=al + 2 if t == 3 else 2)
+        if isinstance(src, list):
+            for h, v in enumerate(src):
+                op("V", lambda h=h, v=v: V.tensor_tensor_scan(SC[n][:, al, 512 * h:512 * h + 512], rp[:, 0:512], D[where[v]][:], 0.0, o0, o1),
+                   r=["vd%d" % v, key], w=["sc%d%d%d" % (n, al, h)], use=[v], n=512)
             return
-        sign = (-1.0 if al > 1 and not fused else 1.0) if t == 3 else (-1.0 if al % 2 else 1.0)
-        for e in "VS":
-            hs = [h for h in range(2) if ((al, h) in VG[t][n]) == (e == "V")]
-            for some in ([[h] for h in hs] if (n % 2, al) in HALVES[t == 3] else [hs] if hs else []):
-                gather(n, al, some, sign, e)
+        for hs in ([[0], [1]] if (n % 2, al) in SPLIT[kind(t, n)] else [[0, 1]]):
+            op("V", lambda hs=hs: V.tensor_tensor_scan(SC[n][:, al, 512 * hs[0]:512 * hs[-1] + 512], rp[:, 0:512 * len(hs)], part(n, src, hs), 0.0, o0, o1),
+               r=ekeys(n, src, hs) + [key], w=["sc%d%d%d" % (n, al, h) for h in hs], n=256 * len(hs))
 
     def chunk(t, n):
         mode = MODE[t][n]
-
-        def held(al):
-            return [(part(n, al, [h]), "e%d%d%d" % (n, al, h), None) for h in range(2)]
-
         if t == 3:
-            low = [True, True, False, False]
             for p, m in enumerate(mode):
-                if m == "F":
-                    src = held(p)
-                else:
-                    src = added(n, p, p, p + 2) if m == "A" else [bank_diff(n, h, [(p, False, 1), (p + 2, False, 1)]) for h in range(2)]
-                for h in range(2):
-                    scan(n, p, h, src[h], True)
-                    scan(n, p + 2, h, src[h], False)
-            return low
+                src = p if m == "F" else added(n, p, p, p + 2) if m == "A" else [bank_diff(n, h, [(p + 2, False, 1), (p, False, 1)]) for h in range(2)]
+                scans(t, n, p, src, True)
+                scans(t, n, p + 2, src, False)
+            return [True, True, False, False]
         flip = t != 1
         low = [True, mode[1] == "P" and mode[2] != "F", mode[2] != "F", mode != "AAA"]
-        src, s1, s3 = {}, -1 if low[1] else 1, 1 if low[3] else -1
+        src, s1, s3 = {2: 3}, -1 if low[1] else 1, 1 if low[3] else -1
         src[3] = [bank_diff(n, h, [(3, False, s3), (2, False, s3), (0, flip, -s3)] if mode[2] == "F" else [(3, False, -s3), (0, flip, -s3)],
                             EARLY[n % 2] * (2 if mode[2] == "F" else 1)) for h in range(2)]
-        if mode[0] == "P":
-            src[0] = [bank_diff(n, h, [(0, False, 1), (1, False, 1)]) for h in range(2)]
-        if mode[1] == "P":
-            src[1] = [bank_diff(n, h, [(1, False, s1), (2, False, s1)]) for h in range(2)]
-        if mode[2] == "P":
-            src[2] = [bank_diff(n, h, [(2, False, 1), (3, False, 1)]) for h in range(2)]
-        if mode[2] == "F":
-            src[2] = held(3)
-        if mode[2] == "A":
-            src[2] = added(n, 2, 3, 2)
-        if mode[0] == "A":
-            src[0] = added(n, 0, 0, 1)
-        if mode[1] == "A":
-            src[1] = added(n, 1, 2, 1)
+        for k, s in ((0, 1), (1, s1), (2, 1)):
+            if mode[k] == "P":
+                src[k] = [bank_diff(n, h, [(k, False, s), (k + 1, False, s)]) for h in range(2)]
+        for k, into, what in ((2, 3, 2), (0, 0, 1), (1, 2, 1)):
+            if mode[k] == "A":
+                src[k] = added(n, k, into, what)
         for al in (2, 3, 0, 1):
-            for h in range(2):
-                scan(n, al, h, src[al][h], low[al])
+            scans(t, n, al, src[al], low[al])
         return low
 
     def post(t, n, low):
@@ -539,9 +581,9 @@ def rank_program(g, core, T, topo):
         gp, bk, grp = GP[c], "gp%d" % c, "grp%d" % c
         gap, cnt, flg = gp[:, 0:4, :, :], gp[:, 4:8, :, :], T.flg[:, n, :]
         if t == 3:
-            op("P", [mm(gp[:, 8:12, :, slot(t, k % 4, k // 4)], T.selk[:], T.crow[:, ph, 32 * k + 16 * c:32 * k + 16 * c + 16], True, True) for k in range(8)],
-               r=["crow%d" % ph, "selk"], w=["rows%d" % c], wo=[grp], x=[bk], us=pe(*[64] * 8))
-            op(ON["rows"], cp(T.crx[:, n, :], gp[:, 8:12, :, :], ON["rows"]), r=["rows%d" % c], w=["crx%d" % n], x=[bk], n=128)
+            op("P", [mm(gp[:, 8:12, :, slot(t, k % 4, k // 4)], T.casel[:, 0, :], T.crow[:, ph, 32 * k + 16 * c:32 * k + 16 * c + 16], True, True) for k in range(8)],
+               r=["crow%d" % ph, "casel"], w=["rows%d" % c], wo=[grp], x=[bk], us=pe(*[64] * 8))
+            op("S", cp(T.crx[:, n, :], gp[:, 8:12, :, :], "S"), r=["rows%d" % c], w=["crx%d" % n], x=[bk], n=128)
         calls = [mm(gap, T.zero[:], T.ones[:], True, False)]
 
         def own(b, a0, a1):
@@ -560,15 +602,11 @@ def rank_program(g, core, T, topo):
             sets = [[0, 2], [1, 3]]
         else:
             sets = [[0, 3]] + ([[1, 2]] if low[1] == low[2] else [[1], [2]])
-        left = [4 * len(sets)]
-
-        def last():
-            left[0] -= 1
-            return left[0] == 0
+        last = countdown(4 * len(sets))
         for als in sets:
             pick = slice(als[0], als[-1] + 1, max(1, als[-1] - als[0]))
             out = gp[:, 0:4, :, 2 * als[0]:2 * als[0] + 2] if t == 3 else gp[:, pick, :, :]
-            calls = [lambda out=out, pick=pick, j=j: P.matmul(out, (T.ip if low[pick.start] else T.im)[:], SC[n][:, pick, 256 * j + 7:256 * j + 256:8], False, last()) for j in range(4)]
+            calls = [lambda out=out, rhs=SC[n][:, pick, lo + 7:lo + 256:8], sign=(T.ip if low[als[0]] else T.im)[:]: P.matmul(out, sign, rhs, False, last()) for lo in range(0, 1024, 256)]
             op("P", calls, r=["ip", "im"] + ["sc%d%d%d" % (n, al, h) for al in als for h in range(2)], ro=[grp] + ["gap%d%d" % (c, al) for al in als],
                w=["sum%d%d" % (c, al) for al in als], x=[bk], us=pe(64, 64, 64, 64))
         GK = ["gap%d%d" % (c, al) for al in range(4)] + ["sum%d%d" % (c, al) for al in range(4)]
@@ -581,7 +619,7 @@ def rank_program(g, core, T, topo):
             op("V", tt(T.ycb[:, n, :], cnt, T.crx[:, n, :], A.min), r=["cnt%d" % c, "crx%d" % n], w=["yc%d" % n], x=[bk], n=128)
             dma("Y", [(T.yc[4 * ph:4 * ph + 4, 256 * c:256 * c + 256], T.ycb[0:128:16, n, :])], r=["yc%d" % n])
             if c:
-                op(ON["yg"], cp(T.ygb[:, ph, :], T.mb[:, 8:16, :, :], ON["yg"]), r=["mby0", "mby1"], w=["yg%d" % ph], x=["mb"], n=256)
+                op("S", cp(T.ygb[:, ph, :], T.mb[:, 8:16, :, :], "S"), r=["mby0", "mby1"], w=["yg%d" % ph], x=["mb"], n=256)
                 for e, k in (("Y", 0), ("S" if ph else "Y", 1)):
                     dma(e, [(T.yg[64 * ph:64 * ph + 64, 256 * k:256 * k + 256], T.ygb[64 * k:64 * k + 64, ph, :])], r=["yg%d" % ph])
             return
@@ -591,12 +629,8 @@ def rank_program(g, core, T, topo):
             call = ts(flg, gap, 0.0, A.is_gt)
         op(ON["flag"], call, r=GK, w=["flg%d" % n], x=[bk], n=128)
         dm = T.dm[:, 4 * t + n, :]
-        if ON["dead"] == "S":
-            op("P", [mm(cnt, T.ip[:], T.thr[:], True, False), mm(cnt, flg, T.bm[:], False, True)], r=["flg%d" % n, "bm", "thr", "ip"], w=["cnt%d" % c], wo=[grp], x=[bk], us=pe(128, 128))
-            op("S", lambda: S.activation(dm, cnt, ACT.Relu), r=["cnt%d" % c], w=["dm%d%d" % (t, n)], x=[bk], n=128)
-        else:
-            op("P", mm(cnt, flg, T.bm[:], True, True), r=["flg%d" % n, "bm"], w=["cnt%d" % c], wo=[grp], x=[bk], us=pe(128))
-            op("V", tt(dm, cnt, T.thr[:], A.is_ge), r=["cnt%d" % c, "thr"], w=["dm%d%d" % (t, n)], x=[bk], n=128)
+        op("P", mm(cnt, flg, T.bm[:], True, True), r=["flg%d" % n, "bm"], w=["cnt%d" % c], wo=[grp], x=[bk], us=pe(128))
+        op("V", tt(dm, cnt, T.thr[:], A.is_ge), r=["cnt%d" % c, "thr"], w=["dm%d%d" % (t, n)], x=[bk], n=128)
         out = T.mb[:, 0, :, c:16:2]
         calls = [mm(out, T.ip[:], T.kk[:, c, :], True, False)] + [mm(out, T.dm[:, 4 * s + n, :], T.ones[:, 0:16], False, False) for s in range(t)]
         calls.append(mm(out, dm, T.rt[:, t, :], False, True))
@@ -604,63 +638,50 @@ def rank_program(g, core, T, topo):
         if c == 1:
             op("V", tt(T.pos[:, ph, :, :], T.mb[:, 0, :, :], T.pos[:, ph, :, :], A.max), r=["mbp0", "mbp1", "pos"], w=["pos%d" % ph], x=["mb"])
 
-    for name, v in (("ip", 1.0), ("im", -1.0), ("ip16", 1.0), ("im16", -1.0)):
-        op("V", ts(T[name][:], T.prow[:], fcol(0), A.is_equal, v, A.mult), r=["prow", "cf0"], w=[name], n=128)
-    op("V", ms(T.rmin[:], -BIG), w=["rmin"], n=256)
-    op("V", ms(T.rmax[:], BIG), w=["rmax"], n=256)
-    op("V", ms(T.rmin[:, 0:512:8], BIG), w=["rmin"])
-    op("V", ms(T.rmax[:, 0:512:8], -BIG), w=["rmax"])
-    sg = -1.0 if ON["dead"] == "S" else 1.0
-    op("V", ts(T.thr[:], T.qrow[:], fcol(5), A.not_equal, 64.0 * sg, A.mult), r=["qrow", "cf5"], w=["thr"])
-    op("V", ts(T.thr[:], T.thr[:], -15.0 if sg < 0 else 15.5, A.add), w=["thr"])
-    op("V", ms(T.kk[:, 0, :], -56.0), w=["kk"])
-    op("V", ms(T.kk[:, 1, :], 392.0), w=["kk"])
-    for t, (m, k) in enumerate(((1.0, 4.0), (2.0, 1.0), (3.0, 4.0))):
+    for name, v in (("ip", 1.0), ("ip16", 1.0), ("im16", -1.0)):
+        op("V", ts(T[name][:], T.prow[:], fcol(0), A.is_equal, v, A.mult), r=["prow", "cf"], w=[name])
+    op("S", lin(T.im[:], T.ip[:], -1.0), r=["ip"], w=["im"], n=128)
+    op("V", ms(T.rmin[:], -BIG), w=["rmin"], n=512)
+    op("V", ms(T.rmin[:, 0:1024:8], BIG), w=["rmin"])
+    op("S", lin(T.rmax[:], T.rmin[:], -1.0), r=["rmin"], w=["rmax"], n=1024)
+    op("V", ts(T.thr[:], T.qrow[:], fcol(4), A.not_equal, 64.0, A.mult), r=["qrow", "cf"], w=["thr"])
+    op("S", lin(T.thr[:], T.thr[:], 1.0, 15.5), w=["thr"], n=128)
+    op("S", lin(fcol(9), fcol(5), 4.0), r=["cf"], w=["cf9"])
+    for t, (m, b) in enumerate(((1.0, 9), (2.0, 5), (3.0, 9))):
         a, key = fcol(10 + t), "cf%d" % (10 + t)
-        op("V", ts(fcol(13 + t), fcol(6), k, A.mult), r=["cf6"], w=["cf%d" % (13 + t)])
-        op("V", ts(icol(10 + t) if t == 2 else a, fcol(3), m, A.mult, fcol(13 + t), A.add), r=["cf3", "cf%d" % (13 + t)], w=[key])
+        op("S", lin(a, fcol(3), m, fcol(b)), r=["cf", "cf9"], w=[key])
         if t == 2:
-            op("V", ts(icol(12), icol(12), 7, A.bitwise_and), r=[key], w=[key])
-            op("V", cp(a, icol(12)), r=[key], w=[key])
-        op("V", ts(T.rt[:, t, :], T.arow[:], a, A.is_equal, 64.0, A.mult), r=["arow", key], w=["rt%d" % t])
-        op("V", ts(T.ru[:, t, :], T.arow[:], a, A.is_gt), r=["arow", key], w=["ru%d" % t])
-        op("V", tt(T.rt[:, t, :], T.rt[:, t, :], T.ru[:, t, :], A.add), r=["ru%d" % t], w=["rt%d" % t])
+            op("V", ts(fcol(13), a, 7.5, A.is_gt, -8.0, A.mult), r=[key], w=["cf13"])
+            op("S", lin(a, a, 1.0, fcol(13)), r=["cf13"], w=[key])
+        op("V", [ts(T.rt[:, t, :], T.arow[:], a, A.is_equal, 64.0, A.mult), ts(T.ru[:, t, :], T.arow[:], a, A.is_gt)], r=["arow", key], w=["rt%d" % t, "ru%d" % t], n=128)
+    op("V", tt(T.rt[:], T.rt[:], T.ru[:], A.add), r=["ru0", "ru1", "ru2"], w=["rt0", "rt1", "rt2"], n=96)
     for h in range(2):
-        op("V", ts(fcol(16 + h), fcol(4), 16.0 * h - .5, A.is_gt, -64.0, A.mult), r=["cf4"], w=["cf%d" % (16 + h)])
-        op("V", ts(fcol(18 + h), fcol(4), 16.0 * h + 1.5, A.is_gt, 64.0, A.mult), r=["cf4"], w=["cf%d" % (18 + h)])
-        op("V", ts(fcol(20 + h), fcol(3), 8.0, A.mult, fcol(16 + h), A.add), r=["cf3", "cf%d" % (16 + h)], w=["cf%d" % (20 + h)])
-        op("V", ts(fcol(20 + h), fcol(20 + h), 64.0, A.add, fcol(18 + h), A.add), r=["cf%d" % (18 + h)], w=["cf%d" % (20 + h)])
-        op("V", ts(T.tg[:, 8 * h:8 * h + 8], T.qrow[:, 0:8], fcol(20 + h), A.add), r=["qrow", "cf%d" % (20 + h)], w=["tg%d" % h])
+        op("V", ts(T.xsel[:, h, :], T.krow[:], 2.0 * h, A.add, fcol(7), A.is_equal), r=["krow", "cf7"], w=["xsel%d" % h])
         for u in range(8):
-            k = 8 * h + u
-            op("V", ts(T.csel[:, k, :], T.krow[:], T.tg[:, k:k + 1], A.is_equal), r=["krow", "tg%d" % h], w=["csel%d" % k])
-    op("V", [ts(T.back[:, h, :], T.brow[:], 16.0 * h, A.add, fcol(0), A.is_equal) for h in range(2)], r=["brow", "cf0"], w=["back"], n=128)
-    op("V", ts(T.bn[:], T.bm[:], -4096.0, A.mult), r=["bm"], w=["bn"])
-    op("V", ts(fcol(22), fcol(0), 0.0, A.is_equal, 65536.0, A.mult), r=["cf0"], w=["cf22"])
-    op("V", ts(fcol(23), fcol(0), 1.0, A.is_equal), r=["cf0"], w=["cf23"])
-    op("V", ts(T.kc[:], T.ones[:], fcol(22), A.mult, fcol(23), A.subtract), r=["ones", "cf22", "cf23"], w=["kc"], n=128)
+            select(T.csel[:, 8 * h + u, :], T.xsel[:, h, :], [[0, 16], [1, 8]], -u, 0, ["xsel%d" % h, "sent1"], ["csel%d" % (8 * h + u)])
+    op("V", [ts(T.back[:, h, :], T.brow[:], 16.0 * h, A.add, fcol(0), A.is_equal) for h in range(2)], r=["brow", "cf"], w=["back"], n=128)
+    op("S", lin(T.bn[:], T.bm[:], -4096.0), r=["bm"], w=["bn"], n=128)
+    op("V", ts(fcol(14), T.ip[:, 0:1], 65536.0, A.mult, T.ip[:, 1:2], A.subtract), r=["ip"], w=["cf14"])
+    op("S", lin(T.kc[:], T.ones[:], fcol(14)), r=["ones", "cf14"], w=["kc"], n=128)
 
+    sends(0, 0)
+    sends(0, 1)
+    dma("Y", table(T.pw1, T.pe, 1, range(4)), w=["pw1"], r=["sent0", "sent1"], wo=["qY"], load=TAB, pre=lambda: g.sync.wait_ge(T.sem.loc0, nsig[0] + nsig[1]))
     for t in range(4):
-        if t == 0:
-            sends(0, 0)
-            sends(0, 1)
-            dma("Y", table(T.pw1, T.pe, 1, range(4)), w=["pw1"], r=["sent0", "sent1"], wo=["qY"], load=TAB, pre=lambda: g.sync.wait_ge(T.sem.loc0, nsig[0] + nsig[1]))
         for ph in range(2):
-            now[0] = 2 * ph
             if t:
                 sends(t, ph)
             codes(t, ph)
             neighbours(t, ph)
-            for c, als in LISTS[t == 3]:
-                index(2 * ph + c, [als])
-            for i, (c, al) in enumerate(UNITS[t == 3]):
+            for als in LISTS[kind(t, 2 * ph)]:
+                index(ph, als)
+            for i, (c, al) in enumerate(UNITS[kind(t, 2 * ph)]):
                 unit(t, 2 * ph + c, al)
                 for q in range(8):
                     if t == 0 and PACE[q] == 8 * ph + i:
                         dma("Y", table(SW[q // 4], T.se, q // 4, [q % 4]), r=ekeys(2 * ph + c, al, [0]) if 8 * ph + i else [], w=["sw%d" % q], wo=["qY"], load=TAB / 2)
-            selves(t, ph)
+            selves(ph)
             for n in (2 * ph, 2 * ph + 1):
-                now[0] = n
                 post(t, n, chunk(t, n))
 
     if not ORDER:

@@ -3,23 +3,23 @@ from concourse.mybir import AluOpType, ActivationFunctionType
 
 BF, F16, F32, I32, U16 = "bfloat16", "float16", "float32", "int32", "uint16"
 BIG = 1024.0
-MODE = [["PPF", "PPF", "PAF", "AAF"], ["AAP", "PAF", "AAP", "PAF"], ["AAP", "PAF", "AAP", "PAF"], ["AA", "AA", "AF", "AF"]]
+MODE = [["PAF", "PPF", "AAP", "PAF"], ["AAP", "PAF", "AAP", "PAF"], ["AAP", "PAF", "AAP", "PAF"], ["AA", "AA", "FF", "AP"]]
 VG = [[[], [], [], []], [[], [], [], []], [[], [], [], []], [[], [], [], []]]
-UNITS = [[(0, 2), (1, 2), (0, 3), (1, 3), (0, 0), (0, 1), (1, 1), (1, 0)], [(0, 2), (0, 0), (0, 3), (0, 1), (1, 2), (1, 0), (1, 3), (1, 1)],
-         [(0, 2), (0, 0), (0, 3), (0, 1), (1, 2), (1, 0), (1, 3), (1, 1)]]
-HALVES = [[(1, 0), (0, 3), (1, 3), (0, 0)], [], [(1, 1), (0, 1)]]
+UNITS = [[(0, 2), (1, 2), (0, 3), (1, 3), (0, 1), (0, 0), (1, 1), (1, 0)], [(0, 2), (1, 0), (0, 0), (0, 1), (1, 2), (0, 3), (1, 3), (1, 1)],
+         [(0, 2), (0, 0), (0, 3), (0, 1), (1, 3), (1, 2), (1, 0), (1, 1)]]
+HALVES = [[(1, 0), (0, 3), (1, 3), (0, 0), (1, 1)], [], [(1, 1), (0, 1)]]
 SPLIT = [[], [], [(1, 0), (1, 1), (1, 2), (1, 3)]]
 LISTS = [[[2], [3], [1], [0]], [[2], [0], [3], [1]], [[2], [0], [3], [1]]]
 EARLY = [1, 1]
 PACE = [0, 0, 0, 1, 4, 7, 8, 9]
 ON = {"flag": "V", "cn": "V", "mine": "V"}
-WAKE, EPS, IDLE, ADDUS, FLIGHT = 0.07, 0.3, 8.0, 2.0, 1.9
-START, LAND, TAB, SEND, ISSUE, CALL = 1.4, 0.5, 3.75, 1.5, 0.1, 0.025
-PASSES, MIX = 4, 0.8
-TRIES, STRETCH, NOISE, SEED = 600, 40, 2.0, 1
-PLANS = [(.9e-3, 1.6, .75e-3, .9), (.95e-3, 1.5, .72e-3, .9), (1.0e-3, 1.5, .75e-3, .9), (1.0e-3, 1.75, .8e-3, .85)]
-SPEEDS = [(.83e-3, 1.56, .714e-3, .85), (.91e-3, 1.2, .714e-3, .9), (.95e-3, 2.0, .714e-3, .9), (1.04e-3, 1.56, .714e-3, .8), (1.04e-3, 1.3, .89e-3, .9),
-          (1.16e-3, 1.15, .714e-3, .9), (1.16e-3, 1.8, 1.0e-3, .9), (1.2e-3, 2.0, .714e-3, .9)]
+WAKE, EPS, IDLE, ADDUS, FLIGHT = 0.07, 0.3, 16.0, 1.6, 1.65
+START, LAND, TAB, SEND, ISSUE, CALL = 1.15, 0.5, 3.0, 1.15, 0.15, 0.025
+PASSES, MIX = 3, 0.8
+TRIES, STRETCH, NOISE, SEED = 1500, 25, 1.0, 1
+PLANS = [(.9e-3, 1.6, .75e-3, 1.05), (.95e-3, 1.5, .72e-3, 1.1), (1.0e-3, 1.5, .75e-3, 1.05), (1.0e-3, 1.75, .8e-3, 1.0)]
+SPEEDS = [(.83e-3, 1.56, .714e-3, 1.0), (.91e-3, 1.2, .714e-3, 1.1), (.95e-3, 2.0, .714e-3, 1.0), (1.04e-3, 1.56, .714e-3, 1.2), (1.04e-3, 1.3, .89e-3, 1.0),
+          (1.16e-3, 1.15, .714e-3, 1.0), (1.16e-3, 1.8, 1.0e-3, 1.1), (1.2e-3, 2.0, .714e-3, 1.0)]
 ORDER, LOG = [], []
 ND, NDMA = 4, 30
 SCRATCH = {
@@ -382,11 +382,11 @@ def rank_program(g, core, T, topo):
     def fcol(k):
         return T.cf[:, k:k + 1]
 
-    def iota(name, pattern, base=0):
+    def iota(name, pattern, base=0, r=()):
         n = 1
         for _, m in pattern:
             n *= m
-        op("G", lambda: g.iota(T[name][:], pattern, base, 0, allow_small_or_imprecise_dtypes=True), w=[name], us=(.13, 2 * n, 0, 0))
+        op("G", lambda: g.iota(T[name][:], pattern, base, 0, allow_small_or_imprecise_dtypes=True), ro=r, w=[name], us=(.13, 2 * n, 0, 0))
 
     def select(out, in_, pattern, base, cm, r, w):
         op("G", lambda: g.affine_select(out, in_, pattern, A.is_equal, 0.0, base, cm), r=r, w=w, us=(.17, 256, 0, 0))
@@ -395,12 +395,7 @@ def rank_program(g, core, T, topo):
     iota("qrow", [[0, 8], [1, 16]])
     iota("grow", [[1, 8], [0, 16]])
     iota("pos", [[0, 4], [1, 8], [448, 2]])
-    iota("arow", [[0, 2], [1, 8]])
     iota("hrow", [[2, 8], [1, 2], [0, 8]])
-    iota("prow", [[1, 128]])
-    iota("krow", [[4, 4], [0, 32]])
-    iota("brow", [[32, 4], [1, 16]])
-    iota("kk", [[448, 2], [0, 16]], -56)
     op("V", ms(T.one32[:], 1.0), w=["one32"], n=128)
     op("S", cp(T.ones[:], T.one32[:], "S"), r=["one32"], w=["ones"], n=128)
     op("S", lin(T.zero[:], T.one32[:], 0.0), r=["one32"], w=["zero"], n=128)
@@ -557,7 +552,10 @@ def rank_program(g, core, T, topo):
         mode = MODE[t][n]
         if t == 3:
             for p, m in enumerate(mode):
-                src = p if m == "F" else added(n, p, p, p + 2) if m == "A" else [bank_diff(n, h, [(p + 2, False, 1), (p, False, 1)]) for h in range(2)]
+                src = added(n, p, p, p + 2) if m == "A" else p
+                for h in (range(2) if m == "P" else ()):
+                    v = bank_diff(n, h, [(p + 2, False, 1), (p, False, 1)])
+                    op("S", lambda h=h, v=v, p=p: S.activation(part(n, p, [h]), D[where[v]][:], ACT.Copy), r=["vd%d" % v], w=ekeys(n, p, [h]), use=[v], n=512)
                 scans(t, n, p, src, True)
                 scans(t, n, p + 2, src, False)
             return [True, True, False, False]
@@ -581,9 +579,10 @@ def rank_program(g, core, T, topo):
         gp, bk, grp = GP[c], "gp%d" % c, "grp%d" % c
         gap, cnt, flg = gp[:, 0:4, :, :], gp[:, 4:8, :, :], T.flg[:, n, :]
         if t == 3:
-            op("P", [mm(gp[:, 8:12, :, slot(t, k % 4, k // 4)], T.casel[:, 0, :], T.crow[:, ph, 32 * k + 16 * c:32 * k + 16 * c + 16], True, True) for k in range(8)],
-               r=["crow%d" % ph, "casel"], w=["rows%d" % c], wo=[grp], x=[bk], us=pe(*[64] * 8))
-            op("S", cp(T.crx[:, n, :], gp[:, 8:12, :, :], "S"), r=["rows%d" % c], w=["crx%d" % n], x=[bk], n=128)
+            lo = 8 + 4 * ph
+            op("P", [mm(gp[:, lo:lo + 4, :, slot(t, k % 4, k // 4)], T.casel[:, 0, :], T.crow[:, ph, 32 * k + 16 * c:32 * k + 16 * c + 16], True, True) for k in range(8)],
+               r=["crow%d" % ph, "casel"], w=["rows%d" % n], wo=[grp], x=[bk], us=pe(*[64] * 8))
+            op("S", cp(T.crx[:, n, :], gp[:, lo:lo + 4, :, :], "S"), r=["rows%d" % n], w=["crx%d" % n], x=[bk], n=128)
         calls = [mm(gap, T.zero[:], T.ones[:], True, False)]
 
         def own(b, a0, a1):
@@ -638,6 +637,8 @@ def rank_program(g, core, T, topo):
         if c == 1:
             op("V", tt(T.pos[:, ph, :, :], T.mb[:, 0, :, :], T.pos[:, ph, :, :], A.max), r=["mbp0", "mbp1", "pos"], w=["pos%d" % ph], x=["mb"])
 
+    for name, pattern, base in (("prow", [[1, 128]], 0), ("arow", [[0, 2], [1, 8]], 0), ("krow", [[4, 4], [0, 32]], 0), ("kk", [[448, 2], [0, 16]], -56), ("brow", [[32, 4], [1, 16]], 0)):
+        iota(name, pattern, base, ["sent0"])
     for name, v in (("ip", 1.0), ("ip16", 1.0), ("im16", -1.0)):
         op("V", ts(T[name][:], T.prow[:], fcol(0), A.is_equal, v, A.mult), r=["prow", "cf"], w=[name])
     op("S", lin(T.im[:], T.ip[:], -1.0), r=["ip"], w=["im"], n=128)

from concourse.bass import DstId, RemoteDMATransfer
from concourse.mybir import AluOpType, ActivationFunctionType

BF, F16, F32, I32, U16 = "bfloat16", "float16", "float32", "int32", "uint16"
BIG = 1024.0
MODE = [["PAF", "PPF", "AAP", "PAF"], ["AAP", "PAF", "AAP", "PAF"], ["AAP", "PAF", "AAP", "PAF"], ["AA", "AA", "FF", "AP"]]
VG = [[[], [], [], []], [[], [], [], []], [[], [], [], []], [[], [], [], []]]
UNITS = [[(0, 2), (1, 2), (0, 3), (1, 3), (0, 1), (0, 0), (1, 1), (1, 0)], [(0, 2), (1, 0), (0, 0), (0, 1), (1, 2), (0, 3), (1, 3), (1, 1)],
         [(0, 2), (0, 0), (0, 3), (0, 1), (1, 3), (1, 2), (1, 0), (1, 1)]]
HALVES = [[(1, 0), (0, 3), (1, 3), (0, 0), (1, 1)], [], [(1, 1), (0, 1)]]
SPLIT = [[], [], [(1, 0), (1, 1), (1, 2), (1, 3)]]
LISTS = [[[2], [3], [1], [0]], [[2], [0], [3], [1]], [[2], [0], [3], [1]]]
EARLY = [1, 1]
PACE = [0, 0, 0, 1, 4, 7, 8, 9]
ON = {"flag": "V", "cn": "V", "mine": "V"}
WAKE, EPS, IDLE, ADDUS, FLIGHT = 0.07, 0.3, 16.0, 1.6, 1.65
START, LAND, TAB, SEND, ISSUE, CALL = 1.15, 0.5, 3.0, 1.15, 0.15, 0.025
PASSES, MIX = 3, 0.8
TRIES, STRETCH, NOISE, SEED = 1500, 25, 1.0, 1
PLANS = [(.9e-3, 1.6, .75e-3, 1.05), (.95e-3, 1.5, .72e-3, 1.1), (1.0e-3, 1.5, .75e-3, 1.05), (1.0e-3, 1.75, .8e-3, 1.0)]
SPEEDS = [(.83e-3, 1.56, .714e-3, 1.0), (.91e-3, 1.2, .714e-3, 1.1), (.95e-3, 2.0, .714e-3, 1.0), (1.04e-3, 1.56, .714e-3, 1.2), (1.04e-3, 1.3, .89e-3, 1.0),
          (1.16e-3, 1.15, .714e-3, 1.0), (1.16e-3, 1.8, 1.0e-3, 1.1), (1.2e-3, 2.0, .714e-3, 1.0)]
ORDER, LOG = [], []
ND, NDMA = 4, 30
SCRATCH = {
    "pw0": ("sbuf", [128, 4096], BF), "pw1": ("sbuf", [128, 4096], BF), "sw0": ("sbuf", [128, 4096], I32), "sw1": ("sbuf", [128, 4096], I32),
    "cq0": ("sbuf", [128, 896], I32), "cq1": ("sbuf", [128, 896], I32), "candl": ("sbuf", [128, 4, 28], I32), "tin": ("sbuf", [128, 4, 32], F32),
    "ngi": ("sbuf", [128, 2, 16], I32), "ngf": ("sbuf", [128, 2, 16], F32), "nbu": ("sbuf", [128, 16], U16), "gl": ("sbuf", [128, 2, 8], F32),
    "gm": ("sbuf", [128, 2, 8, 16], F32), "geor": ("sbuf", [128, 2, 4, 128], F32),
    "ones": ("sbuf", [128, 128], BF), "zero": ("sbuf", [128, 128], BF), "ip": ("sbuf", [128, 128], BF), "im": ("sbuf", [128, 128], BF),
    "ip16": ("sbuf", [128, 128], F16), "im16": ("sbuf", [128, 128], F16), "one32": ("sbuf", [128, 128], F32),
    "bm": ("sbuf", [128, 128], BF), "bf32": ("sbuf", [128, 128], F32), "bn": ("sbuf", [128, 128], BF), "kc": ("sbuf", [128, 128], BF),
    "casel": ("sbuf", [128, 2, 128], F16), "xsel": ("sbuf", [128, 2, 128], F16), "csel": ("sbuf", [128, 16, 128], F16),
    "lnb": ("sbuf", [128, 4, 128], F32), "m16": ("sbuf", [128, 16], F32), "thr": ("sbuf", [128, 128], BF), "back": ("sbuf", [128, 2, 64], F16),
    "prow": ("sbuf", [128, 128], BF), "qrow": ("sbuf", [128, 128], BF), "grow": ("sbuf", [128, 128], BF), "hrow": ("sbuf", [128, 128], BF),
    "krow": ("sbuf", [128, 128], BF), "arow": ("sbuf", [128, 16], BF), "brow": ("sbuf", [128, 64], BF),
    "rt": ("sbuf", [128, 3, 16], BF), "ru": ("sbuf", [128, 3, 16], BF), "kk": ("sbuf", [128, 2, 16], BF),
    "rmin": ("sbuf", [128, 1024], BF), "rmax": ("sbuf", [128, 1024], BF),
    "ci": ("sbuf", [128, 8], I32), "cf": ("sbuf", [128, 24], F32),
    "pos": ("sbuf", [128, 2, 16, 2], F32), "offc": ("sbuf", [128, 32], U16), "offs": ("sbuf", [128, 32], U16), "tl": ("sbuf", [128, 2, 2, 32], F32),
    "crow": ("sbuf", [128, 2, 256], F16), "own": ("sbuf", [128, 2, 256], F16), "crx": ("sbuf", [128, 4, 128], F32),
    "cn": ("sbuf", [128, 256], F32), "idx": ("sbuf", [128, 1024], I32), "off": ("sbuf", [128, 1024], U16),
    "flg": ("sbuf", [128, 4, 128], BF), "dm": ("sbuf", [128, 12, 128], BF),
    "gh": ("sbuf", [128, 4, 128], F16), "ygb": ("sbuf", [128, 2, 256], F32), "ycb": ("sbuf", [128, 4, 128], F32),
    "ca": ("psum", [128, 4, 2, 4, 16], F32), "gp0": ("psum", [128, 16, 4, 8], F32), "gp1": ("psum", [128, 16, 4, 8], F32), "mb": ("psum", [128, 16, 2, 16], F32),
}
for _k in range(ND):
    SCRATCH["d%d" % _k] = ("psum", [128, 512], F32)
for _n in range(4):
    SCRATCH["e%d" % _n] = ("sbuf", [128, 4, 1024], BF)
    SCRATCH["sc%d" % _n] = ("sbuf", [128, 4, 1024], BF)
for _n in range(8):
    SCRATCH["w%d" % _n] = ("sbuf", [128, 256], F32)
SEMAPHORES = ["loc0", "loc", "sV", "sS", "sP", "sG"] + ["arr%d" % i for i in range(8)] + ["dma%d" % i for i in range(NDMA)] + ["add%d" % i for i in range(12)]


def kind(t, n):
    return 1 + n // 2 if t == 3 else 0


def lane(t, b):
    return (b, 2) if t % 2 else (4 * b, t + 1)


def slot(t, al, b):
    return (lane(t, b)[0] + al * lane(t, b)[1]) % 8


def order(prog):
    n = len(prog)
    wr, rd, users = {}, {}, {}
    succs, left = [[] for _ in range(n)], []
    for i, p in enumerate(prog):
        s = {}
        for k in p["r"] + p["w"]:
            if k in wr:
                s[wr[k]] = s.get(wr[k], False) or k not in p["soft"]
        for k in p["w"]:
            for q in rd.get(k, ()):
                s[q] = s.get(q, False) or (k not in p["soft"] and (prog[q]["e"] != p["e"] or prog[q]["load"] > 0))
        s.pop(i, None)
        for k in p["r"]:
            rd.setdefault(k, []).append(i)
        for k in p["w"]:
            wr[k] = i
            rd[k] = []
        left.append(len(s))
        for q, hard in s.items():
            succs[q].append((i, hard))
        for v in p["use"]:
            users[v] = users.get(v, 0) + 1

    def way(i, tail):
        p = prog[i]
        wait = p["lat"] + (p["dma"] + START + LAND if p["dma"] else 0.0) + WAKE
        return p["us"] + max([tail[q] + (wait if hard else 0.0) for q, hard in succs[i]] + [wait])

    def speeds(cyc, gat, pec, dma):
        for p in prog:
            c = p["cost"]
            p["us"] = c[0] + (c[1] + c[2] * gat) * cyc + c[3] * pec
            p["dma"], p["lat"] = p["load"] * dma, p["far"] * dma

    found = []
    for plan in PLANS:
        speeds(*plan)
        rank = [0.0] * n
        for i in range(n - 1, -1, -1):
            rank[i] = way(i, rank)
        for _ in range(PASSES):
            seq, where = place(prog, succs, list(left), dict(users), rank)
            found.append((seq, where, plan, list(rank)))
            tail, after = [0.0] * n, {}
            for i in reversed(seq):
                p = prog[i]
                own = way(i, tail)
                tail[i] = max(own, p["us"] + after.get(p["e"], 0.0), p["dma"] + after.get("dma", 0.0) if p["dma"] else 0.0)
                after[p["e"]] = tail[i]
                if p["dma"]:
                    after["dma"] = tail[i]
                rank[i] = MIX * rank[i] + (1 - MIX) * own
    costs, least = [], []
    for s in SPEEDS:
        speeds(*s)
        costs.append([dict(p) for p in prog])
        least.append(min(replay(prog, succs, f[0], f[1]) for f in found))

    def worth(seq, where):
        row = [replay(c, succs, seq, where) / b for c, b in zip(costs, least)]
        return sum(row) / len(row) + max(row)
    seq, where, plan, rank = min(found, key=lambda f: worth(f[0], f[1]))
    speeds(*plan)
    now, x = worth(seq, where), SEED
    for _ in range(TRIES):
        x = (x * 1103515245 + 12345) % 2 ** 31
        lo = x % n
        trial = list(rank)
        for i in seq[lo:lo + STRETCH]:
            x = (x * 1103515245 + 12345) % 2 ** 31
            trial[i] += NOISE * (x / 2.0 ** 30 - 1.0)
        s, w = place(prog, succs, list(left), dict(users), trial)
        v = worth(s, w)
        if v < now:
            now, seq, where, rank = v, s, w, trial
    LOG.append(now)
    return seq, where


def replay(prog, succs, seq, where):
    at = [0.0] * len(prog)
    qfree, bank, engines, total = {}, {}, 0.0, 0.0
    for i in seq:
        p = prog[i]
        e = p["e"]
        t = max(at[i], qfree.get(e, 0.0))
        xs = p["x"] + [where[v] for v in p["use"]] + ([] if p["alloc"] is None else [where[p["alloc"]]])
        for b in xs:
            if b in bank and bank[b][0] != e:
                t = max(t, bank[b][1] + WAKE)
        end = qfree[e] = t + p["us"]
        if p["dma"]:
            engines = max(t + START + (p["us"] if p["lat"] else 0.0), engines) + p["dma"]
            end = engines + (p["lat"] or LAND)
        for b in xs:
            bank[b] = (e, end)
        for q, hard in succs[i]:
            at[q] = max(at[q], end + WAKE if hard else qfree[e])
        total = max(total, end)
    return total


def place(prog, succs, left, users, rank):
    n = len(prog)
    at = [0.0] * n
    ready = [i for i in range(n) if not left[i]]
    qfree, bank, engines = {}, {}, 0.0
    free = {k: 0.0 for k in range(ND)}
    where, seq = {}, []
    while ready:
        cand = []
        for i in ready:
            p = prog[i]
            t = max(at[i], qfree.get(p["e"], 0.0))
            if p["alloc"] is not None:
                if not free:
                    continue
                t = max(t, min(free.values()) + WAKE)
            for b in p["x"]:
                if b in bank and bank[b][0] != p["e"]:
                    t = max(t, bank[b][1] + WAKE)
            cand.append((t, i))
        best, i = min((t + prog[i]["us"], i) for t, i in cand)
        e = prog[i]["e"]
        t, i = max([c for c in cand if prog[c[1]]["e"] == e and c[0] <= best + EPS], key=lambda c: (rank[c[1]] - IDLE * c[0], -c[1]))
        p = prog[i]
        if p["alloc"] is not None:
            k = min(free, key=lambda b: free[b])
            where[p["alloc"]] = k
            del free[k]
        qfree[e] = t + p["us"]
        if p["dma"]:
            engines = max(t + START + (p["us"] if p["lat"] else 0.0), engines) + p["dma"]
            end = engines + (p["lat"] or LAND)
        else:
            end = t + p["us"]
        for b in p["x"]:
            bank[b] = (e, end)
        for v in p["use"]:
            users[v] -= 1
            if not users[v]:
                free[where[v]] = end
        ready.remove(i)
        seq.append(i)
        for q, hard in succs[i]:
            left[q] -= 1
            at[q] = max(at[q], end + WAKE if hard else qfree[e])
            if not left[q]:
                ready.append(q)
    assert len(seq) == n
    return seq, where


def rank_program(g, core, T, topo):
    rank = T.rank_of(core)
    if rank is None:
        return
    A = AluOpType
    ACT = ActivationFunctionType
    V, S, P = g.vector, g.scalar, g.tensor
    queue = {"V": V, "S": S, "P": P, "G": g, "Y": g.sync}

    prog = []
    where = {}

    def rec(e, emit, r, w, x, cost, far=0.0, load=0.0, use=(), alloc=None, soft=()):
        prog.append({"e": e, "emit": emit, "r": list(r), "w": list(w), "x": list(x), "cost": cost, "far": far, "load": load, "use": list(use), "alloc": alloc, "soft": list(soft)})

    def op(e, calls, r=(), w=(), x=(), n=64, us=None, use=(), alloc=None, pre=None, ro=(), wo=()):
        calls = calls if isinstance(calls, list) else [calls]

        def emit():
            if pre:
                pre()
            xs = list(x) + ["d%d" % where[v] for v in list(use) + ([alloc] if alloc is not None else [])]
            need(e, deps(e, r, w, xs))
            sem = "s" + e
            for call in calls:
                call().then_inc(T.sem[sem], 1)
                count[sem] += 1
            done(e, sem, count[sem], r, w, xs)
        rec(e, emit, list(r) + list(ro), list(w) + list(wo), x, (CALL * len(calls), max(64, n), 0, 0) if us is None else us, 0.0, 0.0, use, alloc, list(ro) + list(wo))

    def dma(e, pairs, r=(), w=(), load=0.3, wo=(), pre=None):
        def emit():
            if pre:
                pre()
            need(e, deps("dma", r, w, ()))
            sem = "dma%d" % len(ndma)
            ndma.append(16 * len(pairs))
            for out, in_ in pairs:
                queue[e].dma_start(out, in_).then_inc(T.sem[sem], 16)
            done(e, sem, ndma[-1], r, w)
        rec(e, emit, r, list(w) + list(wo), (), (ISSUE * len(pairs), 0, 0, 0), 0.0, load, soft=wo)

    nadd = [0] * 12

    def dma_add(i, out, in_, r, w):
        def emit():
            need("G", deps("dma", r, w, ()))
            nadd[i] += 16
            g.dma_start(out, in_, accum_op=A.add).then_inc(T.sem["add%d" % i], 16)
            done("G", "add%d" % i, nadd[i], r, w)
        rec("G", emit, r, w, (), (1.0, 0, 0, 0), 0.0, ADDUS)

    count = {"sV": 0, "sS": 0, "sP": 0, "sG": 0}
    know = {e: {} for e in queue}
    snaps = {}
    wr, rd, bank = {}, {}, {}
    ndma = []

    def need(e, tokens):
        todo = {}
        for sem, val in tokens:
            if know[e].get(sem, 0) < val:
                todo[sem] = max(todo.get(sem, 0), val)
        items = sorted(todo.items(), key=lambda it: -sum(snaps[it].values()))
        for sem, val in items:
            if know[e].get(sem, 0) >= val:
                continue
            queue[e].wait_ge(T.sem[sem], val)
            for k, v in snaps[(sem, val)].items():
                know[e][k] = max(know[e].get(k, 0), v)
            know[e][sem] = max(know[e].get(sem, 0), val)

    def deps(e, r, w, x):
        own = "s" + e
        tok = [wr[k] for k in list(r) + list(w) if k in wr]
        for k in w:
            tok += [q for q in rd.get(k, ()) if q[0] != own]
        for k in x:
            tok += [q for q in bank.get(k, {}).values() if q[0] != own]
        return tok

    def done(e, sem, val, r, w, x=()):
        sn = dict(know[e])
        sn[sem] = val
        snaps[(sem, val)] = sn
        tok = (sem, val)
        for k in r:
            rd[k] = [q for q in rd.get(k, []) if q[0] != sem] + [tok]
        for k in w:
            wr[k] = tok
            rd[k] = []
        for k in x:
            bank.setdefault(k, {})[sem] = tok

    W = [T["w%d" % i] for i in range(8)]
    D = [T["d%d" % i] for i in range(ND)]
    E = [T["e%d" % n] for n in range(4)]
    SC = [T["sc%d" % n] for n in range(4)]
    PW, SW, CQ, GP = [T.pw0, T.pw1], [T.sw0, T.sw1], [T.cq0, T.cq1], [T.gp0, T.gp1]
    others = [c for c in T.cores if c != core]

    def ts(out, in0, s1, op0, s2=None, op1=None):
        if op1 is None:
            return lambda: V.tensor_scalar(out, in0, s1, None, op0)
        return lambda: V.tensor_scalar(out, in0, s1, s2, op0, op1)

    def tt(out, a, b, o):
        return lambda: V.tensor_tensor(out, a, b, o)

    def cp(out, a, e="V"):
        if e == "S":
            return lambda: S.activation(out, a, ACT.Copy)
        return lambda: V.tensor_copy(out, a)

    def lin(out, a, scale, bias=0.0):
        return lambda: S.activation(out, a, ACT.Identity, bias=bias, scale=scale)

    def ms(out, v):
        return lambda: V.memset(out, v)

    def mm(out, l, rhs, st, sp):
        return lambda: P.matmul(out, l, rhs, st, sp)

    def gat(n):
        return (.06, 0, n, 0)

    def pe(*ns):
        return (0.0, 0, 0, sum(max(64, n) for n in ns))

    def countdown(k):
        left = [k]

        def last():
            left[0] -= 1
            return left[0] == 0
        return last

    def table(win, src, ph, ks):
        return [(win[32 * k + 16 * h:32 * k + 16 * h + 16, :], src[64 * ph + 16 * k:64 * ph + 16 * k + 16, :]) for k in ks for h in range(2)]

    def queues(ph):
        op("V", ms(CQ[ph][:], 4096), w=["cq%d" % ph], n=896)
        dma("YS"[ph], [(CQ[ph][0:128:16, 448 * c:448 * c + 448], T.cand[4 * ph:4 * ph + 4, 896 * c:896 * c + 896]) for c in range(2)], w=["cq%d" % ph], wo=["q" + "YS"[ph]], load=.1)

    def first(e, n):
        dma(e, [(T.candl[:, n, :], T.cand[4 * (n // 2):4 * (n // 2) + 4, 896 * (n % 2):896 * (n % 2) + 896])], w=["candl%d" % n], wo=["q" + e])

    first("Y", 0)
    first("S", 1)
    dma("S", [(T.ngi[:, 0, :], T.nb[:]), (T.ngi[:, 1, :], T.geo[:])], w=["ngi"], wo=["qS"], load=.6)
    first("Y", 2)
    first("Y", 3)
    queues(0)
    dma("Y", table(T.pw0, T.pe, 0, range(4)), w=["pw0"], wo=["qY"], load=TAB)
    queues(1)

    def icol(k):
        return T.ci[:, k:k + 1]

    def fcol(k):
        return T.cf[:, k:k + 1]

    def iota(name, pattern, base=0, r=()):
        n = 1
        for _, m in pattern:
            n *= m
        op("G", lambda: g.iota(T[name][:], pattern, base, 0, allow_small_or_imprecise_dtypes=True), ro=r, w=[name], us=(.13, 2 * n, 0, 0))

    def select(out, in_, pattern, base, cm, r, w):
        op("G", lambda: g.affine_select(out, in_, pattern, A.is_equal, 0.0, base, cm), r=r, w=w, us=(.17, 256, 0, 0))

    op("G", lambda: g.iota(icol(0), [[0, 1]], 0, 1), w=["ci0"], us=(.13, 0, 0, 0))
    iota("qrow", [[0, 8], [1, 16]])
    iota("grow", [[1, 8], [0, 16]])
    iota("pos", [[0, 4], [1, 8], [448, 2]])
    iota("hrow", [[2, 8], [1, 2], [0, 8]])
    op("V", ms(T.one32[:], 1.0), w=["one32"], n=128)
    op("S", cp(T.ones[:], T.one32[:], "S"), r=["one32"], w=["ones"], n=128)
    op("S", lin(T.zero[:], T.one32[:], 0.0), r=["one32"], w=["zero"], n=128)
    op("V", [ts(icol(k), icol(0), shift, A.arith_shift_right, mask, A.bitwise_and) for k, shift, mask in ((1, 0, 15), (2, 4, 7), (3, 5, 3), (4, 1, 15), (5, 0, 1))], r=["ci0"], w=["ci"], n=320)
    op("V", cp(T.cf[:, 0:6], T.ci[:, 0:6]), r=["ci0", "ci"], w=["cf"])
    op("V", ts(T.bf32[:], T.grow[:], fcol(2), A.is_equal), r=["grow", "cf"], w=["bf32"], n=128)
    op("S", cp(T.bm[:], T.bf32[:], "S"), r=["bf32"], w=["bm"], n=128)
    op("V", ts(fcol(6), fcol(1), 1.5, A.is_gt, 64.0, A.mult), r=["cf"], w=["cf6"])
    op("S", lin(fcol(7), fcol(2), 2.0, fcol(6)), r=["cf", "cf6"], w=["cf7"])
    op("V", [ts(T.casel[:, b, :], T.hrow[:], -1.0 * b, A.add, fcol(7), A.is_equal) for b in range(2)], r=["hrow", "cf7"], w=["casel"], n=128)
    op("S", lin(fcol(8), fcol(1), 28.0), r=["cf"], w=["cf8"])
    op("V", ts(T.m16[:], T.qrow[:, 0:16], fcol(1), A.is_equal), r=["qrow", "cf"], w=["m16"])
    for i in range(4):
        select(T.lnb[:, i, :], T.one32[:], [[-16, 4], [-128, 2], [-1, 16]], 128 * (i % 2) - 64 * (i // 2), 1, ["one32"], ["lnb%d" % i])

    nsig = [0] * 8

    def send(t, ph):
        i = 2 * t + ph
        mine = W[i][:, 64 * rank:64 * rank + 64]

        def emit():
            need("G", deps("G", ["wown%d" % i], [], []))
            m = topo.mask(core, others[0])
            ids = []
            for o in others:
                m &= topo.mask(core, o)
                a = topo.addr(o)
                ids.append(DstId(rid=a[0], pnc=a[1]))
            tr = RemoteDMATransfer(dst_ids=ids, dma_engine_mask=m, remote_sem=T.sem["arr%d" % i], srcs=[mine], dsts=[mine for _ in ids])
            g.remote_dma_fused([tr], local_sem=T.sem["loc" if t else "loc0"])
            nsig[i] += bin(m).count("1")
        rec("G", emit, ["wown%d" % i], ["sent%d" % i], [], (.6 if i else 3.6, 0, 0, 0), FLIGHT, SEND)

    for ph in range(2):
        keys, two = ["candl%d" % (2 * ph), "candl%d" % (2 * ph + 1)], slice(2 * ph, 2 * ph + 2)
        op("V", [cp(T.tin[:, two, 8 * i:8 * i + 8], T.candl[:, two, 0:8]) for i in range(1 if ph else 4)], r=keys, w=["tin%d" % ph], n=64 if ph else 256)
        if ph:
            op("S", [cp(T.tin[:, two, 8 * i:8 * i + 8], T.tin[:, two, 0:8], "S") for i in range(1, 4)], r=["tin1"], w=["tin2"], n=192)
        op("V", lambda ph=ph, two=two: V.transpose(W[ph][:, 64 * rank:64 * rank + 64], T.tin[:, two, :]), r=["tin%d" % ph, "tin%d" % (2 * ph)], w=["wown%d" % ph])
        send(0, ph)
        op("V", [cp(T.offs[:, 16 * ph + 8 * b:16 * ph + 8 * b + 8], T.candl[:, two, 4 * b:4 * b + 4]) for b in range(2)], r=keys, w=["offs%d" % ph], n=128)

    op("V", cp(T.ngf[:], T.ngi[:]), r=["ngi"], w=["ngf"])
    for ph in range(2):
        op("P", [mm(T.mb[:, 8:10, ph, 0:8], T.lnb[:, 2 * ph + h, :], T.ngf[:, :, h:16:2], h == 0, h == 1) for h in range(2)],
           r=["ngf", "lnb%d" % (2 * ph), "lnb%d" % (2 * ph + 1)], w=["mbn%d" % ph], x=["mb"], us=pe(256, 256))
        op("V", [cp(T.nbu[:, 8 * ph + 4 * c:8 * ph + 4 * c + 4], T.mb[:, 8, ph, c:8:2]) for c in range(2)], r=["mbn%d" % ph], w=["nbu%d" % ph], x=["mb"], n=128)
        op("S", cp(T.gl[:, ph, :], T.mb[:, 9, ph, 0:8], "S"), r=["mbn%d" % ph], w=["gl%d" % ph], x=["mb"])
        op("S", [lin(T.gm[:, ph, 4 * (i % 2) + i // 2, :], T.m16[:], T.gl[:, ph, i:i + 1]) for i in range(8)], r=["m16", "gl%d" % ph], w=["gm%d" % ph], n=512)
        op("P", mm(GP[ph][:, 12:16, :, :], T.bf32[:], T.gm[:, ph, :, :], True, True), r=["bf32", "gm%d" % ph], w=["gpg%d" % ph], wo=["grp%d" % ph], x=["gp%d" % ph], us=pe(512))
        for al in (2, 0, 1, 3):
            op("S", lin(T.geor[:, ph, al, :], GP[ph][:, 12:16, :, :], 16.0, -65536.0), r=["gpg%d" % ph], w=["geor%d%d" % (ph, al)], x=["gp%d" % ph], n=128)

    def sends(t, ph):
        lo = 16 * ph
        lanes = [slice(a, a + 3 * s + 1, s) for a, s in (lane(t, 0), lane(t, 1))]
        both = [(T.offc[:, lo + 8 * b:lo + 8 * b + 8], lanes[b]) for b in range(2)] if t else [(T.offc[:, lo:lo + 16], slice(0, 8))]
        op("V", [ts(out, T.pos[:, ph, a, :], fcol(8), A.add) for out, a in both], r=["pos", "pos%d" % ph, "cf8"], w=["offc%d" % ph], n=64 * len(both))
        op("V", ts(T.crow[:, ph, :], CQ[ph][:].indirect(T.offc[:, lo:lo + 16]), -2048.0, A.add), r=["cq%d" % ph, "offc%d" % ph], w=["crow%d" % ph], us=gat(256))
        if t:
            i = 2 * t + ph
            op("P", [mm(T.mb[:, 2:4, h, :], T.csel[:, 8 * h + slot(t, k % 4, k // 4), :], T.crow[:, ph, 32 * k:32 * k + 32], k == 0, k == 7) for h in range(2) for k in range(8)],
               r=["crow%d" % ph] + ["csel%d" % k for k in range(16)], w=["mbc"], x=["mb"], us=pe(*[32] * 16))
            mine = W[i][:, 64 * rank:64 * rank + 64]
            op(ON["mine"], cp(mine, T.mb[:, 2:4, :, :], ON["mine"]), r=["mbc"], w=["wown%d" % i], x=["mb"])
            send(t, ph)
            op("V", lambda: V.transpose(T.tl[:, ph, :, :], mine), r=["wown%d" % i], w=["tl%d" % ph])
            op("V", [cp(T.offs[:, lo + 8 * b:lo + 8 * b + 8], T.tl[:, ph, :, lanes[b]]) for b in range(2)], r=["tl%d" % ph], w=["offs%d" % ph], n=128)

    def codes(t, ph):
        calls = [mm(T.ca[:, :, :, j, :], T.casel[:, b, :], T.crow[:, ph, 128 * b:128 * b + 128], b == 0, b == 1) for j in range(4) for b in range(2)]
        op("P", calls, r=["crow%d" % ph, "casel"], w=["ca%d" % al for al in range(4)], x=["ca"], us=pe(*[128] * 8))

    def selves(ph):
        op("V", cp(T.own[:, ph, :], SW[ph][:].indirect(T.offs[:, 16 * ph:16 * ph + 16])), r=["sw%d" % q for q in range(4 * ph, 4 * ph + 4)] + ["offs%d" % ph], w=["own%d" % ph], us=gat(256))

    def neighbours(t, ph):
        i, e = 2 * t + ph, ON["cn"]
        op(e, cp(T.cn[:, 128 * ph:128 * ph + 128], W[i][:].indirect(T.nbu[:, 8 * ph:8 * ph + 8]), e), r=["nbu%d" % ph, "wown%d" % i, "sent%d" % i],
           w=["cn%d" % ph], us=gat(128), pre=lambda: queue[e].wait_ge(T.sem["arr%d" % i], 3 * nsig[i]))

    def index(ph, als):
        a0, a1 = als[0], als[-1] + 1
        lo, hi, keys = 512 * ph + 128 * a0, 512 * ph + 128 * a1, ["ix%d%d" % (ph, al) for al in als]
        for al in als:
            op("V", tt(T.ca[:, al, :, :, :], T.cn[:, 128 * ph:128 * ph + 128], T.ca[:, al, :, :, :], A.mult), r=["cn%d" % ph], w=["ca%d" % al], x=["ca"], n=128)
        op("V", tt(T.idx[:, lo:hi], T.ca[:, a0:a1, :, :, :], T.geor[:, ph, a0:a1, :], A.add), r=["ca%d" % al for al in als] + ["geor%d%d" % (ph, al) for al in als], w=keys, x=["ca"], n=hi - lo)
        op("V", ts(T.idx[:, lo:hi], T.idx[:, lo:hi], 4, A.arith_shift_right, 4095, A.bitwise_and), w=keys, n=hi - lo)
        op("V", cp(T.off[:, lo:hi], T.idx[:, lo:hi]), r=keys, w=["of%d%d" % (ph, al) for al in als], n=hi - lo)

    def ekeys(n, al, hs=(0, 1)):
        return ["e%d%d%d" % (n, al, h) for h in hs]

    def part(n, al, hs):
        return E[n][:, al, 512 * hs[0]:512 * hs[-1] + 512]

    def gather(n, al, hs, sign=1.0, e="S", minus=None):
        ph, lo = n // 2, 512 * (n // 2) + 128 * al + 64 * (n % 2)
        out, src = part(n, al, hs), PW[ph][:].indirect(T.off[:, lo + 32 * hs[0]:lo + 32 * hs[-1] + 32])
        r = ["pw%d" % ph, "of%d%d" % (ph, al)]
        if minus is not None:
            e, call, r = "V", tt(out, src, part(n, minus, hs), A.subtract), r + ekeys(n, minus, hs)
        elif e == "V":
            call = cp(out, src) if sign == 1.0 else ts(out, src, sign, A.mult)
        else:
            call = lambda: S.activation(out, src, ACT.Copy, scale=sign)
        op(e, call, r=r, w=ekeys(n, al, hs), wo=["turn"] if e == "S" else [], us=gat(512 * len(hs)))

    def unit(t, n, al):
        fused = MODE[t][n][al % 2] == "F" if t == 3 else MODE[t][n][2] == "F"
        minus = (al + 2 if t == 3 else 2) if fused and al in ((0, 1) if t == 3 else (3,)) else None
        sign = (-1.0 if al > 1 and not fused else 1.0) if t == 3 else (-1.0 if al % 2 else 1.0)
        for e in "VS":
            hs = [h for h in range(2) if ((al, h) in VG[t][n]) == (e == "V")]
            for some in ([[h] for h in hs] if (n % 2, al) in HALVES[kind(t, n)] else [hs] if hs else []):
                gather(n, al, some, sign, e, minus)

    def added(n, i, into, what):
        dma_add(3 * n + i, part(n, into, (0, 1)), part(n, what, (0, 1)), ekeys(n, what), ekeys(n, into))
        return into

    nv = [0]

    def bank_diff(n, h, terms, early=0):
        v = nv[0]
        nv[0] += 1
        for lo, hi in ((0, early), (early, len(terms))):
            calls = []
            for i in range(lo, hi):
                al, fl, sg = terms[i]
                for q in (range(16) if fl else [None]):
                    rhs = part(n, al, [h]) if q is None else E[n][:, al, 512 * h + (q + 8) % 16:512 * h + 512:16]
                    calls.append(lambda i=i, q=q, sg=sg, rhs=rhs: P.matmul(D[where[v]][:] if q is None else D[where[v]][:, q:512:16], (T.ip if sg > 0 else T.im)[:], rhs,
                                                                          i == 0, i == len(terms) - 1 and q in (None, 15)))
            if calls:
                op("P", calls, r=["e%d%d%d" % (n, al, h) for al, _, _ in terms[lo:hi]] + ["ip", "im"], w=["vd%d" % v] if hi == len(terms) else [], wo=["vo%d" % v],
                   us=pe(*[1024 if fl else 512 for _, fl, _ in terms[lo:hi]]), alloc=None if lo else v, use=[v] if lo else [])
        return v

    def scans(t, n, al, src, low):
        rp, key = (T.rmin, "rmin") if low else (T.rmax, "rmax")
        o0, o1 = (A.max, A.min) if low else (A.min, A.max)
        if isinstance(src, list):
            for h, v in enumerate(src):
                op("V", lambda h=h, v=v: V.tensor_tensor_scan(SC[n][:, al, 512 * h:512 * h + 512], rp[:, 0:512], D[where[v]][:], 0.0, o0, o1),
                   r=["vd%d" % v, key], w=["sc%d%d%d" % (n, al, h)], use=[v], n=512)
            return
        for hs in ([[0], [1]] if (n % 2, al) in SPLIT[kind(t, n)] else [[0, 1]]):
            op("V", lambda hs=hs: V.tensor_tensor_scan(SC[n][:, al, 512 * hs[0]:512 * hs[-1] + 512], rp[:, 0:512 * len(hs)], part(n, src, hs), 0.0, o0, o1),
               r=ekeys(n, src, hs) + [key], w=["sc%d%d%d" % (n, al, h) for h in hs], n=256 * len(hs))

    def chunk(t, n):
        mode = MODE[t][n]
        if t == 3:
            for p, m in enumerate(mode):
                src = added(n, p, p, p + 2) if m == "A" else p
                for h in (range(2) if m == "P" else ()):
                    v = bank_diff(n, h, [(p + 2, False, 1), (p, False, 1)])
                    op("S", lambda h=h, v=v, p=p: S.activation(part(n, p, [h]), D[where[v]][:], ACT.Copy), r=["vd%d" % v], w=ekeys(n, p, [h]), use=[v], n=512)
                scans(t, n, p, src, True)
                scans(t, n, p + 2, src, False)
            return [True, True, False, False]
        flip = t != 1
        low = [True, mode[1] == "P" and mode[2] != "F", mode[2] != "F", mode != "AAA"]
        src, s1, s3 = {2: 3}, -1 if low[1] else 1, 1 if low[3] else -1
        src[3] = [bank_diff(n, h, [(3, False, s3), (2, False, s3), (0, flip, -s3)] if mode[2] == "F" else [(3, False, -s3), (0, flip, -s3)],
                            EARLY[n % 2] * (2 if mode[2] == "F" else 1)) for h in range(2)]
        for k, s in ((0, 1), (1, s1), (2, 1)):
            if mode[k] == "P":
                src[k] = [bank_diff(n, h, [(k, False, s), (k + 1, False, s)]) for h in range(2)]
        for k, into, what in ((2, 3, 2), (0, 0, 1), (1, 2, 1)):
            if mode[k] == "A":
                src[k] = added(n, k, into, what)
        for al in (2, 3, 0, 1):
            scans(t, n, al, src[al], low[al])
        return low

    def post(t, n, low):
        ph, c = n // 2, n % 2
        gp, bk, grp = GP[c], "gp%d" % c, "grp%d" % c
        gap, cnt, flg = gp[:, 0:4, :, :], gp[:, 4:8, :, :], T.flg[:, n, :]
        if t == 3:
            lo = 8 + 4 * ph
            op("P", [mm(gp[:, lo:lo + 4, :, slot(t, k % 4, k // 4)], T.casel[:, 0, :], T.crow[:, ph, 32 * k + 16 * c:32 * k + 16 * c + 16], True, True) for k in range(8)],
               r=["crow%d" % ph, "casel"], w=["rows%d" % n], wo=[grp], x=[bk], us=pe(*[64] * 8))
            op("S", cp(T.crx[:, n, :], gp[:, lo:lo + 4, :, :], "S"), r=["rows%d" % n], w=["crx%d" % n], x=[bk], n=128)
        calls = [mm(gap, T.zero[:], T.ones[:], True, False)]

        def own(b, a0, a1):
            return T.own[:, ph, 128 * b + 64 * c + 16 * a0:128 * b + 64 * c + 16 * a1]
        for b in range(2):
            if t == 3:
                for al in range(4):
                    calls += [mm(gp[:, 0:4, :, 2 * al + b], sign[:], own(b, a, a + 1), False, False) for sign, a in ((T.ip16, al), (T.im16, (al + 2) % 4))]
            else:
                calls += [mm(gp[:, 0:4, :, b:8:2], T.ip16[:], own(b, 0, 4), False, False), mm(gp[:, 0:3, :, b:8:2], T.im16[:], own(b, 1, 4), False, False),
                          mm(gp[:, 3, :, b:8:2], T.im16[:], own(b if t == 1 else 1 - b, 0, 1), False, False)]
        op("P", calls, r=["own%d" % ph, "zero", "ones", "ip16", "im16"], w=["gap%d%d" % (c, al) for al in range(4)], wo=[grp], x=[bk], us=pe(128, *[64] * (len(calls) - 1)))
        if t == 3:
            sets = [[al] for al in range(4)]
        elif low == [True, False, True, False]:
            sets = [[0, 2], [1, 3]]
        else:
            sets = [[0, 3]] + ([[1, 2]] if low[1] == low[2] else [[1], [2]])
        last = countdown(4 * len(sets))
        for als in sets:
            pick = slice(als[0], als[-1] + 1, max(1, als[-1] - als[0]))
            out = gp[:, 0:4, :, 2 * als[0]:2 * als[0] + 2] if t == 3 else gp[:, pick, :, :]
            calls = [lambda out=out, rhs=SC[n][:, pick, lo + 7:lo + 256:8], sign=(T.ip if low[als[0]] else T.im)[:]: P.matmul(out, sign, rhs, False, last()) for lo in range(0, 1024, 256)]
            op("P", calls, r=["ip", "im"] + ["sc%d%d%d" % (n, al, h) for al in als for h in range(2)], ro=[grp] + ["gap%d%d" % (c, al) for al in als],
               w=["sum%d%d" % (c, al) for al in als], x=[bk], us=pe(64, 64, 64, 64))
        GK = ["gap%d%d" % (c, al) for al in range(4)] + ["sum%d%d" % (c, al) for al in range(4)]
        if t == 3:
            op("V", cp(T.gh[:, n, :], gap), r=GK, w=["gh%d" % n], x=[bk], n=128)
            op("P", [mm(T.mb[64 * c:64 * c + 64, 8 + 4 * h:12 + 4 * h, :, :], T.back[:, h, :], T.gh[:, n, :], True, True) for h in range(2)],
               r=["gh%d" % n, "back"], w=["mby%d" % c], x=["mb"], us=pe(128, 128))
            op("V", ts(flg, T.gh[:, n, :], 0.0, A.is_gt), r=["gh%d" % n], w=["flg%d" % n])
            op("P", [mm(cnt, T.kc[:], T.ones[:], True, False), mm(cnt, T.bn[:], flg, False, True)], r=["flg%d" % n, "bn", "kc", "ones"], w=["cnt%d" % c], wo=[grp], x=[bk], us=pe(128, 128))
            op("V", tt(T.ycb[:, n, :], cnt, T.crx[:, n, :], A.min), r=["cnt%d" % c, "crx%d" % n], w=["yc%d" % n], x=[bk], n=128)
            dma("Y", [(T.yc[4 * ph:4 * ph + 4, 256 * c:256 * c + 256], T.ycb[0:128:16, n, :])], r=["yc%d" % n])
            if c:
                op("S", cp(T.ygb[:, ph, :], T.mb[:, 8:16, :, :], "S"), r=["mby0", "mby1"], w=["yg%d" % ph], x=["mb"], n=256)
                for e, k in (("Y", 0), ("S" if ph else "Y", 1)):
                    dma(e, [(T.yg[64 * ph:64 * ph + 64, 256 * k:256 * k + 256], T.ygb[64 * k:64 * k + 64, ph, :])], r=["yg%d" % ph])
            return
        if ON["flag"] == "S":
            call = lambda: S.activation(flg, gap, ACT.Sign, bias=-0.5)
        else:
            call = ts(flg, gap, 0.0, A.is_gt)
        op(ON["flag"], call, r=GK, w=["flg%d" % n], x=[bk], n=128)
        dm = T.dm[:, 4 * t + n, :]
        op("P", mm(cnt, flg, T.bm[:], True, True), r=["flg%d" % n, "bm"], w=["cnt%d" % c], wo=[grp], x=[bk], us=pe(128))
        op("V", tt(dm, cnt, T.thr[:], A.is_ge), r=["cnt%d" % c, "thr"], w=["dm%d%d" % (t, n)], x=[bk], n=128)
        out = T.mb[:, 0, :, c:16:2]
        calls = [mm(out, T.ip[:], T.kk[:, c, :], True, False)] + [mm(out, T.dm[:, 4 * s + n, :], T.ones[:, 0:16], False, False) for s in range(t)]
        calls.append(mm(out, dm, T.rt[:, t, :], False, True))
        op("P", calls, r=["dm%d%d" % (s, n) for s in range(t + 1)] + ["rt%d" % t, "kk", "ip", "ones"], w=["mbp%d" % c], x=["mb"], us=pe(*[64] * len(calls)))
        if c == 1:
            op("V", tt(T.pos[:, ph, :, :], T.mb[:, 0, :, :], T.pos[:, ph, :, :], A.max), r=["mbp0", "mbp1", "pos"], w=["pos%d" % ph], x=["mb"])

    for name, pattern, base in (("prow", [[1, 128]], 0), ("arow", [[0, 2], [1, 8]], 0), ("krow", [[4, 4], [0, 32]], 0), ("kk", [[448, 2], [0, 16]], -56), ("brow", [[32, 4], [1, 16]], 0)):
        iota(name, pattern, base, ["sent0"])
    for name, v in (("ip", 1.0), ("ip16", 1.0), ("im16", -1.0)):
        op("V", ts(T[name][:], T.prow[:], fcol(0), A.is_equal, v, A.mult), r=["prow", "cf"], w=[name])
    op("S", lin(T.im[:], T.ip[:], -1.0), r=["ip"], w=["im"], n=128)
    op("V", ms(T.rmin[:], -BIG), w=["rmin"], n=512)
    op("V", ms(T.rmin[:, 0:1024:8], BIG), w=["rmin"])
    op("S", lin(T.rmax[:], T.rmin[:], -1.0), r=["rmin"], w=["rmax"], n=1024)
    op("V", ts(T.thr[:], T.qrow[:], fcol(4), A.not_equal, 64.0, A.mult), r=["qrow", "cf"], w=["thr"])
    op("S", lin(T.thr[:], T.thr[:], 1.0, 15.5), w=["thr"], n=128)
    op("S", lin(fcol(9), fcol(5), 4.0), r=["cf"], w=["cf9"])
    for t, (m, b) in enumerate(((1.0, 9), (2.0, 5), (3.0, 9))):
        a, key = fcol(10 + t), "cf%d" % (10 + t)
        op("S", lin(a, fcol(3), m, fcol(b)), r=["cf", "cf9"], w=[key])
        if t == 2:
            op("V", ts(fcol(13), a, 7.5, A.is_gt, -8.0, A.mult), r=[key], w=["cf13"])
            op("S", lin(a, a, 1.0, fcol(13)), r=["cf13"], w=[key])
        op("V", [ts(T.rt[:, t, :], T.arow[:], a, A.is_equal, 64.0, A.mult), ts(T.ru[:, t, :], T.arow[:], a, A.is_gt)], r=["arow", key], w=["rt%d" % t, "ru%d" % t], n=128)
    op("V", tt(T.rt[:], T.rt[:], T.ru[:], A.add), r=["ru0", "ru1", "ru2"], w=["rt0", "rt1", "rt2"], n=96)
    for h in range(2):
        op("V", ts(T.xsel[:, h, :], T.krow[:], 2.0 * h, A.add, fcol(7), A.is_equal), r=["krow", "cf7"], w=["xsel%d" % h])
        for u in range(8):
            select(T.csel[:, 8 * h + u, :], T.xsel[:, h, :], [[0, 16], [1, 8]], -u, 0, ["xsel%d" % h, "sent1"], ["csel%d" % (8 * h + u)])
    op("V", [ts(T.back[:, h, :], T.brow[:], 16.0 * h, A.add, fcol(0), A.is_equal) for h in range(2)], r=["brow", "cf"], w=["back"], n=128)
    op("S", lin(T.bn[:], T.bm[:], -4096.0), r=["bm"], w=["bn"], n=128)
    op("V", ts(fcol(14), T.ip[:, 0:1], 65536.0, A.mult, T.ip[:, 1:2], A.subtract), r=["ip"], w=["cf14"])
    op("S", lin(T.kc[:], T.ones[:], fcol(14)), r=["ones", "cf14"], w=["kc"], n=128)

    sends(0, 0)
    sends(0, 1)
    dma("Y", table(T.pw1, T.pe, 1, range(4)), w=["pw1"], r=["sent0", "sent1"], wo=["qY"], load=TAB, pre=lambda: g.sync.wait_ge(T.sem.loc0, nsig[0] + nsig[1]))
    for t in range(4):
        for ph in range(2):
            if t:
                sends(t, ph)
            codes(t, ph)
            neighbours(t, ph)
            for als in LISTS[kind(t, 2 * ph)]:
                index(ph, als)
            for i, (c, al) in enumerate(UNITS[kind(t, 2 * ph)]):
                unit(t, 2 * ph + c, al)
                for q in range(8):
                    if t == 0 and PACE[q] == 8 * ph + i:
                        dma("Y", table(SW[q // 4], T.se, q // 4, [q % 4]), r=ekeys(2 * ph + c, al, [0]) if 8 * ph + i else [], w=["sw%d" % q], wo=["qY"], load=TAB / 2)
            selves(ph)
            for n in (2 * ph, 2 * ph + 1):
                post(t, n, chunk(t, n))

    if not ORDER:
        ORDER.append(order(prog))
    seq, banks = ORDER[0]
    where.update(banks)
    for i in seq:
        prog[i]["emit"]()
    g.wait_ge(T.sem.loc, sum(nsig[2:]))
    for e in ("sV", "sS", "sP", "sG"):
        if know["Y"].get(e, 0) < count[e]:
            g.sync.wait_ge(T.sem[e], count[e])
    for i, v in enumerate(ndma):
        g.sync.wait_ge(T.sem["dma%d" % i], v)
